import numpy as np
import ml_dtypes


def mxq(x, axis, fmt="e4m3"):
    dtype, down = {"e4m3": (ml_dtypes.float8_e4m3fn, 7), "e5m2": (ml_dtypes.float8_e5m2, 14)}[fmt]
    v = np.moveaxis(np.asarray(x, np.float32).astype(ml_dtypes.bfloat16).astype(np.float64), axis, -1)
    blocks = v.reshape(v.shape[:-1] + (-1, 32))
    amax = np.abs(blocks).max(-1, keepdims=True)
    byte = np.maximum(np.where(amax > 0, np.frexp(amax)[1] - 1 + 127, 0) - down, 1)
    scale = np.exp2(byte - 127.0)
    codes = (blocks / scale).astype(np.float32).astype(dtype).astype(np.float64)
    return np.moveaxis((codes * scale).reshape(v.shape), -1, axis)


WIDE = False


def mx_kscale(k):
    if not WIDE:
        return np.ones(k)
    levels = np.array([18, -18])
    if k % 512:
        return np.exp2(np.random.permutation(np.resize(levels, k // 32))).repeat(32)
    a = np.empty((k // 512, 16))
    for p in range(k // 512):
        a[p, :8] = np.random.permutation(np.resize(levels, 8))
        for g in range(8):
            far = levels[np.abs(levels - a[p, g]) >= 10]
            a[p, g + 8] = far[np.random.randint(len(far))]
    return np.exp2(a.ravel()).repeat(32)


def f64(x):
    return np.asarray(x).astype(np.float64)


def striped(idx):
    return np.tile(np.asarray(idx).reshape(-1, 16).T, (8, 1)).astype(np.uint16)


def unstriped(offs):
    return offs[:16].T.reshape(-1).astype(np.int64)


def setup_inputs():
    n = np.random.standard_normal
    uni = np.random.uniform
    idx = np.random.permutation(1024)[:512]
    f_d = mx_kscale(512)
    f_m = mx_kscale(512)
    return {
        "dy": (n((512, 512)) * f_m[:, None]).astype(np.float32),
        "wo": (n((512, 512)) / np.sqrt(512) / f_m[:, None] * f_d[None, :]).astype(np.float32),
        "gT": (1.0 / (1.0 + np.exp(-2.5 * n((512, 1024))))).astype(np.float32),
        "cT": (np.tanh(1.5 * n((512, 1024)))).astype(np.float32),
        "xT": (n((512, 1024))).astype(np.float32),
        "wg": (n((512, 512)) / np.sqrt(512) / f_d[:, None]).astype(np.float32),
        "wc": (n((512, 512)) / np.sqrt(512) / f_d[:, None]).astype(np.float32),
        "offs": striped(idx),
    }


def reference(dy, wo, gT, cT, xT, wg, wc, offs):
    idx = unstriped(offs)
    g_ = f64(gT)[:, idx]
    c_ = f64(cT)[:, idx]
    x_ = f64(xT)[:, idx]
    dr = mxq(f64(wo), 0, "e4m3").T @ mxq(f64(dy), 0, "e5m2")
    zg = dr * (c_ - x_) * g_ * (1.0 - g_)
    zc = dr * g_ * (1.0 - np.square(c_))
    dd = dr * (1.0 - g_)
    a = mxq(f64(wg), 0, "e4m3").T @ mxq(zg, 0, "e5m2")
    b = mxq(f64(wc), 0, "e4m3").T @ mxq(zc, 0, "e5m2")
    s = a + b
    out_0 = np.zeros((512, 1024))
    out_0[:, idx] = s
    out_1 = np.zeros((512, 1024))
    out_1[:, idx] = dd
    return out_0, out_1

@@ -1,0 +1,169 @@
+from contextlib import ExitStack
+
+import concourse.mybir as mybir
+
+F32 = mybir.dt.float32
+BF16 = mybir.dt.bfloat16
+U32 = mybir.dt.uint32
+U16 = mybir.dt.uint16
+U8 = mybir.dt.uint8
+E4M3 = mybir.dt.float8_e4m3fn_x4
+E5M2 = mybir.dt.float8_e5m2_x4
+ALU = mybir.AluOpType
+ACT = mybir.ActivationFunctionType
+
+P = 128
+PACK = 4
+K = 512
+SLOTS = 512
+TOKENS = 1024
+HALF = 256
+FLOPS = 3 * 2 * K * K * SLOTS
+
+
+def tile_attend_ghighw_kernel(tc, dy, wo, gT, cT, xT, wg, wc, offs, out_0, out_1):
+    nc = tc.nc
+    with ExitStack() as ctx:
+        lists = ctx.enter_context(tc.tile_pool(name="lists", bufs=1))
+        sb = ctx.enter_context(tc.tile_pool(name="sb", bufs=1))
+        psum = ctx.enter_context(tc.psum_pool(name="psum", bufs=1))
+
+        offsets = lists.tile([P, SLOTS // 16], U16, name="offsets")
+        nc.sync.dma_start(offsets[:], offs)
+
+        windows = []
+        for t in range(PACK):
+            window = sb.tile([P, TOKENS], F32, name="window%d" % t)
+            nc.vector.memset(window[:], 0.0)
+            windows.append(window)
+
+        def load_plane(table, label, t):
+            plane = sb.tile([P, TOKENS], F32, name="%s_rows%d" % (label, t))
+            nc.sync.dma_start(plane[:], table.rearrange("(p t) n -> p t n", t=PACK)[:, t, :])
+            return plane
+
+        def load_columns(matrix, label, first, count):
+            raw = sb.tile([P, PACK, count], F32, name="%s_raw%d" % (label, first))
+            nc.sync.dma_start(raw[:], matrix.rearrange("(p j) n -> p j n", j=PACK)[:, :, first : first + count])
+            return raw
+
+        def packed_tiles(label):
+            grouped = sb.tile([P, K, PACK], BF16, name=label + "_grouped", align_bytes=64)
+            codes = sb.tile([P, K], U32, name=label + "_codes", align_bytes=64)
+            scales = sb.tile([P, K], U8, name=label + "_scales", align_bytes=64)
+            return grouped, codes, scales
+
+        def group(grouped, raw, first, count):
+            nc.scalar.copy(
+                out=grouped[:, first : first + count, :].rearrange("p (c i) j -> p c j i", i=4),
+                in_=raw[:].rearrange("p j (c i) -> p c j i", i=4),
+            )
+
+        def group_dealt(grouped, raw, first, count):
+            dealt = grouped[:].rearrange("p (t m) j -> p m j t", t=PACK)
+            nc.scalar.copy(
+                out=dealt[:, first // PACK : (first + count) // PACK, :, :],
+                in_=raw[:].rearrange("p j (m t) -> p m j t", t=PACK),
+            )
+
+        def quantize(packed, fmt):
+            grouped, codes, scales = packed
+            nc.vector.quantize_mx(
+                out=codes[:].bitcast(fmt), scales=scales[:], in_=grouped[:].rearrange("p n j -> p (n j)")
+            )
+
+        def mx_pass(acc, weights, tile_index, moving, start, stop):
+            cols = slice(tile_index * P, (tile_index + 1) * P)
+            nc.tensor.matmul_mx(
+                out=acc[:],
+                lhsT=weights[1][:, cols].bitcast(E4M3),
+                lhsT_scale=weights[2][:, cols],
+                rhs=moving[1][:].bitcast(E5M2),
+                rhs_scale=moving[2][:],
+                start=start,
+                stop=stop,
+            )
+
+        g = sb.tile([P, PACK, SLOTS], F32, name="g")
+        c = sb.tile([P, PACK, SLOTS], F32, name="c")
+        x_less_c = sb.tile([P, PACK, SLOTS], F32, name="x_less_c")
+        c_sq = sb.tile([P, PACK, SLOTS], F32, name="c_sq")
+        one_less_csq = sb.tile([P, PACK, SLOTS], F32, name="one_less_csq")
+        one_less_g = sb.tile([P, PACK, SLOTS], F32, name="one_less_g")
+        h = sb.tile([P, PACK, SLOTS], F32, name="h")
+        u = sb.tile([P, PACK, SLOTS], F32, name="u")
+        dr = sb.tile([P, PACK, SLOTS], F32, name="dr")
+        s = sb.tile([P, PACK, SLOTS], F32, name="s")
+
+        dy_p = packed_tiles("dy")
+        wo_p = packed_tiles("wo")
+        wg_p = packed_tiles("wg")
+        wc_p = packed_tiles("wc")
+        zg_p = packed_tiles("zg")
+        zc_p = packed_tiles("zc")
+
+        def gather_plane(t):
+            c_rows = load_plane(cT, "c", t)
+            g_rows = load_plane(gT, "g", t)
+            x_rows = load_plane(xT, "x", t)
+            nc.vector.tensor_copy(c[:, t, :], c_rows[:].indirect(offsets[:]))
+            nc.vector.tensor_copy(g[:, t, :], g_rows[:].indirect(offsets[:]))
+            nc.vector.tensor_tensor(x_less_c[:, t, :], x_rows[:].indirect(offsets[:]), c[:, t, :], ALU.subtract)
+            nc.vector.scalar_tensor_tensor(
+                h[:, t, :], g[:, t, :], 1.0, x_less_c[:, t, :], op0=ALU.subtract, op1=ALU.mult
+            )
+            nc.scalar.activation(c_sq[:, t, :], c[:, t, :], ACT.Square)
+            nc.scalar.activation(one_less_csq[:, t, :], c_sq[:, t, :], ACT.Copy, bias=1.0, scale=-1.0)
+            nc.scalar.activation(one_less_g[:, t, :], g[:, t, :], ACT.Copy, bias=1.0, scale=-1.0)
+
+        gather_plane(0)
+        group(dy_p[0], load_columns(dy, "dy", 0, HALF), 0, HALF)
+        gather_plane(1)
+        group(dy_p[0], load_columns(dy, "dy", HALF, HALF), HALF, HALF)
+        quantize(dy_p, E5M2)
+        gather_plane(2)
+        for first in (0, HALF):
+            group_dealt(wo_p[0], load_columns(wo, "wo", first, HALF), first, HALF)
+        quantize(wo_p, E4M3)
+        dr_acc = []
+        for t in range(PACK):
+            acc = psum.tile([P, SLOTS], F32, name="dr_acc%d" % t)
+            mx_pass(acc, wo_p, t, dy_p, True, True)
+            dr_acc.append(acc)
+        gather_plane(3)
+
+        for t in range(PACK):
+            nc.vector.tensor_tensor(u[:, t, :], dr_acc[t][:], g[:, t, :], ALU.mult)
+        group(wc_p[0], load_columns(wc, "wc", 0, K), 0, K)
+        group(wg_p[0], load_columns(wg, "wg", 0, K), 0, K)
+        for t in range(PACK):
+            nc.scalar.copy(out=dr[:, t, :], in_=dr_acc[t][:])
+
+        for packed, factor in ((zc_p, one_less_csq), (zg_p, h)):
+            nc.vector.tensor_tensor(
+                packed[0][:].rearrange("p (n i) t -> p n t i", i=2),
+                u[:].rearrange("p t (n i) -> p n t i", i=2),
+                factor[:].rearrange("p t (n i) -> p n t i", i=2),
+                ALU.mult,
+            )
+        quantize(wc_p, E4M3)
+        quantize(zc_p, E5M2)
+        quantize(wg_p, E4M3)
+        quantize(zg_p, E5M2)
+
+        s_acc = []
+        for r in range(PACK):
+            acc = psum.tile([P, SLOTS], F32, name="s_acc%d" % r)
+            mx_pass(acc, wc_p, r, zc_p, True, False)
+            s_acc.append(acc)
+        for r in range(PACK):
+            mx_pass(s_acc[r], wg_p, r, zg_p, False, True)
+            nc.scalar.copy(out=s[:, r, :], in_=s_acc[r][:])
+
+        out_1_planes = out_1.rearrange("(p t) n -> p t n", t=PACK)
+        for t in range(PACK):
+            nc.vector.tensor_tensor(windows[t][:].indirect(offsets[:]), dr[:, t, :], one_less_g[:, t, :], ALU.mult)
+            nc.sync.dma_start(out_1_planes[:, t, :], windows[t][:])
+        for r in range(PACK):
+            nc.vector.tensor_copy(windows[r][:].indirect(offsets[:]), s[:, r, :])
+            nc.sync.dma_start(out_0[r * P : (r + 1) * P, :], windows[r][:])

@@ -5,6 +5,7 @@ import concourse.mybir as mybir
 F32 = mybir.dt.float32
 BF16 = mybir.dt.bfloat16
 U32 = mybir.dt.uint32
+I32 = mybir.dt.int32
 U16 = mybir.dt.uint16
 U8 = mybir.dt.uint8
 E4M3 = mybir.dt.float8_e4m3fn_x4
@@ -17,7 +18,7 @@ PACK = 4
 K = 512
 SLOTS = 512
 TOKENS = 1024
-HALF = 256
+WINDOWS = 3
 FLOPS = 3 * 2 * K * K * SLOTS
 
 
@@ -32,9 +33,9 @@ def tile_attend_ghighw_kernel(tc, dy, wo, gT, cT, xT, wg, wc, offs, out_0, out_1
         nc.sync.dma_start(offsets[:], offs)
 
         windows = []
-        for t in range(PACK):
+        for t in range(WINDOWS):
             window = sb.tile([P, TOKENS], F32, name="window%d" % t)
-            nc.vector.memset(window[:], 0.0)
+            nc.vector.memset(window[:].bitcast(I32), 0)
             windows.append(window)
 
         def load_plane(table, label, t):
@@ -45,7 +46,7 @@ def tile_attend_ghighw_kernel(tc, dy, wo, gT, cT, xT, wg, wc, offs, out_0, out_1
         def load_columns(matrix, label, first, count):
             raw = sb.tile([P, PACK, count], F32, name="%s_raw%d" % (label, first))
             nc.sync.dma_start(raw[:], matrix.rearrange("(p j) n -> p j n", j=PACK)[:, :, first : first + count])
-            return raw
+            return raw[:]
 
         def packed_tiles(label):
             grouped = sb.tile([P, K, PACK], BF16, name=label + "_grouped", align_bytes=64)
@@ -56,14 +57,7 @@ def tile_attend_ghighw_kernel(tc, dy, wo, gT, cT, xT, wg, wc, offs, out_0, out_1
         def group(grouped, raw, first, count):
             nc.scalar.copy(
                 out=grouped[:, first : first + count, :].rearrange("p (c i) j -> p c j i", i=4),
-                in_=raw[:].rearrange("p j (c i) -> p c j i", i=4),
-            )
-
-        def group_dealt(grouped, raw, first, count):
-            dealt = grouped[:].rearrange("p (t m) j -> p m j t", t=PACK)
-            nc.scalar.copy(
-                out=dealt[:, first // PACK : (first + count) // PACK, :, :],
-                in_=raw[:].rearrange("p j (m t) -> p m j t", t=PACK),
+                in_=raw.rearrange("p j (c i) -> p c j i", i=4),
             )
 
         def quantize(packed, fmt):
@@ -88,11 +82,12 @@ def tile_attend_ghighw_kernel(tc, dy, wo, gT, cT, xT, wg, wc, offs, out_0, out_1
         c = sb.tile([P, PACK, SLOTS], F32, name="c")
         x_less_c = sb.tile([P, PACK, SLOTS], F32, name="x_less_c")
         c_sq = sb.tile([P, PACK, SLOTS], F32, name="c_sq")
-        one_less_csq = sb.tile([P, PACK, SLOTS], F32, name="one_less_csq")
         one_less_g = sb.tile([P, PACK, SLOTS], F32, name="one_less_g")
         h = sb.tile([P, PACK, SLOTS], F32, name="h")
         u = sb.tile([P, PACK, SLOTS], F32, name="u")
-        dr = sb.tile([P, PACK, SLOTS], F32, name="dr")
+        dr = sb.tile([P, PACK - 1, SLOTS], F32, name="dr")
+        zc_planes = sb.tile([P, PACK, SLOTS], BF16, name="zc_planes")
+        zg_planes = sb.tile([P, PACK, SLOTS], BF16, name="zg_planes", tag="late")
         s = sb.tile([P, PACK, SLOTS], F32, name="s")
 
         dy_p = packed_tiles("dy")
@@ -113,17 +108,24 @@ def tile_attend_ghighw_kernel(tc, dy, wo, gT, cT, xT, wg, wc, offs, out_0, out_1
                 h[:, t, :], g[:, t, :], 1.0, x_less_c[:, t, :], op0=ALU.subtract, op1=ALU.mult
             )
             nc.scalar.activation(c_sq[:, t, :], c[:, t, :], ACT.Square)
-            nc.scalar.activation(one_less_csq[:, t, :], c_sq[:, t, :], ACT.Copy, bias=1.0, scale=-1.0)
             nc.scalar.activation(one_less_g[:, t, :], g[:, t, :], ACT.Copy, bias=1.0, scale=-1.0)
 
+        dy_raw = sb.tile([P, PACK, SLOTS], F32, name="dy_raw")
+        dy_rows = dy.rearrange("(p j) n -> p j n", j=PACK)
         gather_plane(0)
-        group(dy_p[0], load_columns(dy, "dy", 0, HALF), 0, HALF)
+        nc.sync.dma_start(dy_raw[:, 0:2, :], dy_rows[:, 0:2, :])
         gather_plane(1)
-        group(dy_p[0], load_columns(dy, "dy", HALF, HALF), HALF, HALF)
+        nc.sync.dma_start(dy_raw[:, 2:4, :], dy_rows[:, 2:4, :])
+        group(dy_p[0], dy_raw[:], 0, SLOTS)
         quantize(dy_p, E5M2)
         gather_plane(2)
-        for first in (0, HALF):
-            group_dealt(wo_p[0], load_columns(wo, "wo", first, HALF), first, HALF)
+        wo_dealt = wo_p[0][:].rearrange("p (t m) j -> p m j t", t=PACK)
+        for first in (0, K // 2):
+            wo_raw = load_columns(wo, "wo", first, K // 2)
+            nc.scalar.copy(
+                out=wo_dealt[:, first // PACK : (first + K // 2) // PACK, :, :],
+                in_=wo_raw.rearrange("p j (m t) -> p m j t", t=PACK),
+            )
         quantize(wo_p, E4M3)
         dr_acc = []
         for t in range(PACK):
@@ -133,23 +135,18 @@ def tile_attend_ghighw_kernel(tc, dy, wo, gT, cT, xT, wg, wc, offs, out_0, out_1
         gather_plane(3)
 
         for t in range(PACK):
-            nc.vector.tensor_tensor(u[:, t, :], dr_acc[t][:], g[:, t, :], ALU.mult)
+            nc.vector.scalar_tensor_tensor(u[:, t, :], dr_acc[t][:], -1.0, g[:, t, :], op0=ALU.mult, op1=ALU.mult)
+        for t in range(PACK - 1):
+            nc.scalar.copy(out=dr[:, t, :], in_=dr_acc[t][:])
+        nc.vector.scalar_tensor_tensor(zc_planes[:], c_sq[:], 1.0, u[:], op0=ALU.subtract, op1=ALU.mult)
+        nc.vector.scalar_tensor_tensor(zg_planes[:], u[:], -1.0, h[:], op0=ALU.mult, op1=ALU.mult)
         group(wc_p[0], load_columns(wc, "wc", 0, K), 0, K)
         group(wg_p[0], load_columns(wg, "wg", 0, K), 0, K)
-        for t in range(PACK):
-            nc.scalar.copy(out=dr[:, t, :], in_=dr_acc[t][:])
-
-        for packed, factor in ((zc_p, one_less_csq), (zg_p, h)):
-            nc.vector.tensor_tensor(
-                packed[0][:].rearrange("p (n i) t -> p n t i", i=2),
-                u[:].rearrange("p t (n i) -> p n t i", i=2),
-                factor[:].rearrange("p t (n i) -> p n t i", i=2),
-                ALU.mult,
-            )
         quantize(wc_p, E4M3)
-        quantize(zc_p, E5M2)
         quantize(wg_p, E4M3)
-        quantize(zg_p, E5M2)
+        for packed, planes in ((zc_p, zc_planes), (zg_p, zg_planes)):
+            group(packed[0], planes[:], 0, SLOTS)
+            quantize(packed, E5M2)
 
         s_acc = []
         for r in range(PACK):
@@ -158,12 +155,17 @@ def tile_attend_ghighw_kernel(tc, dy, wo, gT, cT, xT, wg, wc, offs, out_0, out_1
             s_acc.append(acc)
         for r in range(PACK):
             mx_pass(s_acc[r], wg_p, r, zg_p, False, True)
-            nc.scalar.copy(out=s[:, r, :], in_=s_acc[r][:])
 
         out_1_planes = out_1.rearrange("(p t) n -> p t n", t=PACK)
-        for t in range(PACK):
+        for t in range(PACK - 1):
             nc.vector.tensor_tensor(windows[t][:].indirect(offsets[:]), dr[:, t, :], one_less_g[:, t, :], ALU.mult)
             nc.sync.dma_start(out_1_planes[:, t, :], windows[t][:])
+        last = PACK - 1
+        dr_last = sb.tile([P, SLOTS], F32, name="dr_last", tag="late")
+        nc.scalar.copy(out=dr_last[:], in_=dr_acc[last][:])
+        nc.vector.tensor_tensor(windows[0][:].indirect(offsets[:]), dr_last[:], one_less_g[:, last, :], ALU.mult)
+        nc.sync.dma_start(out_1_planes[:, last, :], windows[0][:])
         for r in range(PACK):
-            nc.vector.tensor_copy(windows[r][:].indirect(offsets[:]), s[:, r, :])
-            nc.sync.dma_start(out_0[r * P : (r + 1) * P, :], windows[r][:])
+            nc.scalar.copy(out=s[:, r, :], in_=s_acc[r][:])
+            nc.vector.tensor_copy(windows[(PACK + r) % WINDOWS][:].indirect(offsets[:]), s[:, r, :])
+            nc.sync.dma_start(out_0[r * P : (r + 1) * P, :], windows[(PACK + r) % WINDOWS][:])

@@ -82,32 +82,38 @@ def tile_attend_ghighw_kernel(tc, dy, wo, gT, cT, xT, wg, wc, offs, out_0, out_1
         c = sb.tile([P, PACK, SLOTS], F32, name="c")
         x_less_c = sb.tile([P, PACK, SLOTS], F32, name="x_less_c")
         c_sq = sb.tile([P, PACK, SLOTS], F32, name="c_sq")
+        one_less_csq = sb.tile([P, PACK, SLOTS], F32, name="one_less_csq")
         one_less_g = sb.tile([P, PACK, SLOTS], F32, name="one_less_g")
         h = sb.tile([P, PACK, SLOTS], F32, name="h")
         u = sb.tile([P, PACK, SLOTS], F32, name="u")
-        dr = sb.tile([P, PACK - 1, SLOTS], F32, name="dr")
+        dd = sb.tile([P, PACK - 1, SLOTS], F32, name="dd", tag="dd_then_w", align_bytes=64)
         zc_planes = sb.tile([P, PACK, SLOTS], BF16, name="zc_planes")
         zg_planes = sb.tile([P, PACK, SLOTS], BF16, name="zg_planes", tag="late")
         s = sb.tile([P, PACK, SLOTS], F32, name="s")
 
         dy_p = packed_tiles("dy")
         wo_p = packed_tiles("wo")
-        wg_p = packed_tiles("wg")
-        wc_p = packed_tiles("wc")
         zg_p = packed_tiles("zg")
         zc_p = packed_tiles("zc")
 
+        def gather_g(t):
+            g_rows = load_plane(gT, "g", t)
+            nc.vector.tensor_copy(g[:, t, :], g_rows[:].indirect(offsets[:]))
+
+        def gather_x(t):
+            x_rows = load_plane(xT, "x", t)
+            nc.vector.tensor_tensor(x_less_c[:, t, :], x_rows[:].indirect(offsets[:]), c[:, t, :], ALU.subtract)
+
         def gather_plane(t):
             c_rows = load_plane(cT, "c", t)
-            g_rows = load_plane(gT, "g", t)
-            x_rows = load_plane(xT, "x", t)
             nc.vector.tensor_copy(c[:, t, :], c_rows[:].indirect(offsets[:]))
-            nc.vector.tensor_copy(g[:, t, :], g_rows[:].indirect(offsets[:]))
-            nc.vector.tensor_tensor(x_less_c[:, t, :], x_rows[:].indirect(offsets[:]), c[:, t, :], ALU.subtract)
+            for gather in (gather_g, gather_x) if t < PACK - 1 else (gather_x, gather_g):
+                gather(t)
             nc.vector.scalar_tensor_tensor(
                 h[:, t, :], g[:, t, :], 1.0, x_less_c[:, t, :], op0=ALU.subtract, op1=ALU.mult
             )
             nc.scalar.activation(c_sq[:, t, :], c[:, t, :], ACT.Square)
+            nc.scalar.activation(one_less_csq[:, t, :], c_sq[:, t, :], ACT.Copy, bias=1.0, scale=-1.0)
             nc.scalar.activation(one_less_g[:, t, :], g[:, t, :], ACT.Copy, bias=1.0, scale=-1.0)
 
         dy_raw = sb.tile([P, PACK, SLOTS], F32, name="dy_raw")
@@ -133,33 +139,44 @@ def tile_attend_ghighw_kernel(tc, dy, wo, gT, cT, xT, wg, wc, offs, out_0, out_1
             mx_pass(acc, wo_p, t, dy_p, True, True)
             dr_acc.append(acc)
         gather_plane(3)
+        wc_raw = load_columns(wc, "wc", 0, K)
+        wg_raw = load_columns(wg, "wg", 0, K)
 
         for t in range(PACK):
-            nc.vector.scalar_tensor_tensor(u[:, t, :], dr_acc[t][:], -1.0, g[:, t, :], op0=ALU.mult, op1=ALU.mult)
+            nc.vector.tensor_tensor(u[:, t, :], dr_acc[t][:], g[:, t, :], ALU.mult)
+        nc.gpsimd.tensor_tensor(zc_planes[:], u[:], one_less_csq[:], ALU.mult)
+        for first in (0, SLOTS // 2):
+            cols = slice(first, first + SLOTS // 2)
+            nc.gpsimd.tensor_tensor(zg_planes[:, :, cols], u[:, :, cols], h[:, :, cols], ALU.mult)
+
+        out_1_planes = out_1.rearrange("(p t) n -> p t n", t=PACK)
         for t in range(PACK - 1):
-            nc.scalar.copy(out=dr[:, t, :], in_=dr_acc[t][:])
-        nc.vector.scalar_tensor_tensor(zc_planes[:], c_sq[:], 1.0, u[:], op0=ALU.subtract, op1=ALU.mult)
-        nc.vector.scalar_tensor_tensor(zg_planes[:], u[:], -1.0, h[:], op0=ALU.mult, op1=ALU.mult)
-        group(wc_p[0], load_columns(wc, "wc", 0, K), 0, K)
-        group(wg_p[0], load_columns(wg, "wg", 0, K), 0, K)
-        quantize(wc_p, E4M3)
-        quantize(wg_p, E4M3)
-        for packed, planes in ((zc_p, zc_planes), (zg_p, zg_planes)):
-            group(packed[0], planes[:], 0, SLOTS)
-            quantize(packed, E5M2)
+            nc.vector.tensor_tensor(dd[:, t, :], dr_acc[t][:], one_less_g[:, t, :], ALU.mult)
+        for t in range(PACK - 1):
+            nc.vector.tensor_copy(windows[t][:].indirect(offsets[:]), dd[:, t, :])
+            nc.sync.dma_start(out_1_planes[:, t, :], windows[t][:])
+
+        w_grouped = sb.tile([P, 2 * K, PACK], BF16, name="w_grouped", align_bytes=64)
+        w_codes = sb.tile([P, 2 * K], U32, name="w_codes", tag="dd_then_w", align_bytes=64)
+        w_scales = sb.tile([P, 2 * K], U8, name="w_scales", align_bytes=64)
+        w_p = (w_grouped, w_codes, w_scales)
+        group(w_grouped, wc_raw, 0, K)
+        group(w_grouped, wg_raw, K, K)
+        quantize(w_p, E4M3)
+        group(zc_p[0], zc_planes[:], 0, SLOTS)
+        quantize(zc_p, E5M2)
+        for first in (0, SLOTS // 2):
+            group(zg_p[0], zg_planes[:, :, first : first + SLOTS // 2], first, SLOTS // 2)
+        quantize(zg_p, E5M2)
 
         s_acc = []
         for r in range(PACK):
             acc = psum.tile([P, SLOTS], F32, name="s_acc%d" % r)
-            mx_pass(acc, wc_p, r, zc_p, True, False)
+            mx_pass(acc, w_p, r, zc_p, True, False)
             s_acc.append(acc)
         for r in range(PACK):
-            mx_pass(s_acc[r], wg_p, r, zg_p, False, True)
+            mx_pass(s_acc[r], w_p, PACK + r, zg_p, False, True)
 
-        out_1_planes = out_1.rearrange("(p t) n -> p t n", t=PACK)
-        for t in range(PACK - 1):
-            nc.vector.tensor_tensor(windows[t][:].indirect(offsets[:]), dr[:, t, :], one_less_g[:, t, :], ALU.mult)
-            nc.sync.dma_start(out_1_planes[:, t, :], windows[t][:])
         last = PACK - 1
         dr_last = sb.tile([P, SLOTS], F32, name="dr_last", tag="late")
         nc.scalar.copy(out=dr_last[:], in_=dr_acc[last][:])

@@ -80,7 +80,7 @@ def tile_attend_ghighw_kernel(tc, dy, wo, gT, cT, xT, wg, wc, offs, out_0, out_1
 
         g = sb.tile([P, PACK, SLOTS], F32, name="g")
         c = sb.tile([P, PACK, SLOTS], F32, name="c")
-        x_less_c = sb.tile([P, PACK, SLOTS], F32, name="x_less_c")
+        x_less_c = sb.tile([P, PACK - 1, SLOTS], F32, name="x_less_c")
         c_sq = sb.tile([P, PACK, SLOTS], F32, name="c_sq")
         one_less_csq = sb.tile([P, PACK, SLOTS], F32, name="one_less_csq")
         one_less_g = sb.tile([P, PACK, SLOTS], F32, name="one_less_g")
@@ -96,25 +96,24 @@ def tile_attend_ghighw_kernel(tc, dy, wo, gT, cT, xT, wg, wc, offs, out_0, out_1
         zg_p = packed_tiles("zg")
         zc_p = packed_tiles("zc")
 
-        def gather_g(t):
-            g_rows = load_plane(gT, "g", t)
-            nc.vector.tensor_copy(g[:, t, :], g_rows[:].indirect(offsets[:]))
-
-        def gather_x(t):
-            x_rows = load_plane(xT, "x", t)
-            nc.vector.tensor_tensor(x_less_c[:, t, :], x_rows[:].indirect(offsets[:]), c[:, t, :], ALU.subtract)
-
-        def gather_plane(t):
+        def gather_c(t):
             c_rows = load_plane(cT, "c", t)
             nc.vector.tensor_copy(c[:, t, :], c_rows[:].indirect(offsets[:]))
-            for gather in (gather_g, gather_x) if t < PACK - 1 else (gather_x, gather_g):
-                gather(t)
+            nc.scalar.activation(c_sq[:, t, :], c[:, t, :], ACT.Square)
+            nc.scalar.activation(one_less_csq[:, t, :], c_sq[:, t, :], ACT.Copy, bias=1.0, scale=-1.0)
+
+        def gather_g(t, g_rows):
+            nc.vector.tensor_copy(g[:, t, :], g_rows[:].indirect(offsets[:]))
+            nc.scalar.activation(one_less_g[:, t, :], g[:, t, :], ACT.Copy, bias=1.0, scale=-1.0)
+
+        def gather_plane(t):
+            gather_c(t)
+            gather_g(t, load_plane(gT, "g", t))
+            x_rows = load_plane(xT, "x", t)
+            nc.vector.tensor_tensor(x_less_c[:, t, :], x_rows[:].indirect(offsets[:]), c[:, t, :], ALU.subtract)
             nc.vector.scalar_tensor_tensor(
                 h[:, t, :], g[:, t, :], 1.0, x_less_c[:, t, :], op0=ALU.subtract, op1=ALU.mult
             )
-            nc.scalar.activation(c_sq[:, t, :], c[:, t, :], ACT.Square)
-            nc.scalar.activation(one_less_csq[:, t, :], c_sq[:, t, :], ACT.Copy, bias=1.0, scale=-1.0)
-            nc.scalar.activation(one_less_g[:, t, :], g[:, t, :], ACT.Copy, bias=1.0, scale=-1.0)
 
         dy_raw = sb.tile([P, PACK, SLOTS], F32, name="dy_raw")
         dy_rows = dy.rearrange("(p j) n -> p j n", j=PACK)
@@ -138,20 +137,40 @@ def tile_attend_ghighw_kernel(tc, dy, wo, gT, cT, xT, wg, wc, offs, out_0, out_1
             acc = psum.tile([P, SLOTS], F32, name="dr_acc%d" % t)
             mx_pass(acc, wo_p, t, dy_p, True, True)
             dr_acc.append(acc)
-        gather_plane(3)
+        last = PACK - 1
+        gather_c(last)
+        x_rows = load_plane(xT, "x", last)
+        g_rows = load_plane(gT, "g", last)
         wc_raw = load_columns(wc, "wc", 0, K)
         wg_raw = load_columns(wg, "wg", 0, K)
+        x_last = sb.tile([P, SLOTS], F32, name="x_last")
+        c_less_x = sb.tile([P, SLOTS], F32, name="c_less_x")
+        nc.vector.tensor_copy(x_last[:], x_rows[:].indirect(offsets[:]))
+        nc.gpsimd.tensor_tensor(c_less_x[:], c[:, last, :], x_last[:], ALU.subtract)
 
-        for t in range(PACK):
+        def form_u(t):
             nc.vector.tensor_tensor(u[:, t, :], dr_acc[t][:], g[:, t, :], ALU.mult)
-        nc.gpsimd.tensor_tensor(zc_planes[:], u[:], one_less_csq[:], ALU.mult)
+
+        def form_zc(planes):
+            nc.gpsimd.tensor_tensor(zc_planes[:, planes, :], u[:, planes, :], one_less_csq[:, planes, :], ALU.mult)
+
+        for t in range(last):
+            form_u(t)
+        gather_g(last, g_rows)
+        form_u(last)
+        dr_1 = sb.tile([P, SLOTS], F32, name="dr_1")
+        nc.scalar.copy(out=dr_1[:], in_=dr_acc[1][:])
+        nc.gpsimd.tensor_tensor(dd[:, 1, :], dr_1[:], one_less_g[:, 1, :], ALU.mult)
+        for t in (0, 2):
+            nc.vector.tensor_tensor(dd[:, t, :], dr_acc[t][:], one_less_g[:, t, :], ALU.mult)
+        form_zc(slice(0, last))
+        nc.gpsimd.tensor_tensor(h[:, last, :], one_less_g[:, last, :], c_less_x[:], ALU.mult)
+        form_zc(slice(last, PACK))
         for first in (0, SLOTS // 2):
             cols = slice(first, first + SLOTS // 2)
             nc.gpsimd.tensor_tensor(zg_planes[:, :, cols], u[:, :, cols], h[:, :, cols], ALU.mult)
 
         out_1_planes = out_1.rearrange("(p t) n -> p t n", t=PACK)
-        for t in range(PACK - 1):
-            nc.vector.tensor_tensor(dd[:, t, :], dr_acc[t][:], one_less_g[:, t, :], ALU.mult)
         for t in range(PACK - 1):
             nc.vector.tensor_copy(windows[t][:].indirect(offsets[:]), dd[:, t, :])
             nc.sync.dma_start(out_1_planes[:, t, :], windows[t][:])
@@ -177,7 +196,6 @@ def tile_attend_ghighw_kernel(tc, dy, wo, gT, cT, xT, wg, wc, offs, out_0, out_1
         for r in range(PACK):
             mx_pass(s_acc[r], w_p, PACK + r, zg_p, False, True)
 
-        last = PACK - 1
         dr_last = sb.tile([P, SLOTS], F32, name="dr_last", tag="late")
         nc.scalar.copy(out=dr_last[:], in_=dr_acc[last][:])
         nc.vector.tensor_tensor(windows[0][:].indirect(offsets[:]), dr_last[:], one_less_g[:, last, :], ALU.mult)

@@ -19,6 +19,7 @@ K = 512
 SLOTS = 512
 TOKENS = 1024
 WINDOWS = 3
+VECTOR_SHARE = 320
 FLOPS = 3 * 2 * K * K * SLOTS
 
 
@@ -29,42 +30,28 @@ def tile_attend_ghighw_kernel(tc, dy, wo, gT, cT, xT, wg, wc, offs, out_0, out_1
         sb = ctx.enter_context(tc.tile_pool(name="sb", bufs=1))
         psum = ctx.enter_context(tc.psum_pool(name="psum", bufs=1))
 
-        offsets = lists.tile([P, SLOTS // 16], U16, name="offsets")
-        nc.sync.dma_start(offsets[:], offs)
-
-        windows = []
-        for t in range(WINDOWS):
-            window = sb.tile([P, TOKENS], F32, name="window%d" % t)
-            nc.vector.memset(window[:].bitcast(I32), 0)
-            windows.append(window)
-
-        def load_plane(table, label, t):
-            plane = sb.tile([P, TOKENS], F32, name="%s_rows%d" % (label, t))
+        def load_plane(table, label, t, tag=None):
+            plane = sb.tile([P, TOKENS], F32, name="%s_rows%d" % (label, t), tag=tag or "%s_rows%d" % (label, t), align_bytes=64)
             nc.sync.dma_start(plane[:], table.rearrange("(p t) n -> p t n", t=PACK)[:, t, :])
             return plane
 
-        def load_columns(matrix, label, first, count):
-            raw = sb.tile([P, PACK, count], F32, name="%s_raw%d" % (label, first))
-            nc.sync.dma_start(raw[:], matrix.rearrange("(p j) n -> p j n", j=PACK)[:, :, first : first + count])
-            return raw[:]
+        def load_matrix(matrix, label):
+            raw = sb.tile([P, PACK, K], F32, name=label + "_raw")
+            nc.sync.dma_start(raw[:], matrix.rearrange("(p j) n -> p j n", j=PACK))
+            return raw
 
         def packed_tiles(label):
             grouped = sb.tile([P, K, PACK], BF16, name=label + "_grouped", align_bytes=64)
             codes = sb.tile([P, K], U32, name=label + "_codes", align_bytes=64)
             scales = sb.tile([P, K], U8, name=label + "_scales", align_bytes=64)
-            return grouped, codes, scales
+            return grouped[:], codes[:], scales[:]
 
-        def group(grouped, raw, first, count):
-            nc.scalar.copy(
-                out=grouped[:, first : first + count, :].rearrange("p (c i) j -> p c j i", i=4),
-                in_=raw.rearrange("p j (c i) -> p c j i", i=4),
-            )
+        def group(copy, grouped, raw):
+            copy(out=grouped.rearrange("p (c i) j -> p c j i", i=4), in_=raw.rearrange("p j (c i) -> p c j i", i=4))
 
         def quantize(packed, fmt):
             grouped, codes, scales = packed
-            nc.vector.quantize_mx(
-                out=codes[:].bitcast(fmt), scales=scales[:], in_=grouped[:].rearrange("p n j -> p (n j)")
-            )
+            nc.vector.quantize_mx(out=codes.bitcast(fmt), scales=scales, in_=grouped.rearrange("p n j -> p (n j)"))
 
         def mx_pass(acc, weights, tile_index, moving, start, stop):
             cols = slice(tile_index * P, (tile_index + 1) * P)
@@ -72,64 +59,34 @@ def tile_attend_ghighw_kernel(tc, dy, wo, gT, cT, xT, wg, wc, offs, out_0, out_1
                 out=acc[:],
                 lhsT=weights[1][:, cols].bitcast(E4M3),
                 lhsT_scale=weights[2][:, cols],
-                rhs=moving[1][:].bitcast(E5M2),
-                rhs_scale=moving[2][:],
+                rhs=moving[1].bitcast(E5M2),
+                rhs_scale=moving[2],
                 start=start,
                 stop=stop,
             )
 
-        g = sb.tile([P, PACK, SLOTS], F32, name="g")
-        c = sb.tile([P, PACK, SLOTS], F32, name="c")
-        x_less_c = sb.tile([P, PACK - 1, SLOTS], F32, name="x_less_c")
-        c_sq = sb.tile([P, PACK, SLOTS], F32, name="c_sq")
-        one_less_csq = sb.tile([P, PACK, SLOTS], F32, name="one_less_csq")
-        one_less_g = sb.tile([P, PACK, SLOTS], F32, name="one_less_g")
-        h = sb.tile([P, PACK, SLOTS], F32, name="h")
-        u = sb.tile([P, PACK, SLOTS], F32, name="u")
-        dd = sb.tile([P, PACK - 1, SLOTS], F32, name="dd", tag="dd_then_w", align_bytes=64)
-        zc_planes = sb.tile([P, PACK, SLOTS], BF16, name="zc_planes")
-        zg_planes = sb.tile([P, PACK, SLOTS], BF16, name="zg_planes", tag="late")
-        s = sb.tile([P, PACK, SLOTS], F32, name="s")
+        windows = []
+        for t in range(WINDOWS):
+            window = sb.tile([P, TOKENS], F32, name="window%d" % t)
+            nc.vector.memset(window[:].bitcast(I32), 0)
+            windows.append(window)
 
         dy_p = packed_tiles("dy")
         wo_p = packed_tiles("wo")
-        zg_p = packed_tiles("zg")
-        zc_p = packed_tiles("zc")
+        dy_raw = load_matrix(dy, "dy")
+        wo_raw = load_matrix(wo, "wo")
+        offsets = lists.tile([P, SLOTS // 16], U16, name="offsets")
+        nc.sync.dma_start(offsets[:], offs)
 
-        def gather_c(t):
-            c_rows = load_plane(cT, "c", t)
-            nc.vector.tensor_copy(c[:, t, :], c_rows[:].indirect(offsets[:]))
-            nc.scalar.activation(c_sq[:, t, :], c[:, t, :], ACT.Square)
-            nc.scalar.activation(one_less_csq[:, t, :], c_sq[:, t, :], ACT.Copy, bias=1.0, scale=-1.0)
-
-        def gather_g(t, g_rows):
-            nc.vector.tensor_copy(g[:, t, :], g_rows[:].indirect(offsets[:]))
-            nc.scalar.activation(one_less_g[:, t, :], g[:, t, :], ACT.Copy, bias=1.0, scale=-1.0)
-
-        def gather_plane(t):
-            gather_c(t)
-            gather_g(t, load_plane(gT, "g", t))
-            x_rows = load_plane(xT, "x", t)
-            nc.vector.tensor_tensor(x_less_c[:, t, :], x_rows[:].indirect(offsets[:]), c[:, t, :], ALU.subtract)
-            nc.vector.scalar_tensor_tensor(
-                h[:, t, :], g[:, t, :], 1.0, x_less_c[:, t, :], op0=ALU.subtract, op1=ALU.mult
-            )
-
-        dy_raw = sb.tile([P, PACK, SLOTS], F32, name="dy_raw")
-        dy_rows = dy.rearrange("(p j) n -> p j n", j=PACK)
-        gather_plane(0)
-        nc.sync.dma_start(dy_raw[:, 0:2, :], dy_rows[:, 0:2, :])
-        gather_plane(1)
-        nc.sync.dma_start(dy_raw[:, 2:4, :], dy_rows[:, 2:4, :])
-        group(dy_p[0], dy_raw[:], 0, SLOTS)
+        shares = ((nc.vector.tensor_copy, slice(0, VECTOR_SHARE)), (nc.scalar.copy, slice(VECTOR_SHARE, K)))
+        for copy, cols in shares:
+            group(copy, dy_p[0][:, cols, :], dy_raw[:, :, cols])
         quantize(dy_p, E5M2)
-        gather_plane(2)
-        wo_dealt = wo_p[0][:].rearrange("p (t m) j -> p m j t", t=PACK)
-        for first in (0, K // 2):
-            wo_raw = load_columns(wo, "wo", first, K // 2)
-            nc.scalar.copy(
-                out=wo_dealt[:, first // PACK : (first + K // 2) // PACK, :, :],
-                in_=wo_raw.rearrange("p j (m t) -> p m j t", t=PACK),
+        wo_dealt = wo_p[0].rearrange("p (t m) j -> p m j t", t=PACK)
+        for copy, cols in shares:
+            copy(
+                out=wo_dealt[:, cols.start // PACK : cols.stop // PACK, :, :],
+                in_=wo_raw[:, :, cols].rearrange("p j (m t) -> p m j t", t=PACK),
             )
         quantize(wo_p, E4M3)
         dr_acc = []
@@ -137,64 +94,78 @@ def tile_attend_ghighw_kernel(tc, dy, wo, gT, cT, xT, wg, wc, offs, out_0, out_1
             acc = psum.tile([P, SLOTS], F32, name="dr_acc%d" % t)
             mx_pass(acc, wo_p, t, dy_p, True, True)
             dr_acc.append(acc)
+
         last = PACK - 1
-        gather_c(last)
-        x_rows = load_plane(xT, "x", last)
-        g_rows = load_plane(gT, "g", last)
-        wc_raw = load_columns(wc, "wc", 0, K)
-        wg_raw = load_columns(wg, "wg", 0, K)
-        x_last = sb.tile([P, SLOTS], F32, name="x_last")
-        c_less_x = sb.tile([P, SLOTS], F32, name="c_less_x")
-        nc.vector.tensor_copy(x_last[:], x_rows[:].indirect(offsets[:]))
-        nc.gpsimd.tensor_tensor(c_less_x[:], c[:, last, :], x_last[:], ALU.subtract)
+        g = sb.tile([P, PACK, SLOTS], F32, name="g")
+        c = sb.tile([P, PACK, SLOTS], F32, name="c")
+        x = sb.tile([P, PACK, SLOTS], F32, name="x")
+        c_less_x = sb.tile([P, PACK, SLOTS], F32, name="c_less_x")
+        c_sq = sb.tile([P, PACK, SLOTS], F32, name="c_sq")
+        one_less_csq = sb.tile([P, PACK, SLOTS], F32, name="one_less_csq")
+        one_less_g = sb.tile([P, PACK, SLOTS], F32, name="one_less_g")
+        dr = sb.tile([P, last, SLOTS], F32, name="dr")
+        h = sb.tile([P, PACK, SLOTS], F32, name="h")
+        u = sb.tile([P, PACK, SLOTS], F32, name="u")
+        zc_planes = sb.tile([P, PACK, SLOTS], BF16, name="zc_planes")
+        zg_planes = sb.tile([P, PACK, SLOTS], BF16, name="zg_planes", tag="late")
+        s = sb.tile([P, PACK, SLOTS], F32, name="s")
 
-        def form_u(t):
-            nc.vector.tensor_tensor(u[:, t, :], dr_acc[t][:], g[:, t, :], ALU.mult)
-
-        def form_zc(planes):
-            nc.gpsimd.tensor_tensor(zc_planes[:, planes, :], u[:, planes, :], one_less_csq[:, planes, :], ALU.mult)
-
-        for t in range(last):
-            form_u(t)
-        gather_g(last, g_rows)
-        form_u(last)
-        dr_1 = sb.tile([P, SLOTS], F32, name="dr_1")
-        nc.scalar.copy(out=dr_1[:], in_=dr_acc[1][:])
-        nc.gpsimd.tensor_tensor(dd[:, 1, :], dr_1[:], one_less_g[:, 1, :], ALU.mult)
-        for t in (0, 2):
-            nc.vector.tensor_tensor(dd[:, t, :], dr_acc[t][:], one_less_g[:, t, :], ALU.mult)
-        form_zc(slice(0, last))
-        nc.gpsimd.tensor_tensor(h[:, last, :], one_less_g[:, last, :], c_less_x[:], ALU.mult)
-        form_zc(slice(last, PACK))
+        for t in range(PACK):
+            g_rows = load_plane(gT, "g", t)
+            c_rows = load_plane(cT, "c", t)
+            x_rows = load_plane(xT, "x", t, "held" if t == last else None)
+            nc.vector.tensor_copy(g[:, t, :], g_rows[:].indirect(offsets[:]))
+            if t < last:
+                nc.scalar.copy(out=dr[:, t, :], in_=dr_acc[t][:])
+                nc.gpsimd.tensor_tensor(u[:, t, :], dr[:, t, :], g[:, t, :], ALU.mult)
+            nc.scalar.activation(one_less_g[:, t, :], g[:, t, :], ACT.Copy, bias=1.0, scale=-1.0)
+            nc.vector.tensor_copy(c[:, t, :], c_rows[:].indirect(offsets[:]))
+            nc.scalar.activation(c_sq[:, t, :], c[:, t, :], ACT.Square)
+            nc.scalar.activation(one_less_csq[:, t, :], c_sq[:, t, :], ACT.Copy, bias=1.0, scale=-1.0)
+            if t == last:
+                nc.vector.tensor_tensor(u[:, t, :], dr_acc[t][:], g[:, t, :], ALU.mult)
+            nc.vector.tensor_copy(x[:, t, :], x_rows[:].indirect(offsets[:]))
+            nc.gpsimd.tensor_tensor(zc_planes[:, t, :], u[:, t, :], one_less_csq[:, t, :], ALU.mult)
+            nc.gpsimd.tensor_tensor(c_less_x[:, t, :], c[:, t, :], x[:, t, :], ALU.subtract)
+            nc.gpsimd.tensor_tensor(h[:, t, :], one_less_g[:, t, :], c_less_x[:, t, :], ALU.mult)
+        wc_raw = load_matrix(wc, "wc")
+        wg_raw = load_matrix(wg, "wg")
         for first in (0, SLOTS // 2):
             cols = slice(first, first + SLOTS // 2)
             nc.gpsimd.tensor_tensor(zg_planes[:, :, cols], u[:, :, cols], h[:, :, cols], ALU.mult)
 
+        dd = sb.tile([P, last, SLOTS], F32, name="dd", tag="held", align_bytes=64)
+        for t in range(last):
+            nc.vector.tensor_tensor(dd[:, t, :], dr_acc[t][:], one_less_g[:, t, :], ALU.mult)
         out_1_planes = out_1.rearrange("(p t) n -> p t n", t=PACK)
-        for t in range(PACK - 1):
+        for t in range(last):
             nc.vector.tensor_copy(windows[t][:].indirect(offsets[:]), dd[:, t, :])
             nc.sync.dma_start(out_1_planes[:, t, :], windows[t][:])
 
+        late_codes = sb.tile([P, 3 * K], U32, name="late_codes", tag="held", align_bytes=64)
         w_grouped = sb.tile([P, 2 * K, PACK], BF16, name="w_grouped", align_bytes=64)
-        w_codes = sb.tile([P, 2 * K], U32, name="w_codes", tag="dd_then_w", align_bytes=64)
         w_scales = sb.tile([P, 2 * K], U8, name="w_scales", align_bytes=64)
-        w_p = (w_grouped, w_codes, w_scales)
-        group(w_grouped, wc_raw, 0, K)
-        group(w_grouped, wg_raw, K, K)
+        w_p = (w_grouped[:], late_codes[:, 0 : 2 * K], w_scales[:])
+        zc_grouped = sb.tile([P, K, PACK], BF16, name="zc_grouped", align_bytes=64)
+        zc_scales = sb.tile([P, K], U8, name="zc_scales", align_bytes=64)
+        zc_p = (zc_grouped[:], late_codes[:, 2 * K : 3 * K], zc_scales[:])
+        zg_p = packed_tiles("zg")
+        group(nc.scalar.copy, w_grouped[:, 0:K, :], wc_raw[:])
+        group(nc.scalar.copy, w_grouped[:, K : 2 * K, :], wg_raw[:])
         quantize(w_p, E4M3)
-        group(zc_p[0], zc_planes[:], 0, SLOTS)
+        group(nc.scalar.copy, zc_p[0], zc_planes[:])
         quantize(zc_p, E5M2)
         for first in (0, SLOTS // 2):
-            group(zg_p[0], zg_planes[:, :, first : first + SLOTS // 2], first, SLOTS // 2)
+            cols = slice(first, first + SLOTS // 2)
+            group(nc.scalar.copy, zg_p[0][:, cols, :], zg_planes[:, :, cols])
         quantize(zg_p, E5M2)
 
         s_acc = []
         for r in range(PACK):
             acc = psum.tile([P, SLOTS], F32, name="s_acc%d" % r)
             mx_pass(acc, w_p, r, zc_p, True, False)
+            mx_pass(acc, w_p, PACK + r, zg_p, False, True)
             s_acc.append(acc)
-        for r in range(PACK):
-            mx_pass(s_acc[r], w_p, PACK + r, zg_p, False, True)
 
         dr_last = sb.tile([P, SLOTS], F32, name="dr_last", tag="late")
         nc.scalar.copy(out=dr_last[:], in_=dr_acc[last][:])

@@ -36,7 +36,7 @@ def tile_attend_ghighw_kernel(tc, dy, wo, gT, cT, xT, wg, wc, offs, out_0, out_1
             return plane
 
         def load_matrix(matrix, label):
-            raw = sb.tile([P, PACK, K], F32, name=label + "_raw")
+            raw = sb.tile([P, PACK, K], F32, name=label + "_raw", tag=label + "_raw", align_bytes=64)
             nc.sync.dma_start(raw[:], matrix.rearrange("(p j) n -> p j n", j=PACK))
             return raw
 
@@ -99,65 +99,75 @@ def tile_attend_ghighw_kernel(tc, dy, wo, gT, cT, xT, wg, wc, offs, out_0, out_1
         g = sb.tile([P, PACK, SLOTS], F32, name="g")
         c = sb.tile([P, PACK, SLOTS], F32, name="c")
         x = sb.tile([P, PACK, SLOTS], F32, name="x")
-        c_less_x = sb.tile([P, PACK, SLOTS], F32, name="c_less_x")
-        c_sq = sb.tile([P, PACK, SLOTS], F32, name="c_sq")
-        one_less_csq = sb.tile([P, PACK, SLOTS], F32, name="one_less_csq")
-        one_less_g = sb.tile([P, PACK, SLOTS], F32, name="one_less_g")
+        left = sb.tile([P, PACK, 2, SLOTS], F32, name="left")
+        right = sb.tile([P, PACK, 2, SLOTS], F32, name="right")
+        products = sb.tile([P, PACK, 2, SLOTS], F32, name="products")
+        u, one_less_g = left[:, :, 0, :], left[:, :, 1, :]
+        one_less_csq, c_less_x = right[:, :, 0, :], right[:, :, 1, :]
+        zc_planes, h = products[:, :, 0, :], products[:, :, 1, :]
         dr = sb.tile([P, last, SLOTS], F32, name="dr")
-        h = sb.tile([P, PACK, SLOTS], F32, name="h")
-        u = sb.tile([P, PACK, SLOTS], F32, name="u")
-        zc_planes = sb.tile([P, PACK, SLOTS], BF16, name="zc_planes")
-        zg_planes = sb.tile([P, PACK, SLOTS], BF16, name="zg_planes", tag="late")
         s = sb.tile([P, PACK, SLOTS], F32, name="s")
 
-        for t in range(PACK):
-            g_rows = load_plane(gT, "g", t)
+        def gather_c(t):
             c_rows = load_plane(cT, "c", t)
-            x_rows = load_plane(xT, "x", t, "held" if t == last else None)
+            nc.vector.tensor_copy(c[:, t, :], c_rows[:].indirect(offsets[:]))
+            c_sq = sb.tile([P, SLOTS], F32, name="c_sq%d" % t, tag="held" if t == last else "c_sq%d" % t, align_bytes=64)
+            nc.scalar.activation(c_sq[:], c[:, t, :], ACT.Square)
+            nc.scalar.activation(one_less_csq[:, t, :], c_sq[:], ACT.Copy, bias=1.0, scale=-1.0)
+
+        for t in range(PACK):
+            if t == last:
+                gather_c(t)
+            g_rows = load_plane(gT, "g", t, "g_then_dd" if t == last else None)
             nc.vector.tensor_copy(g[:, t, :], g_rows[:].indirect(offsets[:]))
             if t < last:
                 nc.scalar.copy(out=dr[:, t, :], in_=dr_acc[t][:])
                 nc.gpsimd.tensor_tensor(u[:, t, :], dr[:, t, :], g[:, t, :], ALU.mult)
             nc.scalar.activation(one_less_g[:, t, :], g[:, t, :], ACT.Copy, bias=1.0, scale=-1.0)
-            nc.vector.tensor_copy(c[:, t, :], c_rows[:].indirect(offsets[:]))
-            nc.scalar.activation(c_sq[:, t, :], c[:, t, :], ACT.Square)
-            nc.scalar.activation(one_less_csq[:, t, :], c_sq[:, t, :], ACT.Copy, bias=1.0, scale=-1.0)
+            if t < last:
+                gather_c(t)
+            x_rows = load_plane(xT, "x", t, "x_then_w" if t == last else None)
+            nc.vector.tensor_copy(x[:, t, :], x_rows[:].indirect(offsets[:]))
             if t == last:
                 nc.vector.tensor_tensor(u[:, t, :], dr_acc[t][:], g[:, t, :], ALU.mult)
-            nc.vector.tensor_copy(x[:, t, :], x_rows[:].indirect(offsets[:]))
-            nc.gpsimd.tensor_tensor(zc_planes[:, t, :], u[:, t, :], one_less_csq[:, t, :], ALU.mult)
             nc.gpsimd.tensor_tensor(c_less_x[:, t, :], c[:, t, :], x[:, t, :], ALU.subtract)
-            nc.gpsimd.tensor_tensor(h[:, t, :], one_less_g[:, t, :], c_less_x[:, t, :], ALU.mult)
+            nc.gpsimd.tensor_tensor(products[:, t, :, :], left[:, t, :, :], right[:, t, :, :], ALU.mult)
         wc_raw = load_matrix(wc, "wc")
         wg_raw = load_matrix(wg, "wg")
-        for first in (0, SLOTS // 2):
-            cols = slice(first, first + SLOTS // 2)
-            nc.gpsimd.tensor_tensor(zg_planes[:, :, cols], u[:, :, cols], h[:, :, cols], ALU.mult)
+        halves = [slice(first, first + SLOTS // 2) for first in (0, SLOTS // 2)]
+        zg_halves = []
+        for number, cols in enumerate(halves):
+            zg_half = sb.tile([P, PACK, SLOTS // 2], BF16, name="zg_half%d" % number, tag="zg_half%d" % number)
+            nc.gpsimd.tensor_tensor(zg_half[:], u[:, :, cols], h[:, :, cols], ALU.mult)
+            zg_halves.append(zg_half)
 
-        dd = sb.tile([P, last, SLOTS], F32, name="dd", tag="held", align_bytes=64)
+        dd_first = sb.tile([P, 2, SLOTS], F32, name="dd_first", tag="held", align_bytes=64)
+        dd_third = sb.tile([P, SLOTS], F32, name="dd_third", tag="g_then_dd", align_bytes=64)
+        dd = [dd_first[:, 0, :], dd_first[:, 1, :], dd_third[:]]
         for t in range(last):
-            nc.vector.tensor_tensor(dd[:, t, :], dr_acc[t][:], one_less_g[:, t, :], ALU.mult)
+            nc.vector.tensor_tensor(dd[t], dr_acc[t][:], one_less_g[:, t, :], ALU.mult)
         out_1_planes = out_1.rearrange("(p t) n -> p t n", t=PACK)
         for t in range(last):
-            nc.vector.tensor_copy(windows[t][:].indirect(offsets[:]), dd[:, t, :])
+            nc.vector.tensor_copy(windows[t][:].indirect(offsets[:]), dd[t])
             nc.sync.dma_start(out_1_planes[:, t, :], windows[t][:])
 
         late_codes = sb.tile([P, 3 * K], U32, name="late_codes", tag="held", align_bytes=64)
-        w_grouped = sb.tile([P, 2 * K, PACK], BF16, name="w_grouped", align_bytes=64)
+        w_grouped = sb.tile([P, 2 * K, PACK], BF16, name="w_grouped", tag="x_then_w", align_bytes=64)
         w_scales = sb.tile([P, 2 * K], U8, name="w_scales", align_bytes=64)
         w_p = (w_grouped[:], late_codes[:, 0 : 2 * K], w_scales[:])
-        zc_grouped = sb.tile([P, K, PACK], BF16, name="zc_grouped", align_bytes=64)
+        z_grouped = sb.tile([P, 2 * SLOTS, PACK], BF16, name="z_grouped", tag="wg_raw", align_bytes=64)
         zc_scales = sb.tile([P, K], U8, name="zc_scales", align_bytes=64)
-        zc_p = (zc_grouped[:], late_codes[:, 2 * K : 3 * K], zc_scales[:])
-        zg_p = packed_tiles("zg")
+        zc_p = (z_grouped[:, 0:SLOTS, :], late_codes[:, 2 * K : 3 * K], zc_scales[:])
         group(nc.scalar.copy, w_grouped[:, 0:K, :], wc_raw[:])
         group(nc.scalar.copy, w_grouped[:, K : 2 * K, :], wg_raw[:])
         quantize(w_p, E4M3)
-        group(nc.scalar.copy, zc_p[0], zc_planes[:])
+        group(nc.scalar.copy, zc_p[0], zc_planes)
         quantize(zc_p, E5M2)
-        for first in (0, SLOTS // 2):
-            cols = slice(first, first + SLOTS // 2)
-            group(nc.scalar.copy, zg_p[0][:, cols, :], zg_planes[:, :, cols])
+        zg_codes = sb.tile([P, SLOTS], U32, name="zg_codes", align_bytes=64)
+        zg_scales = sb.tile([P, SLOTS], U8, name="zg_scales", align_bytes=64)
+        zg_p = (z_grouped[:, SLOTS : 2 * SLOTS, :], zg_codes[:], zg_scales[:])
+        for cols, zg_half in zip(halves, zg_halves):
+            group(nc.scalar.copy, zg_p[0][:, cols, :], zg_half[:])
         quantize(zg_p, E5M2)
 
         s_acc = []
@@ -167,7 +177,7 @@ def tile_attend_ghighw_kernel(tc, dy, wo, gT, cT, xT, wg, wc, offs, out_0, out_1
             mx_pass(acc, w_p, PACK + r, zg_p, False, True)
             s_acc.append(acc)
 
-        dr_last = sb.tile([P, SLOTS], F32, name="dr_last", tag="late")
+        dr_last = sb.tile([P, SLOTS], F32, name="dr_last", tag="zg_half1")
         nc.scalar.copy(out=dr_last[:], in_=dr_acc[last][:])
         nc.vector.tensor_tensor(windows[0][:].indirect(offsets[:]), dr_last[:], one_less_g[:, last, :], ALU.mult)
         nc.sync.dma_start(out_1_planes[:, last, :], windows[0][:])

@@ -101,7 +101,7 @@ def tile_attend_ghighw_kernel(tc, dy, wo, gT, cT, xT, wg, wc, offs, out_0, out_1
         x = sb.tile([P, PACK, SLOTS], F32, name="x")
         left = sb.tile([P, PACK, 2, SLOTS], F32, name="left")
         right = sb.tile([P, PACK, 2, SLOTS], F32, name="right")
-        products = sb.tile([P, PACK, 2, SLOTS], F32, name="products")
+        products = sb.tile([P, PACK, 2, SLOTS], F32, name="products", tag="products", align_bytes=64)
         u, one_less_g = left[:, :, 0, :], left[:, :, 1, :]
         one_less_csq, c_less_x = right[:, :, 0, :], right[:, :, 1, :]
         zc_planes, h = products[:, :, 0, :], products[:, :, 1, :]
@@ -129,7 +129,7 @@ def tile_attend_ghighw_kernel(tc, dy, wo, gT, cT, xT, wg, wc, offs, out_0, out_1
             x_rows = load_plane(xT, "x", t, "x_then_w" if t == last else None)
             nc.vector.tensor_copy(x[:, t, :], x_rows[:].indirect(offsets[:]))
             if t == last:
-                nc.vector.tensor_tensor(u[:, t, :], dr_acc[t][:], g[:, t, :], ALU.mult)
+                nc.vector.tensor_tensor(u[:, t, :], g[:, t, :], dr_acc[t][:], ALU.mult)
             nc.gpsimd.tensor_tensor(c_less_x[:, t, :], c[:, t, :], x[:, t, :], ALU.subtract)
             nc.gpsimd.tensor_tensor(products[:, t, :, :], left[:, t, :, :], right[:, t, :, :], ALU.mult)
         wc_raw = load_matrix(wc, "wc")
@@ -145,13 +145,13 @@ def tile_attend_ghighw_kernel(tc, dy, wo, gT, cT, xT, wg, wc, offs, out_0, out_1
         dd_third = sb.tile([P, SLOTS], F32, name="dd_third", tag="g_then_dd", align_bytes=64)
         dd = [dd_first[:, 0, :], dd_first[:, 1, :], dd_third[:]]
         for t in range(last):
-            nc.vector.tensor_tensor(dd[t], dr_acc[t][:], one_less_g[:, t, :], ALU.mult)
+            nc.vector.tensor_tensor(dd[t], one_less_g[:, t, :], dr_acc[t][:], ALU.mult)
         out_1_planes = out_1.rearrange("(p t) n -> p t n", t=PACK)
         for t in range(last):
             nc.vector.tensor_copy(windows[t][:].indirect(offsets[:]), dd[t])
             nc.sync.dma_start(out_1_planes[:, t, :], windows[t][:])
 
-        late_codes = sb.tile([P, 3 * K], U32, name="late_codes", tag="held", align_bytes=64)
+        late_codes = sb.tile([P, 3 * K], U32, name="late_codes", tag="products", align_bytes=64)
         w_grouped = sb.tile([P, 2 * K, PACK], BF16, name="w_grouped", tag="x_then_w", align_bytes=64)
         w_scales = sb.tile([P, 2 * K], U8, name="w_scales", align_bytes=64)
         w_p = (w_grouped[:], late_codes[:, 0 : 2 * K], w_scales[:])

@@ -1,6 +1,7 @@
 from contextlib import ExitStack
 
 import concourse.mybir as mybir
+from concourse.masks import make_identity
 
 F32 = mybir.dt.float32
 BF16 = mybir.dt.bfloat16
@@ -71,6 +72,9 @@ def tile_attend_ghighw_kernel(tc, dy, wo, gT, cT, xT, wg, wc, offs, out_0, out_1
             nc.vector.memset(window[:].bitcast(I32), 0)
             windows.append(window)
 
+        identity = sb.tile([P, P], F32, name="identity")
+        make_identity(nc, identity[:])
+
         dy_p = packed_tiles("dy")
         wo_p = packed_tiles("wo")
         dy_raw = load_matrix(dy, "dy")
@@ -99,60 +103,79 @@ def tile_attend_ghighw_kernel(tc, dy, wo, gT, cT, xT, wg, wc, offs, out_0, out_1
         g = sb.tile([P, PACK, SLOTS], F32, name="g")
         c = sb.tile([P, PACK, SLOTS], F32, name="c")
         x = sb.tile([P, PACK, SLOTS], F32, name="x")
-        left = sb.tile([P, PACK, 2, SLOTS], F32, name="left")
-        right = sb.tile([P, PACK, 2, SLOTS], F32, name="right")
-        products = sb.tile([P, PACK, 2, SLOTS], F32, name="products", tag="products", align_bytes=64)
-        u, one_less_g = left[:, :, 0, :], left[:, :, 1, :]
-        one_less_csq, c_less_x = right[:, :, 0, :], right[:, :, 1, :]
-        zc_planes, h = products[:, :, 0, :], products[:, :, 1, :]
-        dr = sb.tile([P, last, SLOTS], F32, name="dr")
+        u = sb.tile([P, PACK, SLOTS], F32, name="u")
+        one_less_g = sb.tile([P, PACK, SLOTS], F32, name="one_less_g")
+        one_less_csq = sb.tile([P, PACK, SLOTS], F32, name="one_less_csq")
+        c_less_x = sb.tile([P, PACK, SLOTS], F32, name="c_less_x")
+        h = sb.tile([P, PACK, SLOTS], F32, name="h", tag="h_then_codes", align_bytes=64)
+        zc_planes = sb.tile([P, PACK, SLOTS], BF16, name="zc_planes")
+        dr = sb.tile([P, PACK, SLOTS], F32, name="dr")
+        halves = [slice(first, first + SLOTS // 2) for first in (0, SLOTS // 2)]
+        zg_planes = sb.tile([P, 2, PACK, SLOTS // 2], BF16, name="zg_planes", tag="zg_then_dr")
         s = sb.tile([P, PACK, SLOTS], F32, name="s")
 
         def gather_c(t):
             c_rows = load_plane(cT, "c", t)
             nc.vector.tensor_copy(c[:, t, :], c_rows[:].indirect(offsets[:]))
-            c_sq = sb.tile([P, SLOTS], F32, name="c_sq%d" % t, tag="held" if t == last else "c_sq%d" % t, align_bytes=64)
+            c_sq = sb.tile([P, SLOTS], F32, name="c_sq%d" % t)
             nc.scalar.activation(c_sq[:], c[:, t, :], ACT.Square)
             nc.scalar.activation(one_less_csq[:, t, :], c_sq[:], ACT.Copy, bias=1.0, scale=-1.0)
 
-        for t in range(PACK):
-            if t == last:
-                gather_c(t)
-            g_rows = load_plane(gT, "g", t, "g_then_dd" if t == last else None)
+        def gather_g(t):
+            g_rows = load_plane(gT, "g", t)
             nc.vector.tensor_copy(g[:, t, :], g_rows[:].indirect(offsets[:]))
-            if t < last:
-                nc.scalar.copy(out=dr[:, t, :], in_=dr_acc[t][:])
-                nc.gpsimd.tensor_tensor(u[:, t, :], dr[:, t, :], g[:, t, :], ALU.mult)
+            nc.scalar.copy(out=dr[:, t, :], in_=dr_acc[t][:])
+            nc.gpsimd.tensor_tensor(u[:, t, :], dr[:, t, :], g[:, t, :], ALU.mult)
             nc.scalar.activation(one_less_g[:, t, :], g[:, t, :], ACT.Copy, bias=1.0, scale=-1.0)
-            if t < last:
-                gather_c(t)
-            x_rows = load_plane(xT, "x", t, "x_then_w" if t == last else None)
+
+        def gather_x(t):
+            x_rows = load_plane(xT, "x", t, "held" if t == last else None)
             nc.vector.tensor_copy(x[:, t, :], x_rows[:].indirect(offsets[:]))
-            if t == last:
-                nc.vector.tensor_tensor(u[:, t, :], g[:, t, :], dr_acc[t][:], ALU.mult)
-            nc.gpsimd.tensor_tensor(c_less_x[:, t, :], c[:, t, :], x[:, t, :], ALU.subtract)
-            nc.gpsimd.tensor_tensor(products[:, t, :, :], left[:, t, :, :], right[:, t, :, :], ALU.mult)
+            if t == 0:
+                nc.gpsimd.tensor_tensor(c_less_x[:, t, :], c[:, t, :], x[:, t, :], ALU.subtract)
+                return
+            minus_x = sb.tile([P, SLOTS], F32, name="minus_x%d" % t)
+            nc.scalar.activation(minus_x[:], x[:, t, :], ACT.Copy, scale=-1.0)
+            there = psum.tile([P, SLOTS], F32, name="there%d" % t, tag="spare%d" % (2 * (t % 2)))
+            back = psum.tile([P, SLOTS], F32, name="back%d" % t, tag="spare%d" % (2 * (t % 2) + 1))
+            turned = sb.tile([P, SLOTS], F32, name="turned%d" % t)
+            blocks = [slice(j * P, (j + 1) * P) for j in range(SLOTS // P)]
+            for block in blocks:
+                nc.tensor.matmul(there[:, block], c[:, t, block], identity[:], start=True, stop=False, is_transpose=True)
+                nc.tensor.matmul(there[:, block], minus_x[:, block], identity[:], start=False, stop=True, is_transpose=True)
+            nc.scalar.copy(out=turned[:], in_=there[:])
+            for block in blocks:
+                nc.tensor.transpose(back[:, block], turned[:, block], identity[:])
+            nc.scalar.copy(out=c_less_x[:, t, :], in_=back[:])
+
+        for t in range(PACK):
+            for gather in (gather_g, gather_c, gather_x) if t == 0 else (gather_c, gather_x, gather_g):
+                gather(t)
+            nc.gpsimd.tensor_tensor(zc_planes[:, t, :], u[:, t, :], one_less_csq[:, t, :], ALU.mult)
+            nc.gpsimd.tensor_tensor(h[:, t, :], one_less_g[:, t, :], c_less_x[:, t, :], ALU.mult)
+            if t < last:
+                nc.gpsimd.tensor_tensor(
+                    zg_planes[:, :, t, :],
+                    u[:, t, :].rearrange("p (a n) -> p a n", a=2),
+                    h[:, t, :].rearrange("p (a n) -> p a n", a=2),
+                    ALU.mult,
+                )
+            else:
+                for number, cols in enumerate(halves):
+                    nc.gpsimd.tensor_tensor(zg_planes[:, number, t, :], u[:, t, cols], h[:, t, cols], ALU.mult)
         wc_raw = load_matrix(wc, "wc")
         wg_raw = load_matrix(wg, "wg")
-        halves = [slice(first, first + SLOTS // 2) for first in (0, SLOTS // 2)]
-        zg_halves = []
-        for number, cols in enumerate(halves):
-            zg_half = sb.tile([P, PACK, SLOTS // 2], BF16, name="zg_half%d" % number, tag="zg_half%d" % number)
-            nc.gpsimd.tensor_tensor(zg_half[:], u[:, :, cols], h[:, :, cols], ALU.mult)
-            zg_halves.append(zg_half)
 
-        dd_first = sb.tile([P, 2, SLOTS], F32, name="dd_first", tag="held", align_bytes=64)
-        dd_third = sb.tile([P, SLOTS], F32, name="dd_third", tag="g_then_dd", align_bytes=64)
-        dd = [dd_first[:, 0, :], dd_first[:, 1, :], dd_third[:]]
+        dd = sb.tile([P, last, SLOTS], F32, name="dd", tag="held", align_bytes=64)
         for t in range(last):
-            nc.vector.tensor_tensor(dd[t], one_less_g[:, t, :], dr_acc[t][:], ALU.mult)
+            nc.vector.tensor_tensor(dd[:, t, :], one_less_g[:, t, :], dr_acc[t][:], ALU.mult)
         out_1_planes = out_1.rearrange("(p t) n -> p t n", t=PACK)
         for t in range(last):
-            nc.vector.tensor_copy(windows[t][:].indirect(offsets[:]), dd[t])
+            nc.vector.tensor_copy(windows[t][:].indirect(offsets[:]), dd[:, t, :])
             nc.sync.dma_start(out_1_planes[:, t, :], windows[t][:])
 
-        late_codes = sb.tile([P, 3 * K], U32, name="late_codes", tag="products", align_bytes=64)
-        w_grouped = sb.tile([P, 2 * K, PACK], BF16, name="w_grouped", tag="x_then_w", align_bytes=64)
+        late_codes = sb.tile([P, 3 * K], U32, name="late_codes", tag="h_then_codes", align_bytes=64)
+        w_grouped = sb.tile([P, 2 * K, PACK], BF16, name="w_grouped", align_bytes=64)
         w_scales = sb.tile([P, 2 * K], U8, name="w_scales", align_bytes=64)
         w_p = (w_grouped[:], late_codes[:, 0 : 2 * K], w_scales[:])
         z_grouped = sb.tile([P, 2 * SLOTS, PACK], BF16, name="z_grouped", tag="wg_raw", align_bytes=64)
@@ -161,23 +184,23 @@ def tile_attend_ghighw_kernel(tc, dy, wo, gT, cT, xT, wg, wc, offs, out_0, out_1
         group(nc.scalar.copy, w_grouped[:, 0:K, :], wc_raw[:])
         group(nc.scalar.copy, w_grouped[:, K : 2 * K, :], wg_raw[:])
         quantize(w_p, E4M3)
-        group(nc.scalar.copy, zc_p[0], zc_planes)
+        group(nc.scalar.copy, zc_p[0], zc_planes[:])
         quantize(zc_p, E5M2)
         zg_codes = sb.tile([P, SLOTS], U32, name="zg_codes", align_bytes=64)
         zg_scales = sb.tile([P, SLOTS], U8, name="zg_scales", align_bytes=64)
         zg_p = (z_grouped[:, SLOTS : 2 * SLOTS, :], zg_codes[:], zg_scales[:])
-        for cols, zg_half in zip(halves, zg_halves):
-            group(nc.scalar.copy, zg_p[0][:, cols, :], zg_half[:])
+        for number, cols in enumerate(halves):
+            group(nc.scalar.copy, zg_p[0][:, cols, :], zg_planes[:, number, :, :])
         quantize(zg_p, E5M2)
 
         s_acc = []
         for r in range(PACK):
-            acc = psum.tile([P, SLOTS], F32, name="s_acc%d" % r)
+            acc = psum.tile([P, SLOTS], F32, name="s_acc%d" % r, tag="spare%d" % r)
             mx_pass(acc, w_p, r, zc_p, True, False)
             mx_pass(acc, w_p, PACK + r, zg_p, False, True)
             s_acc.append(acc)
 
-        dr_last = sb.tile([P, SLOTS], F32, name="dr_last", tag="zg_half1")
+        dr_last = sb.tile([P, SLOTS], F32, name="dr_last", tag="zg_then_dr")
         nc.scalar.copy(out=dr_last[:], in_=dr_acc[last][:])
         nc.vector.tensor_tensor(windows[0][:].indirect(offsets[:]), dr_last[:], one_less_g[:, last, :], ALU.mult)
         nc.sync.dma_start(out_1_planes[:, last, :], windows[0][:])

@@ -19,8 +19,11 @@ PACK = 4
 K = 512
 SLOTS = 512
 TOKENS = 1024
-WINDOWS = 3
-VECTOR_SHARE = 320
+PLANES = K // P
+BLOCKS = SLOTS // P
+WINDOWS = 4
+LATE_SLOTS = 256
+FIRST_SLOTS = 128
 FLOPS = 3 * 2 * K * K * SLOTS
 
 
@@ -29,182 +32,267 @@ def tile_attend_ghighw_kernel(tc, dy, wo, gT, cT, xT, wg, wc, offs, out_0, out_1
     with ExitStack() as ctx:
         lists = ctx.enter_context(tc.tile_pool(name="lists", bufs=1))
         sb = ctx.enter_context(tc.tile_pool(name="sb", bufs=1))
+        late = ctx.enter_context(tc.tile_pool(name="late", bufs=1))
         psum = ctx.enter_context(tc.psum_pool(name="psum", bufs=1))
+        blocks = [slice(j * P, (j + 1) * P) for j in range(BLOCKS)]
+        last = PLANES - 1
 
-        def load_plane(table, label, t, tag=None):
-            plane = sb.tile([P, TOKENS], F32, name="%s_rows%d" % (label, t), tag=tag or "%s_rows%d" % (label, t), align_bytes=64)
-            nc.sync.dma_start(plane[:], table.rearrange("(p t) n -> p t n", t=PACK)[:, t, :])
-            return plane
-
-        def load_matrix(matrix, label):
-            raw = sb.tile([P, PACK, K], F32, name=label + "_raw", tag=label + "_raw", align_bytes=64)
+        def load_matrix(matrix, label, tag):
+            raw = sb.tile([P, PACK, K], F32, name=label + "_raw", tag=tag, align_bytes=64)
             nc.sync.dma_start(raw[:], matrix.rearrange("(p j) n -> p j n", j=PACK))
             return raw
-
-        def packed_tiles(label):
-            grouped = sb.tile([P, K, PACK], BF16, name=label + "_grouped", align_bytes=64)
-            codes = sb.tile([P, K], U32, name=label + "_codes", align_bytes=64)
-            scales = sb.tile([P, K], U8, name=label + "_scales", align_bytes=64)
-            return grouped[:], codes[:], scales[:]
 
         def group(copy, grouped, raw):
             copy(out=grouped.rearrange("p (c i) j -> p c j i", i=4), in_=raw.rearrange("p j (c i) -> p c j i", i=4))
 
-        def quantize(packed, fmt):
-            grouped, codes, scales = packed
+        def quantize(grouped, codes, scales, fmt):
             nc.vector.quantize_mx(out=codes.bitcast(fmt), scales=scales, in_=grouped.rearrange("p n j -> p (n j)"))
 
-        def mx_pass(acc, weights, tile_index, moving, start, stop):
-            cols = slice(tile_index * P, (tile_index + 1) * P)
-            nc.tensor.matmul_mx(
-                out=acc[:],
-                lhsT=weights[1][:, cols].bitcast(E4M3),
-                lhsT_scale=weights[2][:, cols],
-                rhs=moving[1].bitcast(E5M2),
-                rhs_scale=moving[2],
-                start=start,
-                stop=stop,
-            )
+        def turn(bank, term, start=True, stop=True):
+            for j, block in enumerate(blocks):
+                nc.tensor.matmul(
+                    bank[:, block], term[:, block], identity[:],
+                    start=start and j == 0, stop=stop and j == BLOCKS - 1, is_transpose=True,
+                )
 
         windows = []
-        for t in range(WINDOWS):
-            window = sb.tile([P, TOKENS], F32, name="window%d" % t)
+
+        def zeroed_window(tag):
+            window = sb.tile([P, TOKENS], F32, name="window%d" % len(windows), tag=tag, align_bytes=64)
             nc.vector.memset(window[:].bitcast(I32), 0)
             windows.append(window)
 
+        for w in range(WINDOWS - 1):
+            zeroed_window("window%d" % w)
         identity = sb.tile([P, P], F32, name="identity")
         make_identity(nc, identity[:])
 
-        dy_p = packed_tiles("dy")
-        wo_p = packed_tiles("wo")
-        dy_raw = load_matrix(dy, "dy")
-        wo_raw = load_matrix(wo, "wo")
         offsets = lists.tile([P, SLOTS // 16], U16, name="offsets")
         nc.sync.dma_start(offsets[:], offs)
+        left = sb.tile([P, PLANES, 2, SLOTS], F32, name="left")
+        right = sb.tile([P, PLANES, 2, SLOTS], F32, name="right")
+        made = sb.tile([P, PLANES, 3, SLOTS], F32, name="made", tag="made_then_codes", align_bytes=64)
+        c_sq = sb.tile([P, PLANES, SLOTS], F32, name="c_sq")
+        z_turned = sb.tile([P, 2, BLOCKS, K], BF16, name="z_turned", tag="z_then_dd", align_bytes=64)
 
-        shares = ((nc.vector.tensor_copy, slice(0, VECTOR_SHARE)), (nc.scalar.copy, slice(VECTOR_SHARE, K)))
-        for copy, cols in shares:
-            group(copy, dy_p[0][:, cols, :], dy_raw[:, :, cols])
-        quantize(dy_p, E5M2)
-        wo_dealt = wo_p[0].rearrange("p (t m) j -> p m j t", t=PACK)
-        for copy, cols in shares:
-            copy(
-                out=wo_dealt[:, cols.start // PACK : cols.stop // PACK, :, :],
-                in_=wo_raw[:, :, cols].rearrange("p j (m t) -> p m j t", t=PACK),
+        def rows_tile(label, planes):
+            return sb.tile([P, planes * TOKENS], F32, name=label, tag=label, align_bytes=64)
+
+        def load_plane(rows, table, a):
+            nc.sync.dma_start(rows, table[blocks[a], :])
+
+        def picked_tile(label):
+            return sb.tile([P, SLOTS], F32, name=label, tag=label, align_bytes=64)
+
+        def gather(label, rows):
+            picked = picked_tile(label)
+            nc.vector.tensor_copy(picked[:], rows.indirect(offsets[:]))
+            return picked
+
+        def gather_negated(label, rows):
+            picked = picked_tile(label)
+            nc.vector.tensor_scalar(picked[:], rows.indirect(offsets[:]), -1.0, 0.0, ALU.mult, ALU.add)
+            return picked
+
+        def bring_g(a):
+            rows = rows_tile("g_rows%d" % a, 1)
+            load_plane(rows[:], gT, a)
+            bank = psum.tile([P, SLOTS], F32, name="g_bank%d" % a, tag="bank_g")
+            turn(bank, gather("g_picked%d" % a, rows[:]))
+            nc.scalar.activation(right[:, a, 0, :], bank[:], ACT.Copy, scale=-1.0)
+            if a < 2:
+                nc.scalar.activation(left[:, a, 1, :], bank[:], ACT.Copy, bias=1.0, scale=-1.0)
+
+        def turned(term, label, tag, stop=True):
+            bank = psum.tile([P, SLOTS], F32, name=label, tag=tag)
+            turn(bank, term, True, stop)
+            return bank
+
+        def by_block(ap):
+            return ap.rearrange("p z (j d) -> p z j d", d=P)
+
+        def form_z(a, factors):
+            nc.gpsimd.tensor_tensor(
+                z_turned[:, :, :, blocks[a]], by_block(made[:, a, 0:1, :].to_broadcast([P, 2, SLOTS])), by_block(factors), ALU.mult
             )
-        quantize(wo_p, E4M3)
-        dr_acc = []
-        for t in range(PACK):
-            acc = psum.tile([P, SLOTS], F32, name="dr_acc%d" % t)
-            mx_pass(acc, wo_p, t, dy_p, True, True)
-            dr_acc.append(acc)
 
-        last = PACK - 1
-        g = sb.tile([P, PACK, SLOTS], F32, name="g")
-        c = sb.tile([P, PACK, SLOTS], F32, name="c")
-        x = sb.tile([P, PACK, SLOTS], F32, name="x")
-        u = sb.tile([P, PACK, SLOTS], F32, name="u")
-        one_less_g = sb.tile([P, PACK, SLOTS], F32, name="one_less_g")
-        one_less_csq = sb.tile([P, PACK, SLOTS], F32, name="one_less_csq")
-        c_less_x = sb.tile([P, PACK, SLOTS], F32, name="c_less_x")
-        h = sb.tile([P, PACK, SLOTS], F32, name="h", tag="h_then_codes", align_bytes=64)
-        zc_planes = sb.tile([P, PACK, SLOTS], BF16, name="zc_planes")
-        dr = sb.tile([P, PACK, SLOTS], F32, name="dr")
-        halves = [slice(first, first + SLOTS // 2) for first in (0, SLOTS // 2)]
-        zg_planes = sb.tile([P, 2, PACK, SLOTS // 2], BF16, name="zg_planes", tag="zg_then_dr")
-        s = sb.tile([P, PACK, SLOTS], F32, name="s")
+        def bring_c(a, rows, pick):
+            c = pick("c_picked%d" % a, rows)
+            nc.scalar.activation(c_sq[:, a, :], turned(c, "c_bank%d" % a, "bank_c")[:], ACT.Square)
+            if a < 2:
+                nc.scalar.activation(made[:, a, 2, :], c_sq[:, a, :], ACT.Copy, bias=-1.0)
+            return c
 
-        def gather_c(t):
-            c_rows = load_plane(cT, "c", t)
-            nc.vector.tensor_copy(c[:, t, :], c_rows[:].indirect(offsets[:]))
-            c_sq = sb.tile([P, SLOTS], F32, name="c_sq%d" % t)
-            nc.scalar.activation(c_sq[:], c[:, t, :], ACT.Square)
-            nc.scalar.activation(one_less_csq[:, t, :], c_sq[:], ACT.Copy, bias=1.0, scale=-1.0)
+        x_low = rows_tile("x_rows_low", 2)
+        load_plane(x_low[:, TOKENS:], xT, 0)
+        minus_x = sb.tile([P, SLOTS], F32, name="minus_x")
+        nc.scalar.activation(minus_x[:], gather("x_picked0", x_low[:, TOKENS:])[:], ACT.Copy, scale=-1.0)
+        e_bank = turned(minus_x, "e_bank0", "bank_e", stop=False)
+        c_rows = rows_tile("c_rows0", 1)
+        load_plane(c_rows[:], cT, 0)
+        turn(e_bank, bring_c(0, c_rows[:], gather), False, True)
+        nc.scalar.activation(right[:, 0, 1, :], e_bank[:], ACT.Copy, scale=-1.0)
+        bring_g(0)
+        zeroed_window("g_rows0")
+        nc.gpsimd.tensor_tensor(made[:, 0, 1, :], left[:, 0, 1, :], right[:, 0, 1, :], ALU.mult)
 
-        def gather_g(t):
-            g_rows = load_plane(gT, "g", t)
-            nc.vector.tensor_copy(g[:, t, :], g_rows[:].indirect(offsets[:]))
-            nc.scalar.copy(out=dr[:, t, :], in_=dr_acc[t][:])
-            nc.gpsimd.tensor_tensor(u[:, t, :], dr[:, t, :], g[:, t, :], ALU.mult)
-            nc.scalar.activation(one_less_g[:, t, :], g[:, t, :], ACT.Copy, bias=1.0, scale=-1.0)
+        wo_raw = load_matrix(wo, "wo", "raw_a")
+        wo_grouped = sb.tile([P, K, PACK], BF16, name="wo_grouped", tag="grouped_a", align_bytes=64)
+        wo_codes = sb.tile([P, K], U32, name="wo_codes", align_bytes=64)
+        wo_scales = sb.tile([P, K], U8, name="wo_scales", align_bytes=64)
+        group(nc.vector.tensor_copy, wo_grouped[:], wo_raw[:])
+        quantize(wo_grouped[:], wo_codes[:], wo_scales[:], E4M3)
 
-        def gather_x(t):
-            x_rows = load_plane(xT, "x", t, "held" if t == last else None)
-            nc.vector.tensor_copy(x[:, t, :], x_rows[:].indirect(offsets[:]))
-            if t == 0:
-                nc.gpsimd.tensor_tensor(c_less_x[:, t, :], c[:, t, :], x[:, t, :], ALU.subtract)
-                return
-            minus_x = sb.tile([P, SLOTS], F32, name="minus_x%d" % t)
-            nc.scalar.activation(minus_x[:], x[:, t, :], ACT.Copy, scale=-1.0)
-            there = psum.tile([P, SLOTS], F32, name="there%d" % t, tag="spare%d" % (2 * (t % 2)))
-            back = psum.tile([P, SLOTS], F32, name="back%d" % t, tag="spare%d" % (2 * (t % 2) + 1))
-            turned = sb.tile([P, SLOTS], F32, name="turned%d" % t)
-            blocks = [slice(j * P, (j + 1) * P) for j in range(SLOTS // P)]
-            for block in blocks:
-                nc.tensor.matmul(there[:, block], c[:, t, block], identity[:], start=True, stop=False, is_transpose=True)
-                nc.tensor.matmul(there[:, block], minus_x[:, block], identity[:], start=False, stop=True, is_transpose=True)
-            nc.scalar.copy(out=turned[:], in_=there[:])
-            for block in blocks:
-                nc.tensor.transpose(back[:, block], turned[:, block], identity[:])
-            nc.scalar.copy(out=c_less_x[:, t, :], in_=back[:])
+        dy_raw = load_matrix(dy, "dy", "raw_b")
+        dy_grouped, dy_blocks = [], []
 
-        for t in range(PACK):
-            for gather in (gather_g, gather_c, gather_x) if t == 0 else (gather_c, gather_x, gather_g):
-                gather(t)
-            nc.gpsimd.tensor_tensor(zc_planes[:, t, :], u[:, t, :], one_less_csq[:, t, :], ALU.mult)
-            nc.gpsimd.tensor_tensor(h[:, t, :], one_less_g[:, t, :], c_less_x[:, t, :], ALU.mult)
-            if t < last:
-                nc.gpsimd.tensor_tensor(
-                    zg_planes[:, :, t, :],
-                    u[:, t, :].rearrange("p (a n) -> p a n", a=2),
-                    h[:, t, :].rearrange("p (a n) -> p a n", a=2),
-                    ALU.mult,
-                )
+        def group_dy(copy, j):
+            grouped = sb.tile([P, P, PACK], BF16, name="dy_grouped%d" % j, tag=("dy_grouped0", "dy_grouped1", "g_picked0", "c_picked0")[j], align_bytes=64)
+            group(copy, grouped[:], dy_raw[:, :, blocks[j]])
+            return grouped
+
+        def quantize_dy(grouped, j):
+            codes = sb.tile([P, P], U32, name="dy_codes%d" % j, align_bytes=64)
+            scales = sb.tile([P, P], U8, name="dy_scales%d" % j, align_bytes=64)
+            quantize(grouped[:], codes[:], scales[:], E5M2)
+            dy_blocks.append((codes[:], scales[:]))
+
+        for j in range(BLOCKS):
+            dy_grouped.append(group_dy(nc.vector.tensor_copy if j < BLOCKS // 2 else nc.scalar.copy, j))
+        for j in range(BLOCKS):
+            quantize_dy(dy_grouped[j], j)
+        for j, (codes, scales) in enumerate(dy_blocks):
+            bank = psum.tile([P, K], F32, name="dr_bank%d" % j, tag="bank_wide%d" % j)
+            nc.tensor.matmul_mx(
+                out=bank[:], lhsT=codes.bitcast(E5M2), lhsT_scale=scales,
+                rhs=wo_codes[:].bitcast(E4M3), rhs_scale=wo_scales[:], start=True, stop=True,
+            )
+            nc.scalar.copy(out=left[:, :, 0, blocks[j]], in_=bank[:].rearrange("p (a d) -> p a d", d=P))
+        for cols in (slice(0, 2 * P), slice(2 * P, SLOTS)):
+            nc.gpsimd.tensor_tensor(made[:, 0, 0, cols], left[:, 0, 0, cols], right[:, 0, 0, cols], ALU.mult)
+        form_z(0, made[:, 0, 1:3, :])
+
+        def turn_dd(a, tag):
+            bank = turned(left[:, a, 0, :], "dd_bank%d" % a, tag, stop=False)
+            turn(bank, made[:, a, 0, :], False, True)
+            return bank
+
+        bring_g(1)
+        c_rows = rows_tile("c_rows1", 1)
+        load_plane(c_rows[:], cT, 1)
+        e_bank = turned(bring_c(1, c_rows[:], gather), "e_bank1", "bank_e", stop=False)
+        load_plane(x_low[:, 0:TOKENS], xT, 1)
+        turn(e_bank, gather_negated("x_picked1", x_low[:]), False, True)
+        nc.scalar.activation(right[:, 1, 1, :], e_bank[:], ACT.Copy, scale=-1.0)
+        nc.gpsimd.tensor_tensor(made[:, 1, 0:2, :], left[:, 1, :, :], right[:, 1, :, :], ALU.mult)
+        form_z(1, made[:, 1, 1:3, :])
+
+        high = slice(2, PLANES)
+        c_high = rows_tile("c_rows_high", 2)
+        bring_g(2)
+        load_plane(c_high[:, TOKENS:], cT, 2)
+        e_bank2 = turned(bring_c(2, c_high[:, TOKENS:], gather), "e_bank2", "bank_e", stop=False)
+        bring_g(3)
+        load_plane(c_high[:, 0:TOKENS], cT, 3)
+        e_bank3 = turned(bring_c(3, c_high[:], gather_negated), "e_bank3", "bank_g", stop=False)
+        nc.gpsimd.tensor_tensor(made[:, high, 0, :], left[:, high, 0, :], right[:, high, 0, :], ALU.mult)
+        dd_bank0 = turn_dd(0, "bank_dd")
+        x_high = rows_tile("x_rows_high", 2)
+        nc.sync.dma_start(x_high[:].rearrange("p (a n) -> p a n", a=2), xT[2 * P :, :].rearrange("(a p) n -> p a n", p=P))
+        turn(e_bank2, gather_negated("x_picked2", x_high[:]), False, True)
+        turn(e_bank3, gather("x_picked3", x_high[:, TOKENS:]), False, True)
+        behind_x2 = sb.tile([P, 5, SLOTS], F32, name="behind_x2", tag="x_picked2", align_bytes=64)
+        dd0 = behind_x2[:, 0, :]
+        one_less_g_high = behind_x2[:, 1:3, :]
+        csq_less_one_high = behind_x2[:, 3:5, :]
+        dd0_parts = (slice(0, FIRST_SLOTS), slice(FIRST_SLOTS, SLOTS))
+        for part in dd0_parts:
+            nc.scalar.copy(out=dd0[:, part], in_=dd_bank0[:, part])
+        nc.scalar.activation(csq_less_one_high, c_sq[:, high, :], ACT.Copy, bias=-1.0)
+        wc_raw = load_matrix(wc, "wc", "raw_a")
+        wg_raw = late.tile([P, PACK, K], F32, name="wg_raw", align_bytes=64, offset=0)
+        nc.sync.dma_start(wg_raw[:], wg.rearrange("(p j) n -> p j n", j=PACK))
+        for part in dd0_parts:
+            nc.vector.tensor_copy(windows[0][:].indirect(offsets[:, part.start // 16 : part.stop // 16]), dd0[:, part])
+        nc.sync.dma_start(out_1[blocks[0], :], windows[0][:])
+
+        def scatter_dd(a, bank):
+            dd = sb.tile([P, SLOTS], F32, name="dd%d" % a)
+            nc.scalar.copy(out=dd[:], in_=bank[:])
+            nc.vector.tensor_copy(windows[a][:].indirect(offsets[:]), dd[:])
+            nc.sync.dma_start(out_1[blocks[a], :], windows[a][:])
+
+        def form_z_high(kind, factor):
+            nc.gpsimd.tensor_tensor(
+                z_turned[:, kind, :, 2 * P :].rearrange("p j (a d) -> p a j d", d=P),
+                by_block(made[:, high, 0, :]), by_block(factor), ALU.mult,
+            )
+
+        scatter_dd(1, turn_dd(1, "bank_dd"))
+        nc.scalar.activation(right[:, 2, 1, :], e_bank2[:], ACT.Copy, scale=-1.0)
+        nc.scalar.copy(out=right[:, 3, 1, :], in_=e_bank3[:])
+        nc.scalar.activation(one_less_g_high, right[:, high, 0, :], ACT.Copy, bias=1.0)
+        form_z_high(1, csq_less_one_high)
+        nc.gpsimd.tensor_tensor(made[:, high, 1, :], one_less_g_high, right[:, high, 1, :], ALU.mult)
+        form_z_high(0, made[:, high, 1, :])
+        scatter_dd(2, turn_dd(2, "bank_g"))
+        last_bank = turn_dd(last, "bank_e")
+        early = SLOTS - LATE_SLOTS
+        dd_early = late.tile([P, early], F32, name="dd_early", align_bytes=64, offset=4 * PACK * K)[:]
+        nc.scalar.copy(out=dd_early, in_=last_bank[:, 0:early])
+        nc.vector.tensor_copy(windows[last][:].indirect(offsets[:, 0 : early // 16]), dd_early)
+
+        w_grouped = sb.tile([P, 2 * K, PACK], BF16, name="w_grouped", tag="x_picked3", align_bytes=64)
+        for number, raw in enumerate((wc_raw, wg_raw)):
+            for start in (0, K // 2):
+                group(nc.scalar.copy, w_grouped[:, number * K + start : number * K + start + K // 2, :], raw[:, :, start : start + K // 2])
+        late_codes = sb.tile([P, 4 * K], U32, name="late_codes", tag="made_then_codes", align_bytes=64)
+        w_codes = late_codes[:, 0 : 2 * K]
+        w_scales = late.tile([P, 2 * K], U8, name="w_scales", align_bytes=64, offset=4 * PACK * K)[:]
+        quantize(w_grouped[:], w_codes, w_scales, E4M3)
+
+        words = z_turned[:].rearrange("p z j d -> p (z j d)").bitcast(F32)
+        z_packed = {}
+        for kind in (1, 0):
+            if kind == 1:
+                flat_words = late.tile([P, 2 * SLOTS], F32, name="zc_grouped", align_bytes=64, offset=4 * SLOTS)[:]
             else:
-                for number, cols in enumerate(halves):
-                    nc.gpsimd.tensor_tensor(zg_planes[:, number, t, :], u[:, t, cols], h[:, t, cols], ALU.mult)
-        wc_raw = load_matrix(wc, "wc")
-        wg_raw = load_matrix(wg, "wg")
+                flat_words = sb.tile([P, 2 * SLOTS], F32, name="zg_grouped", align_bytes=64)[:]
+            grouped_words = flat_words.rearrange("p (n u) -> p n u", u=2)
+            for half in range(2):
+                bank = psum.tile([P, 2, 2 * P], F32, name="z_bank%d%d" % (kind, half), tag=("bank_g", "bank_dd")[half])
+                for inner in range(2):
+                    base = (kind * BLOCKS + 2 * half + inner) * (K // 2)
+                    for u in range(2):
+                        nc.tensor.transpose(bank[:, u, blocks[inner]], words[:, base + u : base + K // 2 : 2], identity[:])
+                nc.scalar.copy(out=grouped_words[:, 2 * P * half : 2 * P * (half + 1), :], in_=bank[:].rearrange("p u n -> p n u"))
+            codes = late_codes[:, (2 + kind) * K : (3 + kind) * K]
+            if kind == 1:
+                scales = sb.tile([P, SLOTS], U8, name="zc_scales", tag="x_picked3", align_bytes=64)
+            else:
+                scales = late.tile([P, SLOTS], U8, name="zg_scales", align_bytes=64, offset=4 * SLOTS)
+            quantize(flat_words.bitcast(BF16).rearrange("p (n j) -> p n j", j=PACK), codes, scales[:], E5M2)
+            z_packed[kind] = (codes, scales[:])
 
-        dd = sb.tile([P, last, SLOTS], F32, name="dd", tag="held", align_bytes=64)
-        for t in range(last):
-            nc.vector.tensor_tensor(dd[:, t, :], one_less_g[:, t, :], dr_acc[t][:], ALU.mult)
-        out_1_planes = out_1.rearrange("(p t) n -> p t n", t=PACK)
-        for t in range(last):
-            nc.vector.tensor_copy(windows[t][:].indirect(offsets[:]), dd[:, t, :])
-            nc.sync.dma_start(out_1_planes[:, t, :], windows[t][:])
+        s_banks = []
+        for r in range(PLANES):
+            bank = psum.tile([P, SLOTS], F32, name="s_bank%d" % r, tag="bank_wide%d" % r)
+            for number, kind in enumerate((1, 0) if r == 0 else (0, 1)):
+                cols = slice((1 - kind) * K + r * P, (1 - kind) * K + (r + 1) * P)
+                nc.tensor.matmul_mx(
+                    out=bank[:], lhsT=w_codes[:, cols].bitcast(E4M3), lhsT_scale=w_scales[:, cols],
+                    rhs=z_packed[kind][0].bitcast(E5M2), rhs_scale=z_packed[kind][1],
+                    start=number == 0, stop=number == 1,
+                )
+            s_banks.append(bank)
 
-        late_codes = sb.tile([P, 3 * K], U32, name="late_codes", tag="h_then_codes", align_bytes=64)
-        w_grouped = sb.tile([P, 2 * K, PACK], BF16, name="w_grouped", align_bytes=64)
-        w_scales = sb.tile([P, 2 * K], U8, name="w_scales", align_bytes=64)
-        w_p = (w_grouped[:], late_codes[:, 0 : 2 * K], w_scales[:])
-        z_grouped = sb.tile([P, 2 * SLOTS, PACK], BF16, name="z_grouped", tag="wg_raw", align_bytes=64)
-        zc_scales = sb.tile([P, K], U8, name="zc_scales", align_bytes=64)
-        zc_p = (z_grouped[:, 0:SLOTS, :], late_codes[:, 2 * K : 3 * K], zc_scales[:])
-        group(nc.scalar.copy, w_grouped[:, 0:K, :], wc_raw[:])
-        group(nc.scalar.copy, w_grouped[:, K : 2 * K, :], wg_raw[:])
-        quantize(w_p, E4M3)
-        group(nc.scalar.copy, zc_p[0], zc_planes[:])
-        quantize(zc_p, E5M2)
-        zg_codes = sb.tile([P, SLOTS], U32, name="zg_codes", align_bytes=64)
-        zg_scales = sb.tile([P, SLOTS], U8, name="zg_scales", align_bytes=64)
-        zg_p = (z_grouped[:, SLOTS : 2 * SLOTS, :], zg_codes[:], zg_scales[:])
-        for number, cols in enumerate(halves):
-            group(nc.scalar.copy, zg_p[0][:, cols, :], zg_planes[:, number, :, :])
-        quantize(zg_p, E5M2)
-
-        s_acc = []
-        for r in range(PACK):
-            acc = psum.tile([P, SLOTS], F32, name="s_acc%d" % r, tag="spare%d" % r)
-            mx_pass(acc, w_p, r, zc_p, True, False)
-            mx_pass(acc, w_p, PACK + r, zg_p, False, True)
-            s_acc.append(acc)
-
-        dr_last = sb.tile([P, SLOTS], F32, name="dr_last", tag="zg_then_dr")
-        nc.scalar.copy(out=dr_last[:], in_=dr_acc[last][:])
-        nc.vector.tensor_tensor(windows[0][:].indirect(offsets[:]), dr_last[:], one_less_g[:, last, :], ALU.mult)
-        nc.sync.dma_start(out_1_planes[:, last, :], windows[0][:])
-        for r in range(PACK):
-            nc.scalar.copy(out=s[:, r, :], in_=s_acc[r][:])
-            nc.vector.tensor_copy(windows[(PACK + r) % WINDOWS][:].indirect(offsets[:]), s[:, r, :])
-            nc.sync.dma_start(out_0[r * P : (r + 1) * P, :], windows[(PACK + r) % WINDOWS][:])
+        dd_late = sb.tile([P, LATE_SLOTS], F32, name="dd_late", tag="z_then_dd", align_bytes=64)
+        nc.scalar.copy(out=dd_late[:], in_=last_bank[:, early:])
+        nc.vector.tensor_copy(windows[last][:].indirect(offsets[:, early // 16 :]), dd_late[:])
+        nc.sync.dma_start(out_1[blocks[last], :], windows[last][:])
+        for r in range(PLANES):
+            s = sb.tile([P, SLOTS], F32, name="s%d" % r)
+            nc.scalar.copy(out=s[:], in_=s_banks[r][:])
+            window = windows[(PLANES + r) % WINDOWS]
+            nc.vector.tensor_copy(window[:].indirect(offsets[:]), s[:])
+            nc.sync.dma_start(out_0[blocks[r], :], window[:])

@@ -72,7 +72,7 @@ def tile_attend_ghighw_kernel(tc, dy, wo, gT, cT, xT, wg, wc, offs, out_0, out_1
         left = sb.tile([P, PLANES, 2, SLOTS], F32, name="left")
         right = sb.tile([P, PLANES, 2, SLOTS], F32, name="right")
         made = sb.tile([P, PLANES, 3, SLOTS], F32, name="made", tag="made_then_codes", align_bytes=64)
-        c_sq = sb.tile([P, PLANES, SLOTS], F32, name="c_sq")
+        c_sq = sb.tile([P, PLANES, SLOTS], F32, name="c_sq", tag="c_sq", align_bytes=64)
         z_turned = sb.tile([P, 2, BLOCKS, K], BF16, name="z_turned", tag="z_then_dd", align_bytes=64)
 
         def rows_tile(label, planes):
@@ -116,21 +116,21 @@ def tile_attend_ghighw_kernel(tc, dy, wo, gT, cT, xT, wg, wc, offs, out_0, out_1
                 z_turned[:, :, :, blocks[a]], by_block(made[:, a, 0:1, :].to_broadcast([P, 2, SLOTS])), by_block(factors), ALU.mult
             )
 
-        def bring_c(a, rows, pick):
+        def bring_c(a, rows, pick, tag):
             c = pick("c_picked%d" % a, rows)
             nc.scalar.activation(c_sq[:, a, :], turned(c, "c_bank%d" % a, "bank_c")[:], ACT.Square)
-            if a < 2:
+            if a < last:
                 nc.scalar.activation(made[:, a, 2, :], c_sq[:, a, :], ACT.Copy, bias=-1.0)
-            return c
+            return turned(c, "e_bank%d" % a, tag, stop=False)
 
+        c_rows = rows_tile("c_rows0", 1)
+        load_plane(c_rows[:], cT, 0)
+        e_bank = bring_c(0, c_rows[:], gather, "bank_e")
         x_low = rows_tile("x_rows_low", 2)
         load_plane(x_low[:, TOKENS:], xT, 0)
         minus_x = sb.tile([P, SLOTS], F32, name="minus_x")
         nc.scalar.activation(minus_x[:], gather("x_picked0", x_low[:, TOKENS:])[:], ACT.Copy, scale=-1.0)
-        e_bank = turned(minus_x, "e_bank0", "bank_e", stop=False)
-        c_rows = rows_tile("c_rows0", 1)
-        load_plane(c_rows[:], cT, 0)
-        turn(e_bank, bring_c(0, c_rows[:], gather), False, True)
+        turn(e_bank, minus_x, False, True)
         nc.scalar.activation(right[:, 0, 1, :], e_bank[:], ACT.Copy, scale=-1.0)
         bring_g(0)
         zeroed_window("g_rows0")
@@ -147,7 +147,7 @@ def tile_attend_ghighw_kernel(tc, dy, wo, gT, cT, xT, wg, wc, offs, out_0, out_1
         dy_grouped, dy_blocks = [], []
 
         def group_dy(copy, j):
-            grouped = sb.tile([P, P, PACK], BF16, name="dy_grouped%d" % j, tag=("dy_grouped0", "dy_grouped1", "g_picked0", "c_picked0")[j], align_bytes=64)
+            grouped = sb.tile([P, P, PACK], BF16, name="dy_grouped%d" % j, tag=("dy_grouped0", "dy_grouped1", "g_picked0", "x_picked0")[j], align_bytes=64)
             group(copy, grouped[:], dy_raw[:, :, blocks[j]])
             return grouped
 
@@ -180,7 +180,7 @@ def tile_attend_ghighw_kernel(tc, dy, wo, gT, cT, xT, wg, wc, offs, out_0, out_1
         bring_g(1)
         c_rows = rows_tile("c_rows1", 1)
         load_plane(c_rows[:], cT, 1)
-        e_bank = turned(bring_c(1, c_rows[:], gather), "e_bank1", "bank_e", stop=False)
+        e_bank = bring_c(1, c_rows[:], gather, "bank_dd")
         load_plane(x_low[:, 0:TOKENS], xT, 1)
         turn(e_bank, gather_negated("x_picked1", x_low[:]), False, True)
         nc.scalar.activation(right[:, 1, 1, :], e_bank[:], ACT.Copy, scale=-1.0)
@@ -191,24 +191,23 @@ def tile_attend_ghighw_kernel(tc, dy, wo, gT, cT, xT, wg, wc, offs, out_0, out_1
         c_high = rows_tile("c_rows_high", 2)
         bring_g(2)
         load_plane(c_high[:, TOKENS:], cT, 2)
-        e_bank2 = turned(bring_c(2, c_high[:, TOKENS:], gather), "e_bank2", "bank_e", stop=False)
+        e_bank2 = bring_c(2, c_high[:, TOKENS:], gather, "bank_e")
         bring_g(3)
         load_plane(c_high[:, 0:TOKENS], cT, 3)
-        e_bank3 = turned(bring_c(3, c_high[:], gather_negated), "e_bank3", "bank_g", stop=False)
+        e_bank3 = bring_c(3, c_high[:], gather_negated, "bank_wide0")
         nc.gpsimd.tensor_tensor(made[:, high, 0, :], left[:, high, 0, :], right[:, high, 0, :], ALU.mult)
         dd_bank0 = turn_dd(0, "bank_dd")
         x_high = rows_tile("x_rows_high", 2)
         nc.sync.dma_start(x_high[:].rearrange("p (a n) -> p a n", a=2), xT[2 * P :, :].rearrange("(a p) n -> p a n", p=P))
         turn(e_bank2, gather_negated("x_picked2", x_high[:]), False, True)
-        turn(e_bank3, gather("x_picked3", x_high[:, TOKENS:]), False, True)
-        behind_x2 = sb.tile([P, 5, SLOTS], F32, name="behind_x2", tag="x_picked2", align_bytes=64)
+        nc.vector.tensor_copy(made[:, last, 2, :], x_high[:, TOKENS:].indirect(offsets[:]))
+        turn(e_bank3, made[:, last, 2, :], False, True)
+        behind_x2 = sb.tile([P, 3, SLOTS], F32, name="behind_x2", tag="x_picked2", align_bytes=64)
         dd0 = behind_x2[:, 0, :]
         one_less_g_high = behind_x2[:, 1:3, :]
-        csq_less_one_high = behind_x2[:, 3:5, :]
         dd0_parts = (slice(0, FIRST_SLOTS), slice(FIRST_SLOTS, SLOTS))
         for part in dd0_parts:
             nc.scalar.copy(out=dd0[:, part], in_=dd_bank0[:, part])
-        nc.scalar.activation(csq_less_one_high, c_sq[:, high, :], ACT.Copy, bias=-1.0)
         wc_raw = load_matrix(wc, "wc", "raw_a")
         wg_raw = late.tile([P, PACK, K], F32, name="wg_raw", align_bytes=64, offset=0)
         nc.sync.dma_start(wg_raw[:], wg.rearrange("(p j) n -> p j n", j=PACK))
@@ -222,62 +221,61 @@ def tile_attend_ghighw_kernel(tc, dy, wo, gT, cT, xT, wg, wc, offs, out_0, out_1
             nc.vector.tensor_copy(windows[a][:].indirect(offsets[:]), dd[:])
             nc.sync.dma_start(out_1[blocks[a], :], windows[a][:])
 
-        def form_z_high(kind, factor):
+        def form_z_high(kind, within):
             nc.gpsimd.tensor_tensor(
-                z_turned[:, kind, :, 2 * P :].rearrange("p j (a d) -> p a j d", d=P),
-                by_block(made[:, high, 0, :]), by_block(factor), ALU.mult,
+                z_turned[:, kind, within, 2 * P :].rearrange("p j (a d) -> p a j d", d=P),
+                by_block(made[:, high, 0, :])[:, :, within, :], by_block(made[:, high, 1 + kind, :])[:, :, within, :], ALU.mult,
             )
 
-        scatter_dd(1, turn_dd(1, "bank_dd"))
         nc.scalar.activation(right[:, 2, 1, :], e_bank2[:], ACT.Copy, scale=-1.0)
         nc.scalar.copy(out=right[:, 3, 1, :], in_=e_bank3[:])
         nc.scalar.activation(one_less_g_high, right[:, high, 0, :], ACT.Copy, bias=1.0)
-        form_z_high(1, csq_less_one_high)
+        scatter_dd(1, turn_dd(1, "bank_dd"))
+        nc.scalar.activation(made[:, last, 2, :], c_sq[:, last, :], ACT.Copy, bias=-1.0)
         nc.gpsimd.tensor_tensor(made[:, high, 1, :], one_less_g_high, right[:, high, 1, :], ALU.mult)
-        form_z_high(0, made[:, high, 1, :])
-        scatter_dd(2, turn_dd(2, "bank_g"))
+        form_z_high(0, slice(0, BLOCKS))
+        for half in range(2):
+            form_z_high(1, slice(2 * half, 2 * half + 2))
+        scatter_dd(2, turn_dd(2, "bank_wide0"))
         last_bank = turn_dd(last, "bank_e")
         early = SLOTS - LATE_SLOTS
-        dd_early = late.tile([P, early], F32, name="dd_early", align_bytes=64, offset=4 * PACK * K)[:]
+        dd_early = late.tile([P, early], F32, name="dd_early", align_bytes=64, offset=18 * SLOTS)[:]
         nc.scalar.copy(out=dd_early, in_=last_bank[:, 0:early])
         nc.vector.tensor_copy(windows[last][:].indirect(offsets[:, 0 : early // 16]), dd_early)
 
-        w_grouped = sb.tile([P, 2 * K, PACK], BF16, name="w_grouped", tag="x_picked3", align_bytes=64)
+        w_grouped = sb.tile([P, 2 * K, PACK], BF16, name="w_grouped", tag="c_sq", align_bytes=64)
         for number, raw in enumerate((wc_raw, wg_raw)):
             for start in (0, K // 2):
                 group(nc.scalar.copy, w_grouped[:, number * K + start : number * K + start + K // 2, :], raw[:, :, start : start + K // 2])
         late_codes = sb.tile([P, 4 * K], U32, name="late_codes", tag="made_then_codes", align_bytes=64)
         w_codes = late_codes[:, 0 : 2 * K]
-        w_scales = late.tile([P, 2 * K], U8, name="w_scales", align_bytes=64, offset=4 * PACK * K)[:]
+        w_scales = late.tile([P, 2 * K], U8, name="w_scales", align_bytes=64, offset=18 * SLOTS)[:]
         quantize(w_grouped[:], w_codes, w_scales, E4M3)
 
         words = z_turned[:].rearrange("p z j d -> p (z j d)").bitcast(F32)
         z_packed = {}
-        for kind in (1, 0):
-            if kind == 1:
-                flat_words = late.tile([P, 2 * SLOTS], F32, name="zc_grouped", align_bytes=64, offset=4 * SLOTS)[:]
-            else:
-                flat_words = sb.tile([P, 2 * SLOTS], F32, name="zg_grouped", align_bytes=64)[:]
+        for kind in range(2):
+            flat_words = late.tile([P, 2 * SLOTS], F32, name="z_grouped%d" % kind, align_bytes=64, offset=10 * SLOTS * kind)[:]
             grouped_words = flat_words.rearrange("p (n u) -> p n u", u=2)
             for half in range(2):
-                bank = psum.tile([P, 2, 2 * P], F32, name="z_bank%d%d" % (kind, half), tag=("bank_g", "bank_dd")[half])
+                bank = psum.tile([P, 2, 2 * P], F32, name="z_bank%d%d" % (kind, half), tag=("bank_wide1", "bank_wide2", "bank_wide3", "bank_c")[2 * kind + half])
                 for inner in range(2):
                     base = (kind * BLOCKS + 2 * half + inner) * (K // 2)
                     for u in range(2):
                         nc.tensor.transpose(bank[:, u, blocks[inner]], words[:, base + u : base + K // 2 : 2], identity[:])
                 nc.scalar.copy(out=grouped_words[:, 2 * P * half : 2 * P * (half + 1), :], in_=bank[:].rearrange("p u n -> p n u"))
             codes = late_codes[:, (2 + kind) * K : (3 + kind) * K]
-            if kind == 1:
-                scales = sb.tile([P, SLOTS], U8, name="zc_scales", tag="x_picked3", align_bytes=64)
+            if kind == 0:
+                scales = sb.tile([P, SLOTS], U8, name="zg_scales", tag="c_sq", align_bytes=64)
             else:
-                scales = late.tile([P, SLOTS], U8, name="zg_scales", align_bytes=64, offset=4 * SLOTS)
+                scales = late.tile([P, SLOTS], U8, name="zc_scales", align_bytes=64, offset=0)
             quantize(flat_words.bitcast(BF16).rearrange("p (n j) -> p n j", j=PACK), codes, scales[:], E5M2)
             z_packed[kind] = (codes, scales[:])
 
         s_banks = []
-        for r in range(PLANES):
-            bank = psum.tile([P, SLOTS], F32, name="s_bank%d" % r, tag="bank_wide%d" % r)
-            for number, kind in enumerate((1, 0) if r == 0 else (0, 1)):
+        for r, tag in enumerate(("bank_g", "bank_dd", "bank_wide0", "bank_wide1")):
+            bank = psum.tile([P, SLOTS], F32, name="s_bank%d" % r, tag=tag)
+            for number, kind in enumerate((0, 1) if r == 0 else (1, 0)):
                 cols = slice((1 - kind) * K + r * P, (1 - kind) * K + (r + 1) * P)
                 nc.tensor.matmul_mx(
                     out=bank[:], lhsT=w_codes[:, cols].bitcast(E4M3), lhsT_scale=w_scales[:, cols],
@@ -286,7 +284,7 @@ def tile_attend_ghighw_kernel(tc, dy, wo, gT, cT, xT, wg, wc, offs, out_0, out_1
                 )
             s_banks.append(bank)
 
-        dd_late = sb.tile([P, LATE_SLOTS], F32, name="dd_late", tag="z_then_dd", align_bytes=64)
+        dd_late = late.tile([P, LATE_SLOTS], F32, name="dd_late", align_bytes=64, offset=8 * SLOTS)
         nc.scalar.copy(out=dd_late[:], in_=last_bank[:, early:])
         nc.vector.tensor_copy(windows[last][:].indirect(offsets[:, early // 16 :]), dd_late[:])
         nc.sync.dma_start(out_1[blocks[last], :], windows[last][:])

@@ -134,7 +134,6 @@ def tile_attend_ghighw_kernel(tc, dy, wo, gT, cT, xT, wg, wc, offs, out_0, out_1
         nc.scalar.activation(right[:, 0, 1, :], e_bank[:], ACT.Copy, scale=-1.0)
         bring_g(0)
         zeroed_window("g_rows0")
-        nc.gpsimd.tensor_tensor(made[:, 0, 1, :], left[:, 0, 1, :], right[:, 0, 1, :], ALU.mult)
 
         wo_raw = load_matrix(wo, "wo", "raw_a")
         wo_grouped = sb.tile([P, K, PACK], BF16, name="wo_grouped", tag="grouped_a", align_bytes=64)
@@ -147,20 +146,24 @@ def tile_attend_ghighw_kernel(tc, dy, wo, gT, cT, xT, wg, wc, offs, out_0, out_1
         dy_grouped, dy_blocks = [], []
 
         def group_dy(copy, j):
-            grouped = sb.tile([P, P, PACK], BF16, name="dy_grouped%d" % j, tag=("dy_grouped0", "dy_grouped1", "g_picked0", "x_picked0")[j], align_bytes=64)
-            group(copy, grouped[:], dy_raw[:, :, blocks[j]])
+            if j < BLOCKS - 1:
+                grouped = sb.tile([P, P, PACK], BF16, name="dy_grouped%d" % j, tag=("dy_grouped0", "dy_grouped1", "g_picked0")[j], align_bytes=64)[:]
+            else:
+                grouped = made[:, 0, 1, 0 : P * PACK // 2].bitcast(BF16).rearrange("p (n j) -> p n j", j=PACK)
+            group(copy, grouped, dy_raw[:, :, blocks[j]])
             return grouped
 
         def quantize_dy(grouped, j):
             codes = sb.tile([P, P], U32, name="dy_codes%d" % j, align_bytes=64)
             scales = sb.tile([P, P], U8, name="dy_scales%d" % j, align_bytes=64)
-            quantize(grouped[:], codes[:], scales[:], E5M2)
+            quantize(grouped, codes[:], scales[:], E5M2)
             dy_blocks.append((codes[:], scales[:]))
 
         for j in range(BLOCKS):
             dy_grouped.append(group_dy(nc.vector.tensor_copy if j < BLOCKS // 2 else nc.scalar.copy, j))
         for j in range(BLOCKS):
             quantize_dy(dy_grouped[j], j)
+        nc.gpsimd.tensor_tensor(made[:, 0, 1, :], left[:, 0, 1, :], right[:, 0, 1, :], ALU.mult)
         for j, (codes, scales) in enumerate(dy_blocks):
             bank = psum.tile([P, K], F32, name="dr_bank%d" % j, tag="bank_wide%d" % j)
             nc.tensor.matmul_mx(

@@ -22,8 +22,8 @@ TOKENS = 1024
 PLANES = K // P
 BLOCKS = SLOTS // P
 WINDOWS = 4
+VECTOR_SHARE = 320
 LATE_SLOTS = 256
-FIRST_SLOTS = 128
 FLOPS = 3 * 2 * K * K * SLOTS
 
 
@@ -69,10 +69,11 @@ def tile_attend_ghighw_kernel(tc, dy, wo, gT, cT, xT, wg, wc, offs, out_0, out_1
 
         offsets = lists.tile([P, SLOTS // 16], U16, name="offsets")
         nc.sync.dma_start(offsets[:], offs)
-        left = sb.tile([P, PLANES, 2, SLOTS], F32, name="left")
+        left = sb.tile([P, 2, 2, SLOTS], F32, name="left")
         right = sb.tile([P, PLANES, 2, SLOTS], F32, name="right")
         made = sb.tile([P, PLANES, 3, SLOTS], F32, name="made", tag="made_then_codes", align_bytes=64)
         c_sq = sb.tile([P, PLANES, SLOTS], F32, name="c_sq", tag="c_sq", align_bytes=64)
+        one_less_g_first = sb.tile([P, SLOTS], F32, name="one_less_g_first", tag="one_less_g_first", align_bytes=64)
         z_turned = sb.tile([P, 2, BLOCKS, K], BF16, name="z_turned", tag="z_then_dd", align_bytes=64)
 
         def rows_tile(label, planes):
@@ -82,25 +83,26 @@ def tile_attend_ghighw_kernel(tc, dy, wo, gT, cT, xT, wg, wc, offs, out_0, out_1
             nc.sync.dma_start(rows, table[blocks[a], :])
 
         def picked_tile(label):
-            return sb.tile([P, SLOTS], F32, name=label, tag=label, align_bytes=64)
+            return sb.tile([P, SLOTS], F32, name=label, tag=label, align_bytes=64)[:]
 
-        def gather(label, rows):
-            picked = picked_tile(label)
-            nc.vector.tensor_copy(picked[:], rows.indirect(offsets[:]))
+        def gather(picked, rows):
+            nc.vector.tensor_copy(picked, rows.indirect(offsets[:]))
             return picked
 
-        def gather_negated(label, rows):
-            picked = picked_tile(label)
-            nc.vector.tensor_scalar(picked[:], rows.indirect(offsets[:]), -1.0, 0.0, ALU.mult, ALU.add)
+        def gather_negated(picked, rows):
+            nc.vector.tensor_scalar(picked, rows.indirect(offsets[:]), -1.0, 0.0, ALU.mult, ALU.add)
             return picked
 
-        def bring_g(a):
+        def bring_g(a, picked):
             rows = rows_tile("g_rows%d" % a, 1)
             load_plane(rows[:], gT, a)
+            nc.vector.tensor_copy(picked, rows[:].indirect(offsets[:]))
             bank = psum.tile([P, SLOTS], F32, name="g_bank%d" % a, tag="bank_g")
-            turn(bank, gather("g_picked%d" % a, rows[:]))
+            turn(bank, picked)
+            if a == 0:
+                nc.scalar.activation(one_less_g_first[:], bank[:], ACT.Copy, bias=1.0, scale=-1.0)
             nc.scalar.activation(right[:, a, 0, :], bank[:], ACT.Copy, scale=-1.0)
-            if a < 2:
+            if a == 1:
                 nc.scalar.activation(left[:, a, 1, :], bank[:], ACT.Copy, bias=1.0, scale=-1.0)
 
         def turned(term, label, tag, stop=True):
@@ -116,40 +118,47 @@ def tile_attend_ghighw_kernel(tc, dy, wo, gT, cT, xT, wg, wc, offs, out_0, out_1
                 z_turned[:, :, :, blocks[a]], by_block(made[:, a, 0:1, :].to_broadcast([P, 2, SLOTS])), by_block(factors), ALU.mult
             )
 
-        def bring_c(a, rows, pick, tag):
-            c = pick("c_picked%d" % a, rows)
-            nc.scalar.activation(c_sq[:, a, :], turned(c, "c_bank%d" % a, "bank_c")[:], ACT.Square)
-            if a < last:
-                nc.scalar.activation(made[:, a, 2, :], c_sq[:, a, :], ACT.Copy, bias=-1.0)
+        def square_c(a, c, c_sq, out):
+            nc.scalar.activation(c_sq, turned(c, "c_bank%d" % a, "bank_c")[:], ACT.Square)
+            if out is not None:
+                nc.scalar.activation(out, c_sq, ACT.Copy, bias=-1.0)
+
+        def bring_c(a, c, tag):
+            square_c(a, c, c_sq[:, a - 1, :], made[:, a, 2, :] if a < last else None)
             return turned(c, "e_bank%d" % a, tag, stop=False)
 
-        c_rows = rows_tile("c_rows0", 1)
-        load_plane(c_rows[:], cT, 0)
-        e_bank = bring_c(0, c_rows[:], gather, "bank_e")
         x_low = rows_tile("x_rows_low", 2)
         load_plane(x_low[:, TOKENS:], xT, 0)
         minus_x = sb.tile([P, SLOTS], F32, name="minus_x")
-        nc.scalar.activation(minus_x[:], gather("x_picked0", x_low[:, TOKENS:])[:], ACT.Copy, scale=-1.0)
-        turn(e_bank, minus_x, False, True)
-        nc.scalar.activation(right[:, 0, 1, :], e_bank[:], ACT.Copy, scale=-1.0)
-        bring_g(0)
-        zeroed_window("g_rows0")
+        nc.scalar.activation(minus_x[:], gather(picked_tile("x_picked0"), x_low[:, TOKENS:]), ACT.Copy, scale=-1.0)
+        e_bank = turned(minus_x, "e_bank0", "bank_e", stop=False)
+        wo_grouped = sb.tile([P, K, PACK], BF16, name="wo_grouped", align_bytes=64)
+        bring_g(0, wo_grouped[:, K // 2 :, :].rearrange("p n j -> p (n j)").bitcast(F32))
+        c_rows = rows_tile("c_rows0", 1)
+        load_plane(c_rows[:], cT, 0)
+        c = gather(picked_tile("c_picked0"), c_rows[:])
+        turn(e_bank, c, False, True)
+        c_sq_first = sb.tile([P, SLOTS], F32, name="c_sq_first", tag="c_sq_first", align_bytes=64)
+        square_c(0, c, c_sq_first[:], made[:, 0, 2, :])
+        zeroed_window("c_rows0")
+        nc.vector.scalar_tensor_tensor(made[:, 0, 1, :], e_bank[:], -1.0, one_less_g_first[:], ALU.mult, ALU.mult)
 
         wo_raw = load_matrix(wo, "wo", "raw_a")
-        wo_grouped = sb.tile([P, K, PACK], BF16, name="wo_grouped", tag="grouped_a", align_bytes=64)
         wo_codes = sb.tile([P, K], U32, name="wo_codes", align_bytes=64)
-        wo_scales = sb.tile([P, K], U8, name="wo_scales", align_bytes=64)
-        group(nc.vector.tensor_copy, wo_grouped[:], wo_raw[:])
+        wo_scales = sb.tile([P, K], U8, name="wo_scales", tag="one_less_g_first", align_bytes=64)
+        for copy, cols in ((nc.vector.tensor_copy, slice(0, VECTOR_SHARE)), (nc.scalar.copy, slice(VECTOR_SHARE, K))):
+            group(copy, wo_grouped[:, cols, :], wo_raw[:, :, cols])
         quantize(wo_grouped[:], wo_codes[:], wo_scales[:], E4M3)
 
         dy_raw = load_matrix(dy, "dy", "raw_b")
         dy_grouped, dy_blocks = [], []
+        dy_halves = [
+            sb.tile([P, 2 * P, PACK], BF16, name="dy_grouped%d" % half, tag=tag, align_bytes=64)
+            for half, tag in enumerate(("raw_a", "c_sq_first"))
+        ]
 
         def group_dy(copy, j):
-            if j < BLOCKS - 1:
-                grouped = sb.tile([P, P, PACK], BF16, name="dy_grouped%d" % j, tag=("dy_grouped0", "dy_grouped1", "g_picked0")[j], align_bytes=64)[:]
-            else:
-                grouped = made[:, 0, 1, 0 : P * PACK // 2].bitcast(BF16).rearrange("p (n j) -> p n j", j=PACK)
+            grouped = dy_halves[j // 2][:, blocks[j % 2], :]
             group(copy, grouped, dy_raw[:, :, blocks[j]])
             return grouped
 
@@ -163,83 +172,95 @@ def tile_attend_ghighw_kernel(tc, dy, wo, gT, cT, xT, wg, wc, offs, out_0, out_1
             dy_grouped.append(group_dy(nc.vector.tensor_copy if j < BLOCKS // 2 else nc.scalar.copy, j))
         for j in range(BLOCKS):
             quantize_dy(dy_grouped[j], j)
-        nc.gpsimd.tensor_tensor(made[:, 0, 1, :], left[:, 0, 1, :], right[:, 0, 1, :], ALU.mult)
+        dr_banks = []
         for j, (codes, scales) in enumerate(dy_blocks):
             bank = psum.tile([P, K], F32, name="dr_bank%d" % j, tag="bank_wide%d" % j)
             nc.tensor.matmul_mx(
                 out=bank[:], lhsT=codes.bitcast(E5M2), lhsT_scale=scales,
                 rhs=wo_codes[:].bitcast(E4M3), rhs_scale=wo_scales[:], start=True, stop=True,
             )
-            nc.scalar.copy(out=left[:, :, 0, blocks[j]], in_=bank[:].rearrange("p (a d) -> p a d", d=P))
+            nc.scalar.copy(out=left[:, :, 0, blocks[j]], in_=bank[:, 0 : 2 * P].rearrange("p (a d) -> p a d", d=P))
+            dr_banks.append(bank)
         for cols in (slice(0, 2 * P), slice(2 * P, SLOTS)):
             nc.gpsimd.tensor_tensor(made[:, 0, 0, cols], left[:, 0, 0, cols], right[:, 0, 0, cols], ALU.mult)
         form_z(0, made[:, 0, 1:3, :])
 
         def turn_dd(a, tag):
-            bank = turned(left[:, a, 0, :], "dd_bank%d" % a, tag, stop=False)
+            bank = turned(left[:, a, 0, :] if a < 2 else dr_high[:, a - 2, :], "dd_bank%d" % a, tag, stop=False)
             turn(bank, made[:, a, 0, :], False, True)
             return bank
 
-        bring_g(1)
+        second = sb.tile([P, 3, SLOTS], F32, name="second_picked", tag="raw_b", align_bytes=64)
+        bring_g(1, second[:, 0, :])
         c_rows = rows_tile("c_rows1", 1)
         load_plane(c_rows[:], cT, 1)
-        e_bank = bring_c(1, c_rows[:], gather, "bank_dd")
+        e_bank = bring_c(1, gather(second[:, 1, :], c_rows[:]), "bank_dd")
         load_plane(x_low[:, 0:TOKENS], xT, 1)
-        turn(e_bank, gather_negated("x_picked1", x_low[:]), False, True)
+        turn(e_bank, gather_negated(second[:, 2, :], x_low[:]), False, True)
         nc.scalar.activation(right[:, 1, 1, :], e_bank[:], ACT.Copy, scale=-1.0)
+        dr_high = sb.tile([P, 2, SLOTS], F32, name="dr_high", tag="raw_b", align_bytes=64)
+        for j, bank in enumerate(dr_banks):
+            nc.scalar.copy(out=dr_high[:, :, blocks[j]], in_=bank[:, 2 * P :].rearrange("p (a d) -> p a d", d=P))
         nc.gpsimd.tensor_tensor(made[:, 1, 0:2, :], left[:, 1, :, :], right[:, 1, :, :], ALU.mult)
         form_z(1, made[:, 1, 1:3, :])
 
         high = slice(2, PLANES)
         c_high = rows_tile("c_rows_high", 2)
-        bring_g(2)
+        bring_g(2, picked_tile("g_picked2"))
         load_plane(c_high[:, TOKENS:], cT, 2)
-        e_bank2 = bring_c(2, c_high[:, TOKENS:], gather, "bank_e")
-        bring_g(3)
-        load_plane(c_high[:, 0:TOKENS], cT, 3)
-        e_bank3 = bring_c(3, c_high[:], gather_negated, "bank_wide0")
-        nc.gpsimd.tensor_tensor(made[:, high, 0, :], left[:, high, 0, :], right[:, high, 0, :], ALU.mult)
-        dd_bank0 = turn_dd(0, "bank_dd")
-        x_high = rows_tile("x_rows_high", 2)
-        nc.sync.dma_start(x_high[:].rearrange("p (a n) -> p a n", a=2), xT[2 * P :, :].rearrange("(a p) n -> p a n", p=P))
-        turn(e_bank2, gather_negated("x_picked2", x_high[:]), False, True)
-        nc.vector.tensor_copy(made[:, last, 2, :], x_high[:, TOKENS:].indirect(offsets[:]))
-        turn(e_bank3, made[:, last, 2, :], False, True)
-        behind_x2 = sb.tile([P, 3, SLOTS], F32, name="behind_x2", tag="x_picked2", align_bytes=64)
-        dd0 = behind_x2[:, 0, :]
-        one_less_g_high = behind_x2[:, 1:3, :]
-        dd0_parts = (slice(0, FIRST_SLOTS), slice(FIRST_SLOTS, SLOTS))
-        for part in dd0_parts:
-            nc.scalar.copy(out=dd0[:, part], in_=dd_bank0[:, part])
-        wc_raw = load_matrix(wc, "wc", "raw_a")
-        wg_raw = late.tile([P, PACK, K], F32, name="wg_raw", align_bytes=64, offset=0)
-        nc.sync.dma_start(wg_raw[:], wg.rearrange("(p j) n -> p j n", j=PACK))
-        for part in dd0_parts:
-            nc.vector.tensor_copy(windows[0][:].indirect(offsets[:, part.start // 16 : part.stop // 16]), dd0[:, part])
-        nc.sync.dma_start(out_1[blocks[0], :], windows[0][:])
+        e_bank2 = bring_c(2, gather(picked_tile("c_picked2"), c_high[:, TOKENS:]), "bank_e")
+        bring_g(3, picked_tile("g_picked3"))
+        nc.gpsimd.tensor_tensor(made[:, high, 0, :], dr_high[:], right[:, high, 0, :], ALU.mult)
 
         def scatter_dd(a, bank):
-            dd = sb.tile([P, SLOTS], F32, name="dd%d" % a)
+            if a == 0:
+                dd = picked_tile("g_picked3")
+            else:
+                dd = late.tile([P, SLOTS], F32, name="dd%d" % a, align_bytes=64, offset=(20 + 4 * a) * SLOTS)
             nc.scalar.copy(out=dd[:], in_=bank[:])
+            return dd
+
+        def store_dd(a, dd):
             nc.vector.tensor_copy(windows[a][:].indirect(offsets[:]), dd[:])
             nc.sync.dma_start(out_1[blocks[a], :], windows[a][:])
 
-        def form_z_high(kind, within):
+        dd0 = scatter_dd(0, turn_dd(0, "bank_dd"))
+        load_plane(c_high[:, 0:TOKENS], cT, 3)
+        e_bank3 = bring_c(3, gather_negated(picked_tile("c_picked3"), c_high[:]), "bank_wide0")
+        x_high = rows_tile("x_rows_high", 2)
+        nc.sync.dma_start(x_high[:].rearrange("p (a n) -> p a n", a=2), xT[2 * P :, :].rearrange("(a p) n -> p a n", p=P))
+        turn(e_bank2, gather_negated(picked_tile("x_picked2"), x_high[:]), False, True)
+        nc.vector.tensor_copy(made[:, last, 2, :], x_high[:, TOKENS:].indirect(offsets[:]))
+        turn(e_bank3, made[:, last, 2, :], False, True)
+        one_less_g_high = sb.tile([P, 2, SLOTS], F32, name="one_less_g_high")[:]
+        wc_raw = load_matrix(wc, "wc", "raw_a")
+        wg_raw = late.tile([P, PACK, K], F32, name="wg_raw", align_bytes=64, offset=0)
+        nc.sync.dma_start(wg_raw[:], wg.rearrange("(p j) n -> p j n", j=PACK))
+        store_dd(0, dd0)
+
+        def form_zg_high():
             nc.gpsimd.tensor_tensor(
-                z_turned[:, kind, within, 2 * P :].rearrange("p j (a d) -> p a j d", d=P),
-                by_block(made[:, high, 0, :])[:, :, within, :], by_block(made[:, high, 1 + kind, :])[:, :, within, :], ALU.mult,
+                z_turned[:, 0, :, 2 * P :].rearrange("p j (a d) -> p a j d", d=P),
+                by_block(made[:, high, 0, :]), by_block(made[:, high, 1, :]), ALU.mult,
             )
 
+        def form_zc(a, within):
+            nc.gpsimd.tensor_tensor(
+                z_turned[:, 1, within, blocks[a]],
+                by_block(made[:, a, 0:1, :])[:, 0, within, :], by_block(made[:, a, 2:3, :])[:, 0, within, :], ALU.mult,
+            )
+
+        form_zc(2, slice(0, BLOCKS))
+        nc.scalar.activation(one_less_g_high, right[:, high, 0, :], ACT.Copy, bias=1.0)
         nc.scalar.activation(right[:, 2, 1, :], e_bank2[:], ACT.Copy, scale=-1.0)
         nc.scalar.copy(out=right[:, 3, 1, :], in_=e_bank3[:])
-        nc.scalar.activation(one_less_g_high, right[:, high, 0, :], ACT.Copy, bias=1.0)
-        scatter_dd(1, turn_dd(1, "bank_dd"))
-        nc.scalar.activation(made[:, last, 2, :], c_sq[:, last, :], ACT.Copy, bias=-1.0)
+        store_dd(1, scatter_dd(1, turn_dd(1, "bank_dd")))
+        nc.scalar.activation(made[:, last, 2, :], c_sq[:, last - 1, :], ACT.Copy, bias=-1.0)
         nc.gpsimd.tensor_tensor(made[:, high, 1, :], one_less_g_high, right[:, high, 1, :], ALU.mult)
-        form_z_high(0, slice(0, BLOCKS))
+        form_zg_high()
         for half in range(2):
-            form_z_high(1, slice(2 * half, 2 * half + 2))
-        scatter_dd(2, turn_dd(2, "bank_wide0"))
+            form_zc(last, slice(2 * half, 2 * half + 2))
+        store_dd(2, scatter_dd(2, turn_dd(2, "bank_wide0")))
         last_bank = turn_dd(last, "bank_e")
         early = SLOTS - LATE_SLOTS
         dd_early = late.tile([P, early], F32, name="dd_early", align_bytes=64, offset=18 * SLOTS)[:]
@@ -252,7 +273,7 @@ def tile_attend_ghighw_kernel(tc, dy, wo, gT, cT, xT, wg, wc, offs, out_0, out_1
                 group(nc.scalar.copy, w_grouped[:, number * K + start : number * K + start + K // 2, :], raw[:, :, start : start + K // 2])
         late_codes = sb.tile([P, 4 * K], U32, name="late_codes", tag="made_then_codes", align_bytes=64)
         w_codes = late_codes[:, 0 : 2 * K]
-        w_scales = late.tile([P, 2 * K], U8, name="w_scales", align_bytes=64, offset=18 * SLOTS)[:]
+        w_scales = late.tile([P, 2 * K], U8, name="w_scales", align_bytes=64, offset=28 * SLOTS)[:]
         quantize(w_grouped[:], w_codes, w_scales, E4M3)
 
         words = z_turned[:].rearrange("p z j d -> p (z j d)").bitcast(F32)
@@ -268,10 +289,7 @@ def tile_attend_ghighw_kernel(tc, dy, wo, gT, cT, xT, wg, wc, offs, out_0, out_1
                         nc.tensor.transpose(bank[:, u, blocks[inner]], words[:, base + u : base + K // 2 : 2], identity[:])
                 nc.scalar.copy(out=grouped_words[:, 2 * P * half : 2 * P * (half + 1), :], in_=bank[:].rearrange("p u n -> p n u"))
             codes = late_codes[:, (2 + kind) * K : (3 + kind) * K]
-            if kind == 0:
-                scales = sb.tile([P, SLOTS], U8, name="zg_scales", tag="c_sq", align_bytes=64)
-            else:
-                scales = late.tile([P, SLOTS], U8, name="zc_scales", align_bytes=64, offset=0)
+            scales = sb.tile([P, SLOTS], U8, name="z_scales%d" % kind, align_bytes=64)
             quantize(flat_words.bitcast(BF16).rearrange("p (n j) -> p n j", j=PACK), codes, scales[:], E5M2)
             z_packed[kind] = (codes, scales[:])
 

@@ -22,7 +22,7 @@ TOKENS = 1024
 PLANES = K // P
 BLOCKS = SLOTS // P
 WINDOWS = 4
-VECTOR_SHARE = 320
+VECTOR_SHARE = 384
 LATE_SLOTS = 256
 FLOPS = 3 * 2 * K * K * SLOTS
 
@@ -55,17 +55,14 @@ def tile_attend_ghighw_kernel(tc, dy, wo, gT, cT, xT, wg, wc, offs, out_0, out_1
                     start=start and j == 0, stop=stop and j == BLOCKS - 1, is_transpose=True,
                 )
 
-        windows = []
-
-        def zeroed_window(tag):
-            window = sb.tile([P, TOKENS], F32, name="window%d" % len(windows), tag=tag, align_bytes=64)
-            nc.vector.memset(window[:].bitcast(I32), 0)
-            windows.append(window)
-
-        for w in range(WINDOWS - 1):
-            zeroed_window("window%d" % w)
         identity = sb.tile([P, P], F32, name="identity")
-        make_identity(nc, identity[:])
+        nc.vector.memset(identity[:], 0.0)
+        make_identity(nc, identity[:], nomemset=True)
+        windows = []
+        for w in range(WINDOWS):
+            window = sb.tile([P, TOKENS], F32, name="window%d" % w)
+            (nc.vector if w < WINDOWS // 2 else nc.gpsimd).memset(window[:].bitcast(I32), 0)
+            windows.append(window)
 
         offsets = lists.tile([P, SLOTS // 16], U16, name="offsets")
         nc.sync.dma_start(offsets[:], offs)
@@ -73,7 +70,6 @@ def tile_attend_ghighw_kernel(tc, dy, wo, gT, cT, xT, wg, wc, offs, out_0, out_1
         right = sb.tile([P, PLANES, 2, SLOTS], F32, name="right")
         made = sb.tile([P, PLANES, 3, SLOTS], F32, name="made", tag="made_then_codes", align_bytes=64)
         c_sq = sb.tile([P, PLANES, SLOTS], F32, name="c_sq", tag="c_sq", align_bytes=64)
-        one_less_g_first = sb.tile([P, SLOTS], F32, name="one_less_g_first", tag="one_less_g_first", align_bytes=64)
         z_turned = sb.tile([P, 2, BLOCKS, K], BF16, name="z_turned", tag="z_then_dd", align_bytes=64)
 
         def rows_tile(label, planes):
@@ -99,11 +95,11 @@ def tile_attend_ghighw_kernel(tc, dy, wo, gT, cT, xT, wg, wc, offs, out_0, out_1
             nc.vector.tensor_copy(picked, rows[:].indirect(offsets[:]))
             bank = psum.tile([P, SLOTS], F32, name="g_bank%d" % a, tag="bank_g")
             turn(bank, picked)
-            if a == 0:
-                nc.scalar.activation(one_less_g_first[:], bank[:], ACT.Copy, bias=1.0, scale=-1.0)
-            nc.scalar.activation(right[:, a, 0, :], bank[:], ACT.Copy, scale=-1.0)
-            if a == 1:
+            if a > 0:
+                nc.scalar.activation(right[:, a, 0, :], bank[:], ACT.Copy, scale=-1.0)
+            if a < 2:
                 nc.scalar.activation(left[:, a, 1, :], bank[:], ACT.Copy, bias=1.0, scale=-1.0)
+            return bank
 
         def turned(term, label, tag, stop=True):
             bank = psum.tile([P, SLOTS], F32, name=label, tag=tag)
@@ -127,25 +123,23 @@ def tile_attend_ghighw_kernel(tc, dy, wo, gT, cT, xT, wg, wc, offs, out_0, out_1
             square_c(a, c, c_sq[:, a - 1, :], made[:, a, 2, :] if a < last else None)
             return turned(c, "e_bank%d" % a, tag, stop=False)
 
+        wo_grouped = sb.tile([P, K, PACK], BF16, name="wo_grouped", align_bytes=64)
+        c_rows = rows_tile("c_rows0", 1)
+        load_plane(c_rows[:], cT, 0)
+        c = gather(picked_tile("c_picked0"), c_rows[:])
+        square_c(0, c, wo_grouped[:, K // 2 :, :].rearrange("p n j -> p (n j)").bitcast(F32), made[:, 0, 2, :])
+        e_bank = turned(c, "e_bank0", "bank_e", stop=False)
         x_low = rows_tile("x_rows_low", 2)
         load_plane(x_low[:, TOKENS:], xT, 0)
         minus_x = sb.tile([P, SLOTS], F32, name="minus_x")
         nc.scalar.activation(minus_x[:], gather(picked_tile("x_picked0"), x_low[:, TOKENS:]), ACT.Copy, scale=-1.0)
-        e_bank = turned(minus_x, "e_bank0", "bank_e", stop=False)
-        wo_grouped = sb.tile([P, K, PACK], BF16, name="wo_grouped", align_bytes=64)
-        bring_g(0, wo_grouped[:, K // 2 :, :].rearrange("p n j -> p (n j)").bitcast(F32))
-        c_rows = rows_tile("c_rows0", 1)
-        load_plane(c_rows[:], cT, 0)
-        c = gather(picked_tile("c_picked0"), c_rows[:])
-        turn(e_bank, c, False, True)
-        c_sq_first = sb.tile([P, SLOTS], F32, name="c_sq_first", tag="c_sq_first", align_bytes=64)
-        square_c(0, c, c_sq_first[:], made[:, 0, 2, :])
-        zeroed_window("c_rows0")
-        nc.vector.scalar_tensor_tensor(made[:, 0, 1, :], e_bank[:], -1.0, one_less_g_first[:], ALU.mult, ALU.mult)
+        turn(e_bank, minus_x, False, True)
+        nc.scalar.activation(right[:, 0, 1, :], e_bank[:], ACT.Copy, scale=-1.0)
+        g_bank = bring_g(0, made[:, 0, 1, :])
 
         wo_raw = load_matrix(wo, "wo", "raw_a")
         wo_codes = sb.tile([P, K], U32, name="wo_codes", align_bytes=64)
-        wo_scales = sb.tile([P, K], U8, name="wo_scales", tag="one_less_g_first", align_bytes=64)
+        wo_scales = sb.tile([P, K], U8, name="wo_scales", align_bytes=64)
         for copy, cols in ((nc.vector.tensor_copy, slice(0, VECTOR_SHARE)), (nc.scalar.copy, slice(VECTOR_SHARE, K))):
             group(copy, wo_grouped[:, cols, :], wo_raw[:, :, cols])
         quantize(wo_grouped[:], wo_codes[:], wo_scales[:], E4M3)
@@ -153,8 +147,8 @@ def tile_attend_ghighw_kernel(tc, dy, wo, gT, cT, xT, wg, wc, offs, out_0, out_1
         dy_raw = load_matrix(dy, "dy", "raw_b")
         dy_grouped, dy_blocks = [], []
         dy_halves = [
-            sb.tile([P, 2 * P, PACK], BF16, name="dy_grouped%d" % half, tag=tag, align_bytes=64)
-            for half, tag in enumerate(("raw_a", "c_sq_first"))
+            sb.tile([P, 2 * P, PACK], BF16, name="dy_grouped", tag="raw_a", align_bytes=64)[:],
+            made[:, 0, 1, :].bitcast(BF16).rearrange("p (n j) -> p n j", j=PACK),
         ]
 
         def group_dy(copy, j):
@@ -170,8 +164,10 @@ def tile_attend_ghighw_kernel(tc, dy, wo, gT, cT, xT, wg, wc, offs, out_0, out_1
 
         for j in range(BLOCKS):
             dy_grouped.append(group_dy(nc.vector.tensor_copy if j < BLOCKS // 2 else nc.scalar.copy, j))
+        nc.scalar.activation(right[:, 0, 0, :], g_bank[:], ACT.Copy, scale=-1.0)
         for j in range(BLOCKS):
             quantize_dy(dy_grouped[j], j)
+        nc.gpsimd.tensor_tensor(made[:, 0, 1, :], left[:, 0, 1, :], right[:, 0, 1, :], ALU.mult)
         dr_banks = []
         for j, (codes, scales) in enumerate(dy_blocks):
             bank = psum.tile([P, K], F32, name="dr_bank%d" % j, tag="bank_wide%d" % j)
@@ -216,7 +212,7 @@ def tile_attend_ghighw_kernel(tc, dy, wo, gT, cT, xT, wg, wc, offs, out_0, out_1
             if a == 0:
                 dd = picked_tile("g_picked3")
             else:
-                dd = late.tile([P, SLOTS], F32, name="dd%d" % a, align_bytes=64, offset=(20 + 4 * a) * SLOTS)
+                dd = sb.tile([P, SLOTS], F32, name="dd%d" % a, tag="raw_a" if a == 2 else "dd1", align_bytes=64)
             nc.scalar.copy(out=dd[:], in_=bank[:])
             return dd
 
@@ -260,6 +256,8 @@ def tile_attend_ghighw_kernel(tc, dy, wo, gT, cT, xT, wg, wc, offs, out_0, out_1
         form_zg_high()
         for half in range(2):
             form_zc(last, slice(2 * half, 2 * half + 2))
+        w_grouped = sb.tile([P, 2 * K, PACK], BF16, name="w_grouped", tag="c_sq", align_bytes=64)
+        group(nc.scalar.copy, w_grouped[:, 0:K, :], wc_raw[:])
         store_dd(2, scatter_dd(2, turn_dd(2, "bank_wide0")))
         last_bank = turn_dd(last, "bank_e")
         early = SLOTS - LATE_SLOTS
@@ -267,13 +265,10 @@ def tile_attend_ghighw_kernel(tc, dy, wo, gT, cT, xT, wg, wc, offs, out_0, out_1
         nc.scalar.copy(out=dd_early, in_=last_bank[:, 0:early])
         nc.vector.tensor_copy(windows[last][:].indirect(offsets[:, 0 : early // 16]), dd_early)
 
-        w_grouped = sb.tile([P, 2 * K, PACK], BF16, name="w_grouped", tag="c_sq", align_bytes=64)
-        for number, raw in enumerate((wc_raw, wg_raw)):
-            for start in (0, K // 2):
-                group(nc.scalar.copy, w_grouped[:, number * K + start : number * K + start + K // 2, :], raw[:, :, start : start + K // 2])
+        group(nc.scalar.copy, w_grouped[:, K:, :], wg_raw[:])
         late_codes = sb.tile([P, 4 * K], U32, name="late_codes", tag="made_then_codes", align_bytes=64)
         w_codes = late_codes[:, 0 : 2 * K]
-        w_scales = late.tile([P, 2 * K], U8, name="w_scales", align_bytes=64, offset=28 * SLOTS)[:]
+        w_scales = sb.tile([P, 2 * K], U8, name="w_scales", align_bytes=64)[:]
         quantize(w_grouped[:], w_codes, w_scales, E4M3)
 
         words = z_turned[:].rearrange("p z j d -> p (z j d)").bitcast(F32)

@@ -249,10 +249,10 @@ def tile_attend_ghighw_kernel(tc, dy, wo, gT, cT, xT, wg, wc, offs, out_0, out_1
         form_zc(2, slice(0, BLOCKS))
         nc.scalar.activation(one_less_g_high, right[:, high, 0, :], ACT.Copy, bias=1.0)
         nc.scalar.activation(right[:, 2, 1, :], e_bank2[:], ACT.Copy, scale=-1.0)
-        nc.scalar.copy(out=right[:, 3, 1, :], in_=e_bank3[:])
+        nc.vector.tensor_tensor(made[:, last, 1, :], one_less_g_high[:, 1, :], e_bank3[:], ALU.mult)
         store_dd(1, scatter_dd(1, turn_dd(1, "bank_dd")))
         nc.scalar.activation(made[:, last, 2, :], c_sq[:, last - 1, :], ACT.Copy, bias=-1.0)
-        nc.gpsimd.tensor_tensor(made[:, high, 1, :], one_less_g_high, right[:, high, 1, :], ALU.mult)
+        nc.gpsimd.tensor_tensor(made[:, 2, 1, :], one_less_g_high[:, 0, :], right[:, 2, 1, :], ALU.mult)
         form_zg_high()
         for half in range(2):
             form_zc(last, slice(2 * half, 2 * half + 2))

@@ -65,12 +65,11 @@ def tile_attend_ghighw_kernel(tc, dy, wo, gT, cT, xT, wg, wc, offs, out_0, out_1
             windows.append(window)
 
         offsets = lists.tile([P, SLOTS // 16], U16, name="offsets")
-        nc.sync.dma_start(offsets[:], offs)
         left = sb.tile([P, 2, 2, SLOTS], F32, name="left")
         right = sb.tile([P, PLANES, 2, SLOTS], F32, name="right")
         made = sb.tile([P, PLANES, 3, SLOTS], F32, name="made", tag="made_then_codes", align_bytes=64)
         c_sq = sb.tile([P, PLANES, SLOTS], F32, name="c_sq", tag="c_sq", align_bytes=64)
-        z_turned = sb.tile([P, 2, BLOCKS, K], BF16, name="z_turned", tag="z_then_dd", align_bytes=64)
+        z_turned = late.tile([P, 2, BLOCKS, K], BF16, name="z_turned", align_bytes=64, offset=20 * SLOTS)
 
         def rows_tile(label, planes):
             return sb.tile([P, planes * TOKENS], F32, name=label, tag=label, align_bytes=64)
@@ -97,7 +96,7 @@ def tile_attend_ghighw_kernel(tc, dy, wo, gT, cT, xT, wg, wc, offs, out_0, out_1
             turn(bank, picked)
             if a > 0:
                 nc.scalar.activation(right[:, a, 0, :], bank[:], ACT.Copy, scale=-1.0)
-            if a < 2:
+            if a == 1:
                 nc.scalar.activation(left[:, a, 1, :], bank[:], ACT.Copy, bias=1.0, scale=-1.0)
             return bank
 
@@ -123,18 +122,18 @@ def tile_attend_ghighw_kernel(tc, dy, wo, gT, cT, xT, wg, wc, offs, out_0, out_1
             square_c(a, c, c_sq[:, a - 1, :], made[:, a, 2, :] if a < last else None)
             return turned(c, "e_bank%d" % a, tag, stop=False)
 
-        wo_grouped = sb.tile([P, K, PACK], BF16, name="wo_grouped", align_bytes=64)
+        wo_grouped = sb.tile([P, VECTOR_SHARE + K // 2, PACK], BF16, name="wo_grouped", align_bytes=64)
         c_rows = rows_tile("c_rows0", 1)
         load_plane(c_rows[:], cT, 0)
+        nc.sync.dma_start(offsets[:], offs)
         c = gather(picked_tile("c_picked0"), c_rows[:])
-        square_c(0, c, wo_grouped[:, K // 2 :, :].rearrange("p n j -> p (n j)").bitcast(F32), made[:, 0, 2, :])
+        square_c(0, c, wo_grouped[:, VECTOR_SHARE:, :].rearrange("p n j -> p (n j)").bitcast(F32), made[:, 0, 2, :])
         e_bank = turned(c, "e_bank0", "bank_e", stop=False)
         x_low = rows_tile("x_rows_low", 2)
         load_plane(x_low[:, TOKENS:], xT, 0)
         minus_x = sb.tile([P, SLOTS], F32, name="minus_x")
         nc.scalar.activation(minus_x[:], gather(picked_tile("x_picked0"), x_low[:, TOKENS:]), ACT.Copy, scale=-1.0)
         turn(e_bank, minus_x, False, True)
-        nc.scalar.activation(right[:, 0, 1, :], e_bank[:], ACT.Copy, scale=-1.0)
         g_bank = bring_g(0, made[:, 0, 1, :])
 
         wo_raw = load_matrix(wo, "wo", "raw_a")
@@ -142,7 +141,9 @@ def tile_attend_ghighw_kernel(tc, dy, wo, gT, cT, xT, wg, wc, offs, out_0, out_1
         wo_scales = sb.tile([P, K], U8, name="wo_scales", align_bytes=64)
         for copy, cols in ((nc.vector.tensor_copy, slice(0, VECTOR_SHARE)), (nc.scalar.copy, slice(VECTOR_SHARE, K))):
             group(copy, wo_grouped[:, cols, :], wo_raw[:, :, cols])
-        quantize(wo_grouped[:], wo_codes[:], wo_scales[:], E4M3)
+        nc.scalar.activation(right[:, 0, 1, :], e_bank[:], ACT.Copy, scale=-1.0)
+        nc.scalar.activation(left[:, 0, 1, :], g_bank[:], ACT.Copy, bias=1.0, scale=-1.0)
+        quantize(wo_grouped[:, 0:K, :], wo_codes[:], wo_scales[:], E4M3)
 
         dy_raw = load_matrix(dy, "dy", "raw_b")
         dy_grouped, dy_blocks = [], []
@@ -230,7 +231,7 @@ def tile_attend_ghighw_kernel(tc, dy, wo, gT, cT, xT, wg, wc, offs, out_0, out_1
         turn(e_bank3, made[:, last, 2, :], False, True)
         one_less_g_high = sb.tile([P, 2, SLOTS], F32, name="one_less_g_high")[:]
         wc_raw = load_matrix(wc, "wc", "raw_a")
-        wg_raw = late.tile([P, PACK, K], F32, name="wg_raw", align_bytes=64, offset=0)
+        wg_raw = late.tile([P, PACK, K], F32, name="wg_raw", align_bytes=64, offset=4 * SLOTS)
         nc.sync.dma_start(wg_raw[:], wg.rearrange("(p j) n -> p j n", j=PACK))
         store_dd(0, dd0)
 
@@ -249,10 +250,10 @@ def tile_attend_ghighw_kernel(tc, dy, wo, gT, cT, xT, wg, wc, offs, out_0, out_1
         form_zc(2, slice(0, BLOCKS))
         nc.scalar.activation(one_less_g_high, right[:, high, 0, :], ACT.Copy, bias=1.0)
         nc.scalar.activation(right[:, 2, 1, :], e_bank2[:], ACT.Copy, scale=-1.0)
-        nc.vector.tensor_tensor(made[:, last, 1, :], one_less_g_high[:, 1, :], e_bank3[:], ALU.mult)
+        nc.scalar.copy(out=right[:, 3, 1, :], in_=e_bank3[:])
         store_dd(1, scatter_dd(1, turn_dd(1, "bank_dd")))
         nc.scalar.activation(made[:, last, 2, :], c_sq[:, last - 1, :], ACT.Copy, bias=-1.0)
-        nc.gpsimd.tensor_tensor(made[:, 2, 1, :], one_less_g_high[:, 0, :], right[:, 2, 1, :], ALU.mult)
+        nc.gpsimd.tensor_tensor(made[:, high, 1, :], one_less_g_high, right[:, high, 1, :], ALU.mult)
         form_zg_high()
         for half in range(2):
             form_zc(last, slice(2 * half, 2 * half + 2))
@@ -261,7 +262,7 @@ def tile_attend_ghighw_kernel(tc, dy, wo, gT, cT, xT, wg, wc, offs, out_0, out_1
         store_dd(2, scatter_dd(2, turn_dd(2, "bank_wide0")))
         last_bank = turn_dd(last, "bank_e")
         early = SLOTS - LATE_SLOTS
-        dd_early = late.tile([P, early], F32, name="dd_early", align_bytes=64, offset=18 * SLOTS)[:]
+        dd_early = sb.tile([P, early], F32, name="dd_early")[:]
         nc.scalar.copy(out=dd_early, in_=last_bank[:, 0:early])
         nc.vector.tensor_copy(windows[last][:].indirect(offsets[:, 0 : early // 16]), dd_early)
 
@@ -274,7 +275,7 @@ def tile_attend_ghighw_kernel(tc, dy, wo, gT, cT, xT, wg, wc, offs, out_0, out_1
         words = z_turned[:].rearrange("p z j d -> p (z j d)").bitcast(F32)
         z_packed = {}
         for kind in range(2):
-            flat_words = late.tile([P, 2 * SLOTS], F32, name="z_grouped%d" % kind, align_bytes=64, offset=10 * SLOTS * kind)[:]
+            flat_words = late.tile([P, 2 * SLOTS], F32, name="z_grouped%d" % kind, align_bytes=64, offset=8 * SLOTS * kind)[:]
             grouped_words = flat_words.rearrange("p (n u) -> p n u", u=2)
             for half in range(2):
                 bank = psum.tile([P, 2, 2 * P], F32, name="z_bank%d%d" % (kind, half), tag=("bank_wide1", "bank_wide2", "bank_wide3", "bank_c")[2 * kind + half])
@@ -300,7 +301,7 @@ def tile_attend_ghighw_kernel(tc, dy, wo, gT, cT, xT, wg, wc, offs, out_0, out_1
                 )
             s_banks.append(bank)
 
-        dd_late = late.tile([P, LATE_SLOTS], F32, name="dd_late", align_bytes=64, offset=8 * SLOTS)
+        dd_late = late.tile([P, LATE_SLOTS], F32, name="dd_late", align_bytes=64, offset=19 * SLOTS)
         nc.scalar.copy(out=dd_late[:], in_=last_bank[:, early:])
         nc.vector.tensor_copy(windows[last][:].indirect(offsets[:, early // 16 :]), dd_late[:])
         nc.sync.dma_start(out_1[blocks[last], :], windows[last][:])

@@ -71,6 +71,11 @@ def tile_attend_ghighw_kernel(tc, dy, wo, gT, cT, xT, wg, wc, offs, out_0, out_1
         c_sq = sb.tile([P, PLANES, SLOTS], F32, name="c_sq", tag="c_sq", align_bytes=64)
         z_turned = late.tile([P, 2, BLOCKS, K], BF16, name="z_turned", align_bytes=64, offset=20 * SLOTS)
 
+        lefts = [left]
+
+        def left_of(a):
+            return lefts[a // 2][:, a % 2, :, :]
+
         def rows_tile(label, planes):
             return sb.tile([P, planes * TOKENS], F32, name=label, tag=label, align_bytes=64)
 
@@ -96,8 +101,7 @@ def tile_attend_ghighw_kernel(tc, dy, wo, gT, cT, xT, wg, wc, offs, out_0, out_1
             turn(bank, picked)
             if a > 0:
                 nc.scalar.activation(right[:, a, 0, :], bank[:], ACT.Copy, scale=-1.0)
-            if a == 1:
-                nc.scalar.activation(left[:, a, 1, :], bank[:], ACT.Copy, bias=1.0, scale=-1.0)
+                nc.scalar.activation(left_of(a)[:, 1, :], bank[:], ACT.Copy, bias=1.0, scale=-1.0)
             return bank
 
         def turned(term, label, tag, stop=True):
@@ -183,90 +187,82 @@ def tile_attend_ghighw_kernel(tc, dy, wo, gT, cT, xT, wg, wc, offs, out_0, out_1
         form_z(0, made[:, 0, 1:3, :])
 
         def turn_dd(a, tag):
-            bank = turned(left[:, a, 0, :] if a < 2 else dr_high[:, a - 2, :], "dd_bank%d" % a, tag, stop=False)
+            bank = turned(left_of(a)[:, 0, :], "dd_bank%d" % a, tag, stop=False)
             turn(bank, made[:, a, 0, :], False, True)
             return bank
 
         second = sb.tile([P, 3, SLOTS], F32, name="second_picked", tag="raw_b", align_bytes=64)
         bring_g(1, second[:, 0, :])
-        c_rows = rows_tile("c_rows1", 1)
-        load_plane(c_rows[:], cT, 1)
-        e_bank = bring_c(1, gather(second[:, 1, :], c_rows[:]), "bank_dd")
+        c_middle = rows_tile("c_rows_middle", 2)
+        load_plane(c_middle[:, TOKENS:], cT, 1)
+        e_bank = bring_c(1, gather(second[:, 1, :], c_middle[:, TOKENS:]), "bank_dd")
         load_plane(x_low[:, 0:TOKENS], xT, 1)
         turn(e_bank, gather_negated(second[:, 2, :], x_low[:]), False, True)
         nc.scalar.activation(right[:, 1, 1, :], e_bank[:], ACT.Copy, scale=-1.0)
-        dr_high = sb.tile([P, 2, SLOTS], F32, name="dr_high", tag="raw_b", align_bytes=64)
+        lefts.append(sb.tile([P, 2, 2, SLOTS], F32, name="left_high", tag="raw_b", align_bytes=64))
         for j, bank in enumerate(dr_banks):
-            nc.scalar.copy(out=dr_high[:, :, blocks[j]], in_=bank[:, 2 * P :].rearrange("p (a d) -> p a d", d=P))
-        nc.gpsimd.tensor_tensor(made[:, 1, 0:2, :], left[:, 1, :, :], right[:, 1, :, :], ALU.mult)
+            nc.scalar.copy(out=lefts[1][:, :, 0, blocks[j]], in_=bank[:, 2 * P :].rearrange("p (a d) -> p a d", d=P))
+
+        def form_u_h(a):
+            nc.gpsimd.tensor_tensor(made[:, a, 0:2, :], left_of(a), right[:, a, :, :], ALU.mult)
+
+        form_u_h(1)
         form_z(1, made[:, 1, 1:3, :])
 
-        high = slice(2, PLANES)
-        c_high = rows_tile("c_rows_high", 2)
         bring_g(2, picked_tile("g_picked2"))
-        load_plane(c_high[:, TOKENS:], cT, 2)
-        e_bank2 = bring_c(2, gather(picked_tile("c_picked2"), c_high[:, TOKENS:]), "bank_e")
+        load_plane(c_middle[:, 0:TOKENS], cT, 2)
+        e_bank = bring_c(2, gather_negated(picked_tile("c_picked2"), c_middle[:]), "bank_e")
+        x_high = rows_tile("x_rows_high", 2)
+        load_plane(x_high[:, TOKENS:], xT, 2)
+        turn(e_bank, gather(picked_tile("x_picked2"), x_high[:, TOKENS:]), False, True)
+        nc.scalar.copy(out=right[:, 2, 1, :], in_=e_bank[:])
+        form_u_h(2)
+        form_z(2, made[:, 2, 1:3, :])
         bring_g(3, picked_tile("g_picked3"))
-        nc.gpsimd.tensor_tensor(made[:, high, 0, :], dr_high[:], right[:, high, 0, :], ALU.mult)
 
-        def scatter_dd(a, bank):
-            if a == 0:
-                dd = picked_tile("g_picked3")
-            else:
-                dd = sb.tile([P, SLOTS], F32, name="dd%d" % a, tag="raw_a" if a == 2 else "dd1", align_bytes=64)
-            nc.scalar.copy(out=dd[:], in_=bank[:])
+        def scatter_dd(a, bank, dd):
+            nc.scalar.copy(out=dd, in_=bank[:])
             return dd
 
         def store_dd(a, dd):
-            nc.vector.tensor_copy(windows[a][:].indirect(offsets[:]), dd[:])
+            nc.vector.tensor_copy(windows[a][:].indirect(offsets[:]), dd)
             nc.sync.dma_start(out_1[blocks[a], :], windows[a][:])
 
-        dd0 = scatter_dd(0, turn_dd(0, "bank_dd"))
-        load_plane(c_high[:, 0:TOKENS], cT, 3)
-        e_bank3 = bring_c(3, gather_negated(picked_tile("c_picked3"), c_high[:]), "bank_wide0")
-        x_high = rows_tile("x_rows_high", 2)
-        nc.sync.dma_start(x_high[:].rearrange("p (a n) -> p a n", a=2), xT[2 * P :, :].rearrange("(a p) n -> p a n", p=P))
-        turn(e_bank2, gather_negated(picked_tile("x_picked2"), x_high[:]), False, True)
-        nc.vector.tensor_copy(made[:, last, 2, :], x_high[:, TOKENS:].indirect(offsets[:]))
-        turn(e_bank3, made[:, last, 2, :], False, True)
-        one_less_g_high = sb.tile([P, 2, SLOTS], F32, name="one_less_g_high")[:]
+        dd0 = scatter_dd(0, turn_dd(0, "bank_dd"), picked_tile("g_picked3"))
+        c_rows = rows_tile("c_rows3", 1)
+        load_plane(c_rows[:], cT, 3)
+        e_bank = bring_c(3, gather(picked_tile("c_picked3"), c_rows[:]), "bank_wide0")
+        load_plane(x_high[:, 0:TOKENS], xT, 3)
+        turn(e_bank, gather_negated(made[:, last, 2, :], x_high[:]), False, True)
         wc_raw = load_matrix(wc, "wc", "raw_a")
         wg_raw = late.tile([P, PACK, K], F32, name="wg_raw", align_bytes=64, offset=4 * SLOTS)
         nc.sync.dma_start(wg_raw[:], wg.rearrange("(p j) n -> p j n", j=PACK))
         store_dd(0, dd0)
 
-        def form_zg_high():
+        def form_z_last(kind, within):
             nc.gpsimd.tensor_tensor(
-                z_turned[:, 0, :, 2 * P :].rearrange("p j (a d) -> p a j d", d=P),
-                by_block(made[:, high, 0, :]), by_block(made[:, high, 1, :]), ALU.mult,
+                z_turned[:, kind, within, blocks[last]],
+                by_block(made[:, last, :, :])[:, 0, within, :], by_block(made[:, last, :, :])[:, 1 + kind, within, :], ALU.mult,
             )
 
-        def form_zc(a, within):
-            nc.gpsimd.tensor_tensor(
-                z_turned[:, 1, within, blocks[a]],
-                by_block(made[:, a, 0:1, :])[:, 0, within, :], by_block(made[:, a, 2:3, :])[:, 0, within, :], ALU.mult,
-            )
-
-        form_zc(2, slice(0, BLOCKS))
-        nc.scalar.activation(one_less_g_high, right[:, high, 0, :], ACT.Copy, bias=1.0)
-        nc.scalar.activation(right[:, 2, 1, :], e_bank2[:], ACT.Copy, scale=-1.0)
-        nc.scalar.copy(out=right[:, 3, 1, :], in_=e_bank3[:])
-        store_dd(1, scatter_dd(1, turn_dd(1, "bank_dd")))
+        nc.scalar.activation(right[:, last, 1, :], e_bank[:], ACT.Copy, scale=-1.0)
+        store_dd(1, scatter_dd(1, turn_dd(1, "bank_dd"), picked_tile("dd1")))
         nc.scalar.activation(made[:, last, 2, :], c_sq[:, last - 1, :], ACT.Copy, bias=-1.0)
-        nc.gpsimd.tensor_tensor(made[:, high, 1, :], one_less_g_high, right[:, high, 1, :], ALU.mult)
-        form_zg_high()
+        form_u_h(last)
+        form_z_last(0, slice(0, BLOCKS))
         for half in range(2):
-            form_zc(last, slice(2 * half, 2 * half + 2))
+            form_z_last(1, slice(2 * half, 2 * half + 2))
         w_grouped = sb.tile([P, 2 * K, PACK], BF16, name="w_grouped", tag="c_sq", align_bytes=64)
         group(nc.scalar.copy, w_grouped[:, 0:K, :], wc_raw[:])
-        store_dd(2, scatter_dd(2, turn_dd(2, "bank_wide0")))
+        behind_wc = sb.tile([P, 2, SLOTS], F32, name="behind_wc", tag="raw_a", align_bytes=64)
+        store_dd(2, scatter_dd(2, turn_dd(2, "bank_wide0"), behind_wc[:, 0, :]))
         last_bank = turn_dd(last, "bank_e")
         early = SLOTS - LATE_SLOTS
-        dd_early = sb.tile([P, early], F32, name="dd_early")[:]
+        group(nc.scalar.copy, w_grouped[:, K : K + K // 2, :], wg_raw[:, :, 0 : K // 2])
+        dd_early = behind_wc[:, 1, 0:early]
         nc.scalar.copy(out=dd_early, in_=last_bank[:, 0:early])
         nc.vector.tensor_copy(windows[last][:].indirect(offsets[:, 0 : early // 16]), dd_early)
-
-        group(nc.scalar.copy, w_grouped[:, K:, :], wg_raw[:])
+        group(nc.scalar.copy, w_grouped[:, K + K // 2 :, :], wg_raw[:, :, K // 2 :])
         late_codes = sb.tile([P, 4 * K], U32, name="late_codes", tag="made_then_codes", align_bytes=64)
         w_codes = late_codes[:, 0 : 2 * K]
         w_scales = sb.tile([P, 2 * K], U8, name="w_scales", align_bytes=64)[:]
@@ -304,7 +300,7 @@ def tile_attend_ghighw_kernel(tc, dy, wo, gT, cT, xT, wg, wc, offs, out_0, out_1
         dd_late = late.tile([P, LATE_SLOTS], F32, name="dd_late", align_bytes=64, offset=19 * SLOTS)
         nc.scalar.copy(out=dd_late[:], in_=last_bank[:, early:])
         nc.vector.tensor_copy(windows[last][:].indirect(offsets[:, early // 16 :]), dd_late[:])
-        nc.sync.dma_start(out_1[blocks[last], :], windows[last][:])
+        nc.gpsimd.dma_start(out_1[blocks[last], :], windows[last][:])
         for r in range(PLANES):
             s = sb.tile([P, SLOTS], F32, name="s%d" % r)
             nc.scalar.copy(out=s[:], in_=s_banks[r][:])

@@ -23,7 +23,7 @@ PLANES = K // P
 BLOCKS = SLOTS // P
 WINDOWS = 4
 VECTOR_SHARE = 384
-LATE_SLOTS = 256
+LATE_SLOTS = 320
 FLOPS = 3 * 2 * K * K * SLOTS
 
 
@@ -218,7 +218,6 @@ def tile_attend_ghighw_kernel(tc, dy, wo, gT, cT, xT, wg, wc, offs, out_0, out_1
         nc.scalar.copy(out=right[:, 2, 1, :], in_=e_bank[:])
         form_u_h(2)
         form_z(2, made[:, 2, 1:3, :])
-        bring_g(3, picked_tile("g_picked3"))
 
         def scatter_dd(a, bank, dd):
             nc.scalar.copy(out=dd, in_=bank[:])
@@ -228,7 +227,8 @@ def tile_attend_ghighw_kernel(tc, dy, wo, gT, cT, xT, wg, wc, offs, out_0, out_1
             nc.vector.tensor_copy(windows[a][:].indirect(offsets[:]), dd)
             nc.sync.dma_start(out_1[blocks[a], :], windows[a][:])
 
-        dd0 = scatter_dd(0, turn_dd(0, "bank_dd"), picked_tile("g_picked3"))
+        dd0 = scatter_dd(0, turn_dd(0, "bank_dd"), picked_tile("x_picked2"))
+        bring_g(3, picked_tile("g_picked3"))
         c_rows = rows_tile("c_rows3", 1)
         load_plane(c_rows[:], cT, 3)
         e_bank = bring_c(3, gather(picked_tile("c_picked3"), c_rows[:]), "bank_wide0")

@@ -231,7 +231,12 @@ def tile_attend_ghighw_kernel(tc, dy, wo, gT, cT, xT, wg, wc, offs, out_0, out_1
         bring_g(3, picked_tile("g_picked3"))
         c_rows = rows_tile("c_rows3", 1)
         load_plane(c_rows[:], cT, 3)
-        e_bank = bring_c(3, gather(picked_tile("c_picked3"), c_rows[:]), "bank_wide0")
+        w_grouped = sb.tile([P, 2 * K, PACK], BF16, name="w_grouped", align_bytes=64)
+        w_words = w_grouped[:].rearrange("p n j -> p (n j)").bitcast(F32)
+        c = gather(w_words[:, 0:SLOTS], c_rows[:])
+        c_sq_last = w_words[:, 5 * SLOTS // 2 : 7 * SLOTS // 2]
+        square_c(last, c, c_sq_last, None)
+        e_bank = turned(c, "e_bank3", "bank_wide0", stop=False)
         load_plane(x_high[:, 0:TOKENS], xT, 3)
         turn(e_bank, gather_negated(made[:, last, 2, :], x_high[:]), False, True)
         wc_raw = load_matrix(wc, "wc", "raw_a")
@@ -247,12 +252,11 @@ def tile_attend_ghighw_kernel(tc, dy, wo, gT, cT, xT, wg, wc, offs, out_0, out_1
 
         nc.scalar.activation(right[:, last, 1, :], e_bank[:], ACT.Copy, scale=-1.0)
         store_dd(1, scatter_dd(1, turn_dd(1, "bank_dd"), picked_tile("dd1")))
-        nc.scalar.activation(made[:, last, 2, :], c_sq[:, last - 1, :], ACT.Copy, bias=-1.0)
+        nc.scalar.activation(made[:, last, 2, :], c_sq_last, ACT.Copy, bias=-1.0)
         form_u_h(last)
         form_z_last(0, slice(0, BLOCKS))
         for half in range(2):
             form_z_last(1, slice(2 * half, 2 * half + 2))
-        w_grouped = sb.tile([P, 2 * K, PACK], BF16, name="w_grouped", tag="c_sq", align_bytes=64)
         group(nc.scalar.copy, w_grouped[:, 0:K, :], wc_raw[:])
         behind_wc = sb.tile([P, 2, SLOTS], F32, name="behind_wc", tag="raw_a", align_bytes=64)
         store_dd(2, scatter_dd(2, turn_dd(2, "bank_wide0"), behind_wc[:, 0, :]))

@@ -24,6 +24,7 @@ BLOCKS = SLOTS // P
 WINDOWS = 4
 VECTOR_SHARE = 384
 LATE_SLOTS = 320
+WG_TAIL = 64
 FLOPS = 3 * 2 * K * K * SLOTS
 
 
@@ -68,7 +69,7 @@ def tile_attend_ghighw_kernel(tc, dy, wo, gT, cT, xT, wg, wc, offs, out_0, out_1
         left = sb.tile([P, 2, 2, SLOTS], F32, name="left")
         right = sb.tile([P, PLANES, 2, SLOTS], F32, name="right")
         made = sb.tile([P, PLANES, 3, SLOTS], F32, name="made", tag="made_then_codes", align_bytes=64)
-        c_sq = sb.tile([P, PLANES, SLOTS], F32, name="c_sq", tag="c_sq", align_bytes=64)
+        c_sq = sb.tile([P, 2, SLOTS], F32, name="c_sq")
         z_turned = late.tile([P, 2, BLOCKS, K], BF16, name="z_turned", align_bytes=64, offset=20 * SLOTS)
 
         lefts = [left]
@@ -121,10 +122,6 @@ def tile_attend_ghighw_kernel(tc, dy, wo, gT, cT, xT, wg, wc, offs, out_0, out_1
             nc.scalar.activation(c_sq, turned(c, "c_bank%d" % a, "bank_c")[:], ACT.Square)
             if out is not None:
                 nc.scalar.activation(out, c_sq, ACT.Copy, bias=-1.0)
-
-        def bring_c(a, c, tag):
-            square_c(a, c, c_sq[:, a - 1, :], made[:, a, 2, :] if a < last else None)
-            return turned(c, "e_bank%d" % a, tag, stop=False)
 
         wo_grouped = sb.tile([P, VECTOR_SHARE + K // 2, PACK], BF16, name="wo_grouped", align_bytes=64)
         c_rows = rows_tile("c_rows0", 1)
@@ -195,7 +192,9 @@ def tile_attend_ghighw_kernel(tc, dy, wo, gT, cT, xT, wg, wc, offs, out_0, out_1
         bring_g(1, second[:, 0, :])
         c_middle = rows_tile("c_rows_middle", 2)
         load_plane(c_middle[:, TOKENS:], cT, 1)
-        e_bank = bring_c(1, gather(second[:, 1, :], c_middle[:, TOKENS:]), "bank_dd")
+        c = gather(second[:, 1, :], c_middle[:, TOKENS:])
+        square_c(1, c, c_sq[:, 0, :], made[:, 1, 2, :])
+        e_bank = turned(c, "e_bank1", "bank_dd", stop=False)
         load_plane(x_low[:, 0:TOKENS], xT, 1)
         turn(e_bank, gather_negated(second[:, 2, :], x_low[:]), False, True)
         nc.scalar.activation(right[:, 1, 1, :], e_bank[:], ACT.Copy, scale=-1.0)
@@ -211,11 +210,13 @@ def tile_attend_ghighw_kernel(tc, dy, wo, gT, cT, xT, wg, wc, offs, out_0, out_1
 
         bring_g(2, picked_tile("g_picked2"))
         load_plane(c_middle[:, 0:TOKENS], cT, 2)
-        e_bank = bring_c(2, gather_negated(picked_tile("c_picked2"), c_middle[:]), "bank_e")
-        x_high = rows_tile("x_rows_high", 2)
-        load_plane(x_high[:, TOKENS:], xT, 2)
-        turn(e_bank, gather(picked_tile("x_picked2"), x_high[:, TOKENS:]), False, True)
+        c = gather_negated(picked_tile("c_picked2"), c_middle[:])
+        e_bank = turned(c, "e_bank2", "bank_e", stop=False)
+        x_rows = rows_tile("x_rows2", 1)
+        load_plane(x_rows[:], xT, 2)
+        turn(e_bank, gather(picked_tile("x_picked2"), x_rows[:]), False, True)
         nc.scalar.copy(out=right[:, 2, 1, :], in_=e_bank[:])
+        square_c(2, c, c_sq[:, 1, :], made[:, 2, 2, :])
         form_u_h(2)
         form_z(2, made[:, 2, 1:3, :])
 
@@ -233,40 +234,44 @@ def tile_attend_ghighw_kernel(tc, dy, wo, gT, cT, xT, wg, wc, offs, out_0, out_1
         load_plane(c_rows[:], cT, 3)
         w_grouped = sb.tile([P, 2 * K, PACK], BF16, name="w_grouped", align_bytes=64)
         w_words = w_grouped[:].rearrange("p n j -> p (n j)").bitcast(F32)
-        c = gather(w_words[:, 0:SLOTS], c_rows[:])
-        c_sq_last = w_words[:, 5 * SLOTS // 2 : 7 * SLOTS // 2]
+        c = gather(picked_tile("c_picked3"), c_rows[:])
+        c_sq_last = w_words[:, 3 * SLOTS :]
         square_c(last, c, c_sq_last, None)
         e_bank = turned(c, "e_bank3", "bank_wide0", stop=False)
-        load_plane(x_high[:, 0:TOKENS], xT, 3)
-        turn(e_bank, gather_negated(made[:, last, 2, :], x_high[:]), False, True)
+        x_rows = rows_tile("x_rows3", 1)
+        load_plane(x_rows[:], xT, 3)
+        nc.scalar.activation(w_words[:, 0:SLOTS], gather(picked_tile("x_picked3"), x_rows[:]), ACT.Copy, scale=-1.0)
+        turn(e_bank, w_words[:, 0:SLOTS], False, True)
         wc_raw = load_matrix(wc, "wc", "raw_a")
         wg_raw = late.tile([P, PACK, K], F32, name="wg_raw", align_bytes=64, offset=4 * SLOTS)
         nc.sync.dma_start(wg_raw[:], wg.rearrange("(p j) n -> p j n", j=PACK))
         store_dd(0, dd0)
 
-        def form_z_last(kind, within):
+        def form_z_last(kind, factor, within):
             nc.gpsimd.tensor_tensor(
                 z_turned[:, kind, within, blocks[last]],
-                by_block(made[:, last, :, :])[:, 0, within, :], by_block(made[:, last, :, :])[:, 1 + kind, within, :], ALU.mult,
+                by_block(made[:, last, :, :])[:, 0, within, :], by_block(factor)[:, 0, within, :], ALU.mult,
             )
 
         nc.scalar.activation(right[:, last, 1, :], e_bank[:], ACT.Copy, scale=-1.0)
         store_dd(1, scatter_dd(1, turn_dd(1, "bank_dd"), picked_tile("dd1")))
-        nc.scalar.activation(made[:, last, 2, :], c_sq_last, ACT.Copy, bias=-1.0)
         form_u_h(last)
-        form_z_last(0, slice(0, BLOCKS))
-        for half in range(2):
-            form_z_last(1, slice(2 * half, 2 * half + 2))
+        form_z_last(0, made[:, last, 1:2, :], slice(0, BLOCKS))
         group(nc.scalar.copy, w_grouped[:, 0:K, :], wc_raw[:])
         behind_wc = sb.tile([P, 2, SLOTS], F32, name="behind_wc", tag="raw_a", align_bytes=64)
         store_dd(2, scatter_dd(2, turn_dd(2, "bank_wide0"), behind_wc[:, 0, :]))
         last_bank = turn_dd(last, "bank_e")
+        csq_less_one_last = left_of(2)[:, 0:1, :]
+        nc.scalar.activation(csq_less_one_last[:, 0, :], c_sq_last, ACT.Copy, bias=-1.0)
+        z_parts = ((slice(0, 2), slice(2, 4)), (slice(0, 2), slice(2, 3), slice(3, 4)))
+        for within in z_parts[1]:
+            form_z_last(1, csq_less_one_last, within)
         early = SLOTS - LATE_SLOTS
-        group(nc.scalar.copy, w_grouped[:, K : K + K // 2, :], wg_raw[:, :, 0 : K // 2])
+        group(nc.scalar.copy, w_grouped[:, K : 2 * K - WG_TAIL, :], wg_raw[:, :, 0 : K - WG_TAIL])
         dd_early = behind_wc[:, 1, 0:early]
         nc.scalar.copy(out=dd_early, in_=last_bank[:, 0:early])
         nc.vector.tensor_copy(windows[last][:].indirect(offsets[:, 0 : early // 16]), dd_early)
-        group(nc.scalar.copy, w_grouped[:, K + K // 2 :, :], wg_raw[:, :, K // 2 :])
+        group(nc.scalar.copy, w_grouped[:, 2 * K - WG_TAIL :, :], wg_raw[:, :, K - WG_TAIL :])
         late_codes = sb.tile([P, 4 * K], U32, name="late_codes", tag="made_then_codes", align_bytes=64)
         w_codes = late_codes[:, 0 : 2 * K]
         w_scales = sb.tile([P, 2 * K], U8, name="w_scales", align_bytes=64)[:]
@@ -274,23 +279,25 @@ def tile_attend_ghighw_kernel(tc, dy, wo, gT, cT, xT, wg, wc, offs, out_0, out_1
 
         words = z_turned[:].rearrange("p z j d -> p (z j d)").bitcast(F32)
         z_packed = {}
+        z_banks = ({0: "bank_wide1", 2: "bank_wide2"}, {0: "bank_wide3", 2: "bank_c", 3: "bank_g"})
         for kind in range(2):
             flat_words = late.tile([P, 2 * SLOTS], F32, name="z_grouped%d" % kind, align_bytes=64, offset=8 * SLOTS * kind)[:]
             grouped_words = flat_words.rearrange("p (n u) -> p n u", u=2)
-            for half in range(2):
-                bank = psum.tile([P, 2, 2 * P], F32, name="z_bank%d%d" % (kind, half), tag=("bank_wide1", "bank_wide2", "bank_wide3", "bank_c")[2 * kind + half])
-                for inner in range(2):
-                    base = (kind * BLOCKS + 2 * half + inner) * (K // 2)
+            for within in z_parts[kind]:
+                count = within.stop - within.start
+                bank = psum.tile([P, 2, count * P], F32, name="z_bank%d%d" % (kind, within.start), tag=z_banks[kind][within.start])
+                for inner in range(count):
+                    base = (kind * BLOCKS + within.start + inner) * (K // 2)
                     for u in range(2):
                         nc.tensor.transpose(bank[:, u, blocks[inner]], words[:, base + u : base + K // 2 : 2], identity[:])
-                nc.scalar.copy(out=grouped_words[:, 2 * P * half : 2 * P * (half + 1), :], in_=bank[:].rearrange("p u n -> p n u"))
+                nc.scalar.copy(out=grouped_words[:, P * within.start : P * within.stop, :], in_=bank[:].rearrange("p u n -> p n u"))
             codes = late_codes[:, (2 + kind) * K : (3 + kind) * K]
             scales = sb.tile([P, SLOTS], U8, name="z_scales%d" % kind, align_bytes=64)
             quantize(flat_words.bitcast(BF16).rearrange("p (n j) -> p n j", j=PACK), codes, scales[:], E5M2)
             z_packed[kind] = (codes, scales[:])
 
         s_banks = []
-        for r, tag in enumerate(("bank_g", "bank_dd", "bank_wide0", "bank_wide1")):
+        for r, tag in enumerate(("bank_dd", "bank_wide0", "bank_wide1", "bank_wide2")):
             bank = psum.tile([P, SLOTS], F32, name="s_bank%d" % r, tag=tag)
             for number, kind in enumerate((0, 1) if r == 0 else (1, 0)):
                 cols = slice((1 - kind) * K + r * P, (1 - kind) * K + (r + 1) * P)

@@ -1,7 +1,6 @@
 from contextlib import ExitStack
 
 import concourse.mybir as mybir
-from concourse.masks import make_identity
 
 F32 = mybir.dt.float32
 BF16 = mybir.dt.bfloat16
@@ -19,12 +18,11 @@ PACK = 4
 K = 512
 SLOTS = 512
 TOKENS = 1024
-PLANES = K // P
 BLOCKS = SLOTS // P
-WINDOWS = 4
-VECTOR_SHARE = 384
-LATE_SLOTS = 320
-WG_TAIL = 64
+WINDOWS = 6
+VECTOR_SHARE = 352
+KIB = 1024
+EDGE = 64
 FLOPS = 3 * 2 * K * K * SLOTS
 
 
@@ -33,288 +31,215 @@ def tile_attend_ghighw_kernel(tc, dy, wo, gT, cT, xT, wg, wc, offs, out_0, out_1
     with ExitStack() as ctx:
         lists = ctx.enter_context(tc.tile_pool(name="lists", bufs=1))
         sb = ctx.enter_context(tc.tile_pool(name="sb", bufs=1))
-        late = ctx.enter_context(tc.tile_pool(name="late", bufs=1))
+        shared = ctx.enter_context(tc.tile_pool(name="shared", bufs=1))
         psum = ctx.enter_context(tc.psum_pool(name="psum", bufs=1))
         blocks = [slice(j * P, (j + 1) * P) for j in range(BLOCKS)]
-        last = PLANES - 1
+        halves = [slice(h * SLOTS // 2, (h + 1) * SLOTS // 2) for h in range(2)]
+        last = PACK - 1
 
-        def load_matrix(matrix, label, tag):
-            raw = sb.tile([P, PACK, K], F32, name=label + "_raw", tag=tag, align_bytes=64)
-            nc.sync.dma_start(raw[:], matrix.rearrange("(p j) n -> p j n", j=PACK))
+        def tile(label, shape, dtype, place=None):
+            if place is None:
+                return sb.tile([P] + shape, dtype, name=label, align_bytes=64)
+            return shared.tile([P] + shape, dtype, name=label, align_bytes=64, offset=place)
+
+        def by_plane(matrix):
+            return matrix.rearrange("(p t) n -> p t n", t=PACK)
+
+        def load_matrix(matrix, label, place):
+            raw = tile(label + "_raw", [PACK, K], F32, place)
+            nc.sync.dma_start(raw[:], by_plane(matrix))
             return raw
+
+        def load_plane(label):
+            rows = tile(label + "_rows", [TOKENS], F32, rows_place.get(label))
+            nc.sync.dma_start(rows[:], by_plane({"g": gT, "c": cT, "x": xT}[label[0]])[:, int(label[1]), :])
+            return rows
 
         def group(copy, grouped, raw):
             copy(out=grouped.rearrange("p (c i) j -> p c j i", i=4), in_=raw.rearrange("p j (c i) -> p c j i", i=4))
 
-        def quantize(grouped, codes, scales, fmt):
-            nc.vector.quantize_mx(out=codes.bitcast(fmt), scales=scales, in_=grouped.rearrange("p n j -> p (n j)"))
+        def quantize(grouped, label, fmt, place=None, codes_place=None):
+            width = grouped.shape[1]
+            codes = tile(label + "_codes", [width], U32, codes_place)
+            scales = tile(label + "_scales", [width], U8, place)
+            nc.vector.quantize_mx(out=codes[:].bitcast(fmt), scales=scales[:], in_=grouped.rearrange("p n j -> p (n j)"))
+            return codes, scales
 
-        def turn(bank, term, start=True, stop=True):
-            for j, block in enumerate(blocks):
-                nc.tensor.matmul(
-                    bank[:, block], term[:, block], identity[:],
-                    start=start and j == 0, stop=stop and j == BLOCKS - 1, is_transpose=True,
-                )
+        def product(out, weights, columns, moving, slots, start, stop):
+            nc.tensor.matmul_mx(
+                out=out, lhsT=weights[0][:, columns].bitcast(E4M3), lhsT_scale=weights[1][:, columns],
+                rhs=moving[0][:, slots].bitcast(E5M2), rhs_scale=moving[1][:, slots], start=start, stop=stop,
+            )
 
-        identity = sb.tile([P, P], F32, name="identity")
-        nc.vector.memset(identity[:], 0.0)
-        make_identity(nc, identity[:], nomemset=True)
+        def listed(slots):
+            return offsets[:, slots.start // 16 : slots.stop // 16]
+
+        def gather_on_vector(picked, rows):
+            nc.vector.tensor_copy(picked, rows[:].indirect(offsets[:]))
+
+        def gather_on_scalar(picked, rows):
+            nc.scalar.activation(picked, rows[:].indirect(offsets[:]), ACT.Copy)
+
+        def by_pairs(planes):
+            return planes.rearrange("p t (c i) -> p c t i", i=2)
+
+        def woven(grouped):
+            return grouped.rearrange("p (c i) t -> p c t i", i=2)
+
+        dy_raw_at, dy_grouped_at = 20 * KIB, 4 * KIB - EDGE
+        wo_codes_at, dy_codes_at, dy_scales_at = 30 * KIB, 36 * KIB, 42 * KIB
+        picked_place = {
+            "g0": dy_raw_at, "c0": dy_raw_at + 2 * KIB, "x0": 4 * KIB,
+            "c1": wo_codes_at - 2 * KIB + EDGE, "g1": wo_codes_at + 2 * KIB - EDGE,
+            "x1": dy_codes_at - 2 * KIB + EDGE, "c2": dy_codes_at + 2 * KIB - EDGE, "c3": dy_scales_at,
+        }
+        ring = [44 * KIB + 8 * KIB * n for n in range(6)]
+        rows_place = dict(zip(("c1", "g1", "x1", "c2", "c3", "x2"), ring))
+        rows_place.update({"g2": ring[1], "g3": ring[2], "x3": ring[3]})
+        rows_place["x2"] = ring[0]
         windows = []
-        for w in range(WINDOWS):
-            window = sb.tile([P, TOKENS], F32, name="window%d" % w)
-            (nc.vector if w < WINDOWS // 2 else nc.gpsimd).memset(window[:].bitcast(I32), 0)
+
+        def clear_window(engine, place=None):
+            window = tile("window%d" % len(windows), [TOKENS], F32, place)
+            engine.memset(window[:].bitcast(I32), 0)
             windows.append(window)
 
+        for engine in (nc.vector, nc.gpsimd, nc.vector, nc.gpsimd):
+            clear_window(engine)
+
+        wo_raw = load_matrix(wo, "wo", None)
+        dy_raw = load_matrix(dy, "dy", dy_raw_at)
         offsets = lists.tile([P, SLOTS // 16], U16, name="offsets")
-        left = sb.tile([P, 2, 2, SLOTS], F32, name="left")
-        right = sb.tile([P, PLANES, 2, SLOTS], F32, name="right")
-        made = sb.tile([P, PLANES, 3, SLOTS], F32, name="made", tag="made_then_codes", align_bytes=64)
-        c_sq = sb.tile([P, 2, SLOTS], F32, name="c_sq")
-        z_turned = late.tile([P, 2, BLOCKS, K], BF16, name="z_turned", align_bytes=64, offset=20 * SLOTS)
-
-        lefts = [left]
-
-        def left_of(a):
-            return lefts[a // 2][:, a % 2, :, :]
-
-        def rows_tile(label, planes):
-            return sb.tile([P, planes * TOKENS], F32, name=label, tag=label, align_bytes=64)
-
-        def load_plane(rows, table, a):
-            nc.sync.dma_start(rows, table[blocks[a], :])
-
-        def picked_tile(label):
-            return sb.tile([P, SLOTS], F32, name=label, tag=label, align_bytes=64)[:]
-
-        def gather(picked, rows):
-            nc.vector.tensor_copy(picked, rows.indirect(offsets[:]))
-            return picked
-
-        def gather_negated(picked, rows):
-            nc.vector.tensor_scalar(picked, rows.indirect(offsets[:]), -1.0, 0.0, ALU.mult, ALU.add)
-            return picked
-
-        def bring_g(a, picked):
-            rows = rows_tile("g_rows%d" % a, 1)
-            load_plane(rows[:], gT, a)
-            nc.vector.tensor_copy(picked, rows[:].indirect(offsets[:]))
-            bank = psum.tile([P, SLOTS], F32, name="g_bank%d" % a, tag="bank_g")
-            turn(bank, picked)
-            if a > 0:
-                nc.scalar.activation(right[:, a, 0, :], bank[:], ACT.Copy, scale=-1.0)
-                nc.scalar.activation(left_of(a)[:, 1, :], bank[:], ACT.Copy, bias=1.0, scale=-1.0)
-            return bank
-
-        def turned(term, label, tag, stop=True):
-            bank = psum.tile([P, SLOTS], F32, name=label, tag=tag)
-            turn(bank, term, True, stop)
-            return bank
-
-        def by_block(ap):
-            return ap.rearrange("p z (j d) -> p z j d", d=P)
-
-        def form_z(a, factors):
-            nc.gpsimd.tensor_tensor(
-                z_turned[:, :, :, blocks[a]], by_block(made[:, a, 0:1, :].to_broadcast([P, 2, SLOTS])), by_block(factors), ALU.mult
-            )
-
-        def square_c(a, c, c_sq, out):
-            nc.scalar.activation(c_sq, turned(c, "c_bank%d" % a, "bank_c")[:], ACT.Square)
-            if out is not None:
-                nc.scalar.activation(out, c_sq, ACT.Copy, bias=-1.0)
-
-        wo_grouped = sb.tile([P, VECTOR_SHARE + K // 2, PACK], BF16, name="wo_grouped", align_bytes=64)
-        c_rows = rows_tile("c_rows0", 1)
-        load_plane(c_rows[:], cT, 0)
         nc.sync.dma_start(offsets[:], offs)
-        c = gather(picked_tile("c_picked0"), c_rows[:])
-        square_c(0, c, wo_grouped[:, VECTOR_SHARE:, :].rearrange("p n j -> p (n j)").bitcast(F32), made[:, 0, 2, :])
-        e_bank = turned(c, "e_bank0", "bank_e", stop=False)
-        x_low = rows_tile("x_rows_low", 2)
-        load_plane(x_low[:, TOKENS:], xT, 0)
-        minus_x = sb.tile([P, SLOTS], F32, name="minus_x")
-        nc.scalar.activation(minus_x[:], gather(picked_tile("x_picked0"), x_low[:, TOKENS:]), ACT.Copy, scale=-1.0)
-        turn(e_bank, minus_x, False, True)
-        g_bank = bring_g(0, made[:, 0, 1, :])
 
-        wo_raw = load_matrix(wo, "wo", "raw_a")
-        wo_codes = sb.tile([P, K], U32, name="wo_codes", align_bytes=64)
-        wo_scales = sb.tile([P, K], U8, name="wo_scales", align_bytes=64)
+        wo_grouped = tile("wo_grouped", [K, PACK], BF16)
+        dealt = wo_grouped[:].rearrange("p (t m) j -> p m j t", t=PACK)
+        source = wo_raw[:].rearrange("p j (m t) -> p m j t", t=PACK)
+        cut = VECTOR_SHARE // PACK
+        nc.vector.tensor_copy(out=dealt[:, 0:cut], in_=source[:, 0:cut])
+        nc.scalar.copy(out=dealt[:, cut:], in_=source[:, cut:])
+        wo_mx = quantize(wo_grouped[:], "wo", E4M3, None, wo_codes_at)
+        dy_grouped = tile("dy_grouped", [SLOTS, PACK], BF16, dy_grouped_at)
         for copy, cols in ((nc.vector.tensor_copy, slice(0, VECTOR_SHARE)), (nc.scalar.copy, slice(VECTOR_SHARE, K))):
-            group(copy, wo_grouped[:, cols, :], wo_raw[:, :, cols])
-        nc.scalar.activation(right[:, 0, 1, :], e_bank[:], ACT.Copy, scale=-1.0)
-        nc.scalar.activation(left[:, 0, 1, :], g_bank[:], ACT.Copy, bias=1.0, scale=-1.0)
-        quantize(wo_grouped[:, 0:K, :], wo_codes[:], wo_scales[:], E4M3)
+            group(copy, dy_grouped[:, cols, :], dy_raw[:, :, cols])
+        dy_mx = quantize(dy_grouped[:], "dy", E5M2, dy_scales_at, dy_codes_at)
+        for place in (0, 6 * KIB):
+            clear_window(nc.gpsimd, place)
 
-        dy_raw = load_matrix(dy, "dy", "raw_b")
-        dy_grouped, dy_blocks = [], []
-        dy_halves = [
-            sb.tile([P, 2 * P, PACK], BF16, name="dy_grouped", tag="raw_a", align_bytes=64)[:],
-            made[:, 0, 1, :].bitcast(BF16).rearrange("p (n j) -> p n j", j=PACK),
-        ]
-
-        def group_dy(copy, j):
-            grouped = dy_halves[j // 2][:, blocks[j % 2], :]
-            group(copy, grouped, dy_raw[:, :, blocks[j]])
-            return grouped
-
-        def quantize_dy(grouped, j):
-            codes = sb.tile([P, P], U32, name="dy_codes%d" % j, align_bytes=64)
-            scales = sb.tile([P, P], U8, name="dy_scales%d" % j, align_bytes=64)
-            quantize(grouped, codes[:], scales[:], E5M2)
-            dy_blocks.append((codes[:], scales[:]))
-
+        dr_planes = [psum.tile([P, SLOTS], F32, name="dr_plane%d" % t, tag="plane%d" % t) for t in range(last)]
+        dr_blocks = [psum.tile([P, PACK, P], F32, name="dr_block%d" % j, tag="block%d" % j) for j in range(BLOCKS)]
+        for t in range(last):
+            product(dr_planes[t][:], wo_mx, blocks[t], dy_mx, slice(0, SLOTS), True, True)
         for j in range(BLOCKS):
-            dy_grouped.append(group_dy(nc.vector.tensor_copy if j < BLOCKS // 2 else nc.scalar.copy, j))
-        nc.scalar.activation(right[:, 0, 0, :], g_bank[:], ACT.Copy, scale=-1.0)
+            for t in range(PACK):
+                product(dr_blocks[j][:, t, :], wo_mx, blocks[t], dy_mx, blocks[j], True, True)
+
+        def apart(label):
+            return [tile("%s%d" % (label, t), [SLOTS], F32)[:] for t in range(PACK)]
+
+        def together(label):
+            return tile(label, [PACK * SLOTS], F32)[:].rearrange("p (t n) -> p t n", t=PACK)
+
+        slope = apart("slope")
+        minus_dd, zg_factor, zc_factor = together("minus_dd"), together("zg_factor"), together("zc_factor")
+
+        def scatter_dd(t, slots):
+            nc.scalar.activation(windows[t][:].indirect(listed(slots)), minus_dd[:, t, slots], ACT.Copy, scale=-1.0)
+
+        def form_dd(t):
+            g = picked["g%d" % t]
+            if t < last:
+                nc.vector.scalar_tensor_tensor(minus_dd[:, t, :], g, 1.0, dr_planes[t][:], ALU.subtract, ALU.mult)
+            else:
+                for j in range(BLOCKS):
+                    nc.vector.scalar_tensor_tensor(
+                        minus_dd[:, t, blocks[j]], g[:, blocks[j]], 1.0, dr_blocks[j][:, t, :], ALU.subtract, ALU.mult
+                    )
+
+        def form_slope(t):
+            c_squared = tile("c_squared%d" % t, [SLOTS], F32, 10 * KIB if t == last else None)
+            nc.scalar.activation(c_squared[:], picked["c%d" % t], ACT.Square)
+            nc.scalar.activation(slope[t], c_squared[:], ACT.Copy, bias=1.0, scale=-1.0)
+
+        def form_factors(t):
+            g, c, x = (picked["%s%d" % (letter, t)] for letter in ("g", "c", "x"))
+            x_less_c = tile("x_less_c%d" % t, [SLOTS], F32, 17 * KIB if t == last else None)
+            if t == last:
+                nc.gpsimd.tensor_tensor(zc_factor[:, t, :], g, slope[t], ALU.mult)
+            nc.gpsimd.tensor_tensor(x_less_c[:], x, c, ALU.subtract)
+            if t < last:
+                nc.gpsimd.tensor_tensor(zc_factor[:, t, :], g, slope[t], ALU.mult)
+            nc.gpsimd.tensor_tensor(zg_factor[:, t, :], g, x_less_c[:], ALU.mult)
+
+        picked = {}
+
+        def bring(label, gather=gather_on_vector):
+            picked[label] = tile(label, [SLOTS], F32, picked_place.get(label))[:]
+            gather(picked[label], load_plane(label))
+
+        bring("g0", gather_on_scalar)
+        bring("c0", gather_on_scalar)
+        form_dd(0)
+        form_slope(0)
+        bring("x0")
+        form_factors(0)
+        scatter_dd(0, halves[0])
+        scatter_dd(0, halves[1])
+        bring("c1")
+        form_slope(1)
+        bring("g1")
+        bring("x1")
+        form_dd(1)
+        form_factors(1)
+        scatter_dd(1, halves[0])
+        for t in (2, 3):
+            bring("c%d" % t)
+            form_slope(t)
+        scatter_dd(1, halves[1])
+        bring("x2")
+        bring("g2")
+        bring("g3")
+        form_dd(2)
+        form_factors(2)
+        bring("x3")
+        form_dd(3)
+        form_factors(3)
+        waiting = [(t, slots) for t in (2, 3) for slots in halves]
+
+        wc_raw = load_matrix(wc, "wc", ring[4])
+        wg_raw = load_matrix(wg, "wg", ring[0])
+        zc_grouped = tile("zc_grouped", [SLOTS, PACK], BF16)
         for j in range(BLOCKS):
-            quantize_dy(dy_grouped[j], j)
-        nc.gpsimd.tensor_tensor(made[:, 0, 1, :], left[:, 0, 1, :], right[:, 0, 1, :], ALU.mult)
-        dr_banks = []
-        for j, (codes, scales) in enumerate(dy_blocks):
-            bank = psum.tile([P, K], F32, name="dr_bank%d" % j, tag="bank_wide%d" % j)
-            nc.tensor.matmul_mx(
-                out=bank[:], lhsT=codes.bitcast(E5M2), lhsT_scale=scales,
-                rhs=wo_codes[:].bitcast(E4M3), rhs_scale=wo_scales[:], start=True, stop=True,
+            nc.vector.tensor_tensor(
+                woven(zc_grouped[:, blocks[j], :]), by_pairs(zc_factor[:, :, blocks[j]]), by_pairs(dr_blocks[j][:]), ALU.mult
             )
-            nc.scalar.copy(out=left[:, :, 0, blocks[j]], in_=bank[:, 0 : 2 * P].rearrange("p (a d) -> p a d", d=P))
-            dr_banks.append(bank)
-        for cols in (slice(0, 2 * P), slice(2 * P, SLOTS)):
-            nc.gpsimd.tensor_tensor(made[:, 0, 0, cols], left[:, 0, 0, cols], right[:, 0, 0, cols], ALU.mult)
-        form_z(0, made[:, 0, 1:3, :])
+        scatter_dd(*waiting.pop(0))
+        wc_grouped = tile("wc_grouped", [K, PACK], BF16, 10 * KIB)
+        group(nc.scalar.copy, wc_grouped[:], wc_raw[:])
+        zg_grouped = tile("zg_grouped", [SLOTS, PACK], BF16)
+        nc.vector.tensor_tensor(woven(zg_grouped[:]), by_pairs(zg_factor[:]), by_pairs(minus_dd[:]), ALU.mult)
+        zc_mx = quantize(zc_grouped[:], "zc", E5M2, 18 * KIB)
+        wg_grouped = tile("wg_grouped", [K, PACK], BF16, 14 * KIB)
+        group(nc.vector.tensor_copy, wg_grouped[:], wg_raw[:])
+        wc_mx = quantize(wc_grouped[:], "wc", E4M3, 18 * KIB + 512)
+        zg_mx = quantize(zg_grouped[:], "zg", E5M2)
+        wg_mx = quantize(wg_grouped[:], "wg", E4M3)
+        for part in waiting:
+            scatter_dd(*part)
+        for t in range(PACK):
+            nc.sync.dma_start(by_plane(out_1)[:, t, :], windows[t][:])
 
-        def turn_dd(a, tag):
-            bank = turned(left_of(a)[:, 0, :], "dd_bank%d" % a, tag, stop=False)
-            turn(bank, made[:, a, 0, :], False, True)
-            return bank
-
-        second = sb.tile([P, 3, SLOTS], F32, name="second_picked", tag="raw_b", align_bytes=64)
-        bring_g(1, second[:, 0, :])
-        c_middle = rows_tile("c_rows_middle", 2)
-        load_plane(c_middle[:, TOKENS:], cT, 1)
-        c = gather(second[:, 1, :], c_middle[:, TOKENS:])
-        square_c(1, c, c_sq[:, 0, :], made[:, 1, 2, :])
-        e_bank = turned(c, "e_bank1", "bank_dd", stop=False)
-        load_plane(x_low[:, 0:TOKENS], xT, 1)
-        turn(e_bank, gather_negated(second[:, 2, :], x_low[:]), False, True)
-        nc.scalar.activation(right[:, 1, 1, :], e_bank[:], ACT.Copy, scale=-1.0)
-        lefts.append(sb.tile([P, 2, 2, SLOTS], F32, name="left_high", tag="raw_b", align_bytes=64))
-        for j, bank in enumerate(dr_banks):
-            nc.scalar.copy(out=lefts[1][:, :, 0, blocks[j]], in_=bank[:, 2 * P :].rearrange("p (a d) -> p a d", d=P))
-
-        def form_u_h(a):
-            nc.gpsimd.tensor_tensor(made[:, a, 0:2, :], left_of(a), right[:, a, :, :], ALU.mult)
-
-        form_u_h(1)
-        form_z(1, made[:, 1, 1:3, :])
-
-        bring_g(2, picked_tile("g_picked2"))
-        load_plane(c_middle[:, 0:TOKENS], cT, 2)
-        c = gather_negated(picked_tile("c_picked2"), c_middle[:])
-        e_bank = turned(c, "e_bank2", "bank_e", stop=False)
-        x_rows = rows_tile("x_rows2", 1)
-        load_plane(x_rows[:], xT, 2)
-        turn(e_bank, gather(picked_tile("x_picked2"), x_rows[:]), False, True)
-        nc.scalar.copy(out=right[:, 2, 1, :], in_=e_bank[:])
-        square_c(2, c, c_sq[:, 1, :], made[:, 2, 2, :])
-        form_u_h(2)
-        form_z(2, made[:, 2, 1:3, :])
-
-        def scatter_dd(a, bank, dd):
-            nc.scalar.copy(out=dd, in_=bank[:])
-            return dd
-
-        def store_dd(a, dd):
-            nc.vector.tensor_copy(windows[a][:].indirect(offsets[:]), dd)
-            nc.sync.dma_start(out_1[blocks[a], :], windows[a][:])
-
-        dd0 = scatter_dd(0, turn_dd(0, "bank_dd"), picked_tile("x_picked2"))
-        bring_g(3, picked_tile("g_picked3"))
-        c_rows = rows_tile("c_rows3", 1)
-        load_plane(c_rows[:], cT, 3)
-        w_grouped = sb.tile([P, 2 * K, PACK], BF16, name="w_grouped", align_bytes=64)
-        w_words = w_grouped[:].rearrange("p n j -> p (n j)").bitcast(F32)
-        c = gather(picked_tile("c_picked3"), c_rows[:])
-        c_sq_last = w_words[:, 3 * SLOTS :]
-        square_c(last, c, c_sq_last, None)
-        e_bank = turned(c, "e_bank3", "bank_wide0", stop=False)
-        x_rows = rows_tile("x_rows3", 1)
-        load_plane(x_rows[:], xT, 3)
-        nc.scalar.activation(w_words[:, 0:SLOTS], gather(picked_tile("x_picked3"), x_rows[:]), ACT.Copy, scale=-1.0)
-        turn(e_bank, w_words[:, 0:SLOTS], False, True)
-        wc_raw = load_matrix(wc, "wc", "raw_a")
-        wg_raw = late.tile([P, PACK, K], F32, name="wg_raw", align_bytes=64, offset=4 * SLOTS)
-        nc.sync.dma_start(wg_raw[:], wg.rearrange("(p j) n -> p j n", j=PACK))
-        store_dd(0, dd0)
-
-        def form_z_last(kind, factor, within):
-            nc.gpsimd.tensor_tensor(
-                z_turned[:, kind, within, blocks[last]],
-                by_block(made[:, last, :, :])[:, 0, within, :], by_block(factor)[:, 0, within, :], ALU.mult,
-            )
-
-        nc.scalar.activation(right[:, last, 1, :], e_bank[:], ACT.Copy, scale=-1.0)
-        store_dd(1, scatter_dd(1, turn_dd(1, "bank_dd"), picked_tile("dd1")))
-        form_u_h(last)
-        form_z_last(0, made[:, last, 1:2, :], slice(0, BLOCKS))
-        group(nc.scalar.copy, w_grouped[:, 0:K, :], wc_raw[:])
-        behind_wc = sb.tile([P, 2, SLOTS], F32, name="behind_wc", tag="raw_a", align_bytes=64)
-        store_dd(2, scatter_dd(2, turn_dd(2, "bank_wide0"), behind_wc[:, 0, :]))
-        last_bank = turn_dd(last, "bank_e")
-        csq_less_one_last = left_of(2)[:, 0:1, :]
-        nc.scalar.activation(csq_less_one_last[:, 0, :], c_sq_last, ACT.Copy, bias=-1.0)
-        z_parts = ((slice(0, 2), slice(2, 4)), (slice(0, 2), slice(2, 3), slice(3, 4)))
-        for within in z_parts[1]:
-            form_z_last(1, csq_less_one_last, within)
-        early = SLOTS - LATE_SLOTS
-        group(nc.scalar.copy, w_grouped[:, K : 2 * K - WG_TAIL, :], wg_raw[:, :, 0 : K - WG_TAIL])
-        dd_early = behind_wc[:, 1, 0:early]
-        nc.scalar.copy(out=dd_early, in_=last_bank[:, 0:early])
-        nc.vector.tensor_copy(windows[last][:].indirect(offsets[:, 0 : early // 16]), dd_early)
-        group(nc.scalar.copy, w_grouped[:, 2 * K - WG_TAIL :, :], wg_raw[:, :, K - WG_TAIL :])
-        late_codes = sb.tile([P, 4 * K], U32, name="late_codes", tag="made_then_codes", align_bytes=64)
-        w_codes = late_codes[:, 0 : 2 * K]
-        w_scales = sb.tile([P, 2 * K], U8, name="w_scales", align_bytes=64)[:]
-        quantize(w_grouped[:], w_codes, w_scales, E4M3)
-
-        words = z_turned[:].rearrange("p z j d -> p (z j d)").bitcast(F32)
-        z_packed = {}
-        z_banks = ({0: "bank_wide1", 2: "bank_wide2"}, {0: "bank_wide3", 2: "bank_c", 3: "bank_g"})
-        for kind in range(2):
-            flat_words = late.tile([P, 2 * SLOTS], F32, name="z_grouped%d" % kind, align_bytes=64, offset=8 * SLOTS * kind)[:]
-            grouped_words = flat_words.rearrange("p (n u) -> p n u", u=2)
-            for within in z_parts[kind]:
-                count = within.stop - within.start
-                bank = psum.tile([P, 2, count * P], F32, name="z_bank%d%d" % (kind, within.start), tag=z_banks[kind][within.start])
-                for inner in range(count):
-                    base = (kind * BLOCKS + within.start + inner) * (K // 2)
-                    for u in range(2):
-                        nc.tensor.transpose(bank[:, u, blocks[inner]], words[:, base + u : base + K // 2 : 2], identity[:])
-                nc.scalar.copy(out=grouped_words[:, P * within.start : P * within.stop, :], in_=bank[:].rearrange("p u n -> p n u"))
-            codes = late_codes[:, (2 + kind) * K : (3 + kind) * K]
-            scales = sb.tile([P, SLOTS], U8, name="z_scales%d" % kind, align_bytes=64)
-            quantize(flat_words.bitcast(BF16).rearrange("p (n j) -> p n j", j=PACK), codes, scales[:], E5M2)
-            z_packed[kind] = (codes, scales[:])
-
-        s_banks = []
-        for r, tag in enumerate(("bank_dd", "bank_wide0", "bank_wide1", "bank_wide2")):
+        s = apart("s")
+        for r, tag in enumerate(("spare", "plane0", "plane1", "plane2")):
             bank = psum.tile([P, SLOTS], F32, name="s_bank%d" % r, tag=tag)
-            for number, kind in enumerate((0, 1) if r == 0 else (1, 0)):
-                cols = slice((1 - kind) * K + r * P, (1 - kind) * K + (r + 1) * P)
-                nc.tensor.matmul_mx(
-                    out=bank[:], lhsT=w_codes[:, cols].bitcast(E4M3), lhsT_scale=w_scales[:, cols],
-                    rhs=z_packed[kind][0].bitcast(E5M2), rhs_scale=z_packed[kind][1],
-                    start=number == 0, stop=number == 1,
-                )
-            s_banks.append(bank)
-
-        dd_late = late.tile([P, LATE_SLOTS], F32, name="dd_late", align_bytes=64, offset=19 * SLOTS)
-        nc.scalar.copy(out=dd_late[:], in_=last_bank[:, early:])
-        nc.vector.tensor_copy(windows[last][:].indirect(offsets[:, early // 16 :]), dd_late[:])
-        nc.gpsimd.dma_start(out_1[blocks[last], :], windows[last][:])
-        for r in range(PLANES):
-            s = sb.tile([P, SLOTS], F32, name="s%d" % r)
-            nc.scalar.copy(out=s[:], in_=s_banks[r][:])
-            window = windows[(PLANES + r) % WINDOWS]
-            nc.vector.tensor_copy(window[:].indirect(offsets[:]), s[:])
+            product(bank[:], wc_mx, blocks[r], zc_mx, slice(0, SLOTS), True, False)
+            product(bank[:], wg_mx, blocks[r], zg_mx, slice(0, SLOTS), False, True)
+            window = windows[(PACK + r) % WINDOWS]
+            if r % 2 == 0:
+                nc.scalar.copy(out=s[r], in_=bank[:])
+                nc.vector.tensor_copy(window[:].indirect(offsets[:]), s[r])
+            else:
+                nc.vector.tensor_copy(s[r], bank[:])
+                for slots in halves:
+                    nc.scalar.activation(window[:].indirect(listed(slots)), s[r][:, slots], ACT.Copy)
             nc.sync.dma_start(out_0[blocks[r], :], window[:])

@@ -50,8 +50,8 @@ def tile_attend_ghighw_kernel(tc, dy, wo, gT, cT, xT, wg, wc, offs, out_0, out_1
             nc.sync.dma_start(raw[:], by_plane(matrix))
             return raw
 
-        def load_plane(label):
-            rows = tile(label + "_rows", [TOKENS], F32, rows_place.get(label))
+        def load_plane(label, place=None):
+            rows = tile(label + "_rows", [TOKENS], F32, place)
             nc.sync.dma_start(rows[:], by_plane({"g": gT, "c": cT, "x": xT}[label[0]])[:, int(label[1]), :])
             return rows
 
@@ -86,29 +86,15 @@ def tile_attend_ghighw_kernel(tc, dy, wo, gT, cT, xT, wg, wc, offs, out_0, out_1
         def woven(grouped):
             return grouped.rearrange("p (c i) t -> p c t i", i=2)
 
-        dy_raw_at, dy_grouped_at = 20 * KIB, 4 * KIB - EDGE
-        wo_codes_at, dy_codes_at, dy_scales_at = 30 * KIB, 36 * KIB, 42 * KIB
-        picked_place = {
-            "g0": dy_raw_at, "c0": dy_raw_at + 2 * KIB, "x0": 4 * KIB,
-            "c1": wo_codes_at - 2 * KIB + EDGE, "g1": wo_codes_at + 2 * KIB - EDGE,
-            "x1": dy_codes_at - 2 * KIB + EDGE, "c2": dy_codes_at + 2 * KIB - EDGE, "c3": dy_scales_at,
-        }
-        ring = [44 * KIB + 8 * KIB * n for n in range(6)]
-        rows_place = dict(zip(("c1", "g1", "x1", "c2", "c3", "x2"), ring))
-        rows_place.update({"g2": ring[1], "g3": ring[2], "x3": ring[3]})
-        rows_place["x2"] = ring[0]
+        x_last_at, square_last_at, x_less_c_at = 0, 6 * KIB, 10 * KIB
         windows = []
-
-        def clear_window(engine, place=None):
-            window = tile("window%d" % len(windows), [TOKENS], F32, place)
+        for engine in (nc.vector, nc.gpsimd) * (WINDOWS // 2):
+            window = tile("window%d" % len(windows), [TOKENS], F32)
             engine.memset(window[:].bitcast(I32), 0)
             windows.append(window)
 
-        for engine in (nc.vector, nc.gpsimd, nc.vector, nc.gpsimd):
-            clear_window(engine)
-
         wo_raw = load_matrix(wo, "wo", None)
-        dy_raw = load_matrix(dy, "dy", dy_raw_at)
+        dy_raw = load_matrix(dy, "dy", None)
         offsets = lists.tile([P, SLOTS // 16], U16, name="offsets")
         nc.sync.dma_start(offsets[:], offs)
 
@@ -118,128 +104,136 @@ def tile_attend_ghighw_kernel(tc, dy, wo, gT, cT, xT, wg, wc, offs, out_0, out_1
         cut = VECTOR_SHARE // PACK
         nc.vector.tensor_copy(out=dealt[:, 0:cut], in_=source[:, 0:cut])
         nc.scalar.copy(out=dealt[:, cut:], in_=source[:, cut:])
-        wo_mx = quantize(wo_grouped[:], "wo", E4M3, None, wo_codes_at)
-        dy_grouped = tile("dy_grouped", [SLOTS, PACK], BF16, dy_grouped_at)
+        wo_mx = quantize(wo_grouped[:], "wo", E4M3)
+        dy_grouped = tile("dy_grouped", [SLOTS, PACK], BF16)
         for copy, cols in ((nc.vector.tensor_copy, slice(0, VECTOR_SHARE)), (nc.scalar.copy, slice(VECTOR_SHARE, K))):
             group(copy, dy_grouped[:, cols, :], dy_raw[:, :, cols])
-        dy_mx = quantize(dy_grouped[:], "dy", E5M2, dy_scales_at, dy_codes_at)
-        for place in (0, 6 * KIB):
-            clear_window(nc.gpsimd, place)
+        dy_mx = quantize(dy_grouped[:], "dy", E5M2)
 
-        dr_planes = [psum.tile([P, SLOTS], F32, name="dr_plane%d" % t, tag="plane%d" % t) for t in range(last)]
+        whole = slice(0, SLOTS)
+        dr_planes = [psum.tile([P, SLOTS], F32, name="dr_plane%d" % t, tag="plane%d" % t) for t in range(PACK)]
         dr_blocks = [psum.tile([P, PACK, P], F32, name="dr_block%d" % j, tag="block%d" % j) for j in range(BLOCKS)]
-        for t in range(last):
-            product(dr_planes[t][:], wo_mx, blocks[t], dy_mx, slice(0, SLOTS), True, True)
+        early = slice(0, last * P)
+        for t in range(PACK):
+            for slots in (halves[0], blocks[2]):
+                product(dr_planes[t][:, slots], wo_mx, blocks[t], dy_mx, slots, True, True)
         for j in range(BLOCKS):
             for t in range(PACK):
                 product(dr_blocks[j][:, t, :], wo_mx, blocks[t], dy_mx, blocks[j], True, True)
 
-        def apart(label):
-            return [tile("%s%d" % (label, t), [SLOTS], F32)[:] for t in range(PACK)]
+        def together(label, width=SLOTS, place=None):
+            return tile(label, [PACK * width], F32, place)[:].rearrange("p (t n) -> p t n", t=PACK)
 
-        def together(label):
-            return tile(label, [PACK * SLOTS], F32)[:].rearrange("p (t n) -> p t n", t=PACK)
+        gates, zg_factor, zc_factor = together("gates"), together("zg_factor"), together("zc_factor")
+        minus_dd = together("minus_dd", last * P)
 
-        slope = apart("slope")
-        minus_dd, zg_factor, zc_factor = together("minus_dd"), together("zg_factor"), together("zc_factor")
+        def load_weights(h):
+            raws = []
+            for label, matrix in (("wc", wc), ("wg", wg)):
+                raw = tile("%s_raw%d" % (label, h), [PACK, K // 2], F32)
+                nc.sync.dma_start(raw[:], by_plane(matrix)[:, :, halves[h]])
+                raws.append(raw)
+            return raws
 
-        def scatter_dd(t, slots):
-            nc.scalar.activation(windows[t][:].indirect(listed(slots)), minus_dd[:, t, slots], ACT.Copy, scale=-1.0)
+        def bring(label, gather=gather_on_vector, place=None):
+            picked = tile(label, [SLOTS], F32)[:]
+            gather(picked, load_plane(label, place))
+            return picked
 
-        def form_dd(t):
-            g = picked["g%d" % t]
-            if t < last:
-                nc.vector.scalar_tensor_tensor(minus_dd[:, t, :], g, 1.0, dr_planes[t][:], ALU.subtract, ALU.mult)
-            else:
-                for j in range(BLOCKS):
-                    nc.vector.scalar_tensor_tensor(
-                        minus_dd[:, t, blocks[j]], g[:, blocks[j]], 1.0, dr_blocks[j][:, t, :], ALU.subtract, ALU.mult
-                    )
-
-        def form_slope(t):
-            c_squared = tile("c_squared%d" % t, [SLOTS], F32, 10 * KIB if t == last else None)
-            nc.scalar.activation(c_squared[:], picked["c%d" % t], ACT.Square)
-            nc.scalar.activation(slope[t], c_squared[:], ACT.Copy, bias=1.0, scale=-1.0)
-
-        def form_factors(t):
-            g, c, x = (picked["%s%d" % (letter, t)] for letter in ("g", "c", "x"))
-            x_less_c = tile("x_less_c%d" % t, [SLOTS], F32, 17 * KIB if t == last else None)
+        for t in range(PACK):
             if t == last:
-                nc.gpsimd.tensor_tensor(zc_factor[:, t, :], g, slope[t], ALU.mult)
+                w_low_raw = load_weights(0)
+            c = bring("c%d" % t, gather_on_scalar if t == 0 else gather_on_vector)
+            square = tile("c_squared%d" % t, [SLOTS], F32, square_last_at if t == last else None)
+            slope = tile("slope%d" % t, [SLOTS], F32)
+            nc.scalar.activation(square[:], c, ACT.Square)
+            nc.scalar.activation(slope[:], square[:], ACT.Copy, bias=1.0, scale=-1.0)
+            g = gates[:, t, :]
+            gather_on_vector(g, load_plane("g%d" % t))
+            nc.gpsimd.tensor_tensor(zc_factor[:, t, :], g, slope[:], ALU.mult)
+            nc.vector.scalar_tensor_tensor(minus_dd[:, t, :], g[:, early], 1.0, dr_planes[t][:, early], ALU.subtract, ALU.mult)
+            if t == last:
+                w_low = tile("w_low", [K, PACK], BF16, square_last_at)
+                for pair in range(2):
+                    group(nc.scalar.copy, w_low[:, halves[pair], :], w_low_raw[pair][:])
+            nc.scalar.activation(windows[t][:].indirect(listed(early)), minus_dd[:, t, :], ACT.Copy, scale=-1.0)
+            x = bring("x%d" % t, gather_on_vector, x_last_at if t == last else None)
+            x_less_c = tile("x_less_c%d" % t, [SLOTS], F32, x_less_c_at if t == last else None)
             nc.gpsimd.tensor_tensor(x_less_c[:], x, c, ALU.subtract)
-            if t < last:
-                nc.gpsimd.tensor_tensor(zc_factor[:, t, :], g, slope[t], ALU.mult)
             nc.gpsimd.tensor_tensor(zg_factor[:, t, :], g, x_less_c[:], ALU.mult)
 
-        picked = {}
-
-        def bring(label, gather=gather_on_vector):
-            picked[label] = tile(label, [SLOTS], F32, picked_place.get(label))[:]
-            gather(picked[label], load_plane(label))
-
-        bring("g0", gather_on_scalar)
-        bring("c0", gather_on_scalar)
-        form_dd(0)
-        form_slope(0)
-        bring("x0")
-        form_factors(0)
-        scatter_dd(0, halves[0])
-        scatter_dd(0, halves[1])
-        bring("c1")
-        form_slope(1)
-        bring("g1")
-        bring("x1")
-        form_dd(1)
-        form_factors(1)
-        scatter_dd(1, halves[0])
-        for t in (2, 3):
-            bring("c%d" % t)
-            form_slope(t)
-        scatter_dd(1, halves[1])
-        bring("x2")
-        bring("g2")
-        bring("g3")
-        form_dd(2)
-        form_factors(2)
-        bring("x3")
-        form_dd(3)
-        form_factors(3)
-        waiting = [(t, slots) for t in (2, 3) for slots in halves]
-
-        wc_raw = load_matrix(wc, "wc", ring[4])
-        wg_raw = load_matrix(wg, "wg", ring[0])
-        zc_grouped = tile("zc_grouped", [SLOTS, PACK], BF16)
+        w_high_raw = load_weights(1)
+        minus_dd_late = together("minus_dd_late", P, x_last_at)
+        nc.vector.scalar_tensor_tensor(minus_dd_late, gates[:, :, blocks[last]], 1.0, dr_blocks[last][:], ALU.subtract, ALU.mult)
+        for t in range(PACK):
+            nc.scalar.activation(windows[t][:].indirect(listed(blocks[last])), minus_dd_late[:, t, :], ACT.Copy, scale=-1.0)
+            nc.sync.dma_start(by_plane(out_1)[:, t, :], windows[t][:])
+        zc_grouped = tile("zc_grouped", [SLOTS, PACK], BF16, x_last_at + 2 * KIB)
         for j in range(BLOCKS):
             nc.vector.tensor_tensor(
                 woven(zc_grouped[:, blocks[j], :]), by_pairs(zc_factor[:, :, blocks[j]]), by_pairs(dr_blocks[j][:]), ALU.mult
             )
-        scatter_dd(*waiting.pop(0))
-        wc_grouped = tile("wc_grouped", [K, PACK], BF16, 10 * KIB)
-        group(nc.scalar.copy, wc_grouped[:], wc_raw[:])
-        zg_grouped = tile("zg_grouped", [SLOTS, PACK], BF16)
-        nc.vector.tensor_tensor(woven(zg_grouped[:]), by_pairs(zg_factor[:]), by_pairs(minus_dd[:]), ALU.mult)
-        zc_mx = quantize(zc_grouped[:], "zc", E5M2, 18 * KIB)
-        wg_grouped = tile("wg_grouped", [K, PACK], BF16, 14 * KIB)
-        group(nc.vector.tensor_copy, wg_grouped[:], wg_raw[:])
-        wc_mx = quantize(wc_grouped[:], "wc", E4M3, 18 * KIB + 512)
-        zg_mx = quantize(zg_grouped[:], "zg", E5M2)
-        wg_mx = quantize(wg_grouped[:], "wg", E4M3)
-        for part in waiting:
-            scatter_dd(*part)
-        for t in range(PACK):
-            nc.sync.dma_start(by_plane(out_1)[:, t, :], windows[t][:])
 
-        s = apart("s")
-        for r, tag in enumerate(("spare", "plane0", "plane1", "plane2")):
-            bank = psum.tile([P, SLOTS], F32, name="s_bank%d" % r, tag=tag)
-            product(bank[:], wc_mx, blocks[r], zc_mx, slice(0, SLOTS), True, False)
-            product(bank[:], wg_mx, blocks[r], zg_mx, slice(0, SLOTS), False, True)
-            window = windows[(PACK + r) % WINDOWS]
-            if r % 2 == 0:
-                nc.scalar.copy(out=s[r], in_=bank[:])
-                nc.vector.tensor_copy(window[:].indirect(offsets[:]), s[r])
+        def form_zg(h):
+            zg_grouped = tile("zg_grouped%d" % h, [SLOTS // 2, PACK], BF16)
+            if h == 0:
+                parts = [(halves[0], halves[0], minus_dd[:, :, halves[0]])]
             else:
-                nc.vector.tensor_copy(s[r], bank[:])
-                for slots in halves:
-                    nc.scalar.activation(window[:].indirect(listed(slots)), s[r][:, slots], ACT.Copy)
-            nc.sync.dma_start(out_0[blocks[r], :], window[:])
+                parts = [(blocks[0], blocks[2], minus_dd[:, :, blocks[2]]), (blocks[1], blocks[last], minus_dd_late)]
+            for place, slots, values in parts:
+                nc.vector.tensor_tensor(woven(zg_grouped[:, place, :]), by_pairs(zg_factor[:, :, slots]), by_pairs(values), ALU.mult)
+            return zg_grouped
+
+        def quantize_zc(h):
+            return quantize(zc_grouped[:, halves[h], :], "zc%d" % h, E5M2, x_less_c_at + h * SLOTS // 2)
+
+        def second_product(tag, rows, w_mx, zc_mx, zg_mx):
+            bank = psum.tile([P, len(rows), SLOTS // 2], F32, name="s_" + tag, tag=tag)
+            for place, r in enumerate(rows):
+                product(bank[:, place, :], w_mx, blocks[r], zc_mx, halves[0], True, False)
+                product(bank[:, place, :], w_mx, blocks[2 + r], zg_mx, halves[0], False, True)
+            return bank
+
+        zg_low = form_zg(0)
+        zc_low = quantize_zc(0)
+        w_low = quantize(w_low[:], "w0", E4M3, x_less_c_at + SLOTS)
+        zg_low = quantize(zg_low[:], "zg0", E5M2)
+        first = [second_product("plane%d" % r, [r], w_low, zc_low, zg_low) for r in range(2)]
+        w_high = tile("w_high", [K, PACK], BF16, x_less_c_at + 2 * SLOTS)
+        for pair in range(2):
+            group(nc.vector.tensor_copy, w_high[:, halves[pair], :], w_high_raw[pair][:])
+        zg_high = form_zg(1)
+        w_high = quantize(w_high[:], "w1", E4M3)
+        high_low = second_product("plane2", [0, 1], w_high, zc_low, zg_low)
+        zc_high = quantize_zc(1)
+        zg_high = quantize(zg_high[:], "zg1", E5M2)
+        low_high = second_product("plane3", [0, 1], w_low, zc_high, zg_high)
+        high_high = second_product("block0", [0, 1], w_high, zc_high, zg_high)
+
+        s = [tile("s%d" % pair, [2 * SLOTS], F32)[:].rearrange("p (r n) -> p r n", r=2) for pair in range(2)]
+        s_windows = [windows[n] for n in (4, 5, 1, 0)]
+
+        def scatter_on_scalar(r, slots):
+            nc.scalar.activation(s_windows[r][:].indirect(listed(slots)), s[r // 2][:, r % 2, slots], ACT.Copy)
+
+        def scatter_on_vector(r, slots):
+            nc.vector.tensor_copy(s_windows[r][:].indirect(listed(slots)), s[r // 2][:, r % 2, slots])
+
+        def store(r):
+            nc.sync.dma_start(out_0[blocks[r], :], s_windows[r][:])
+
+        for r in range(2):
+            nc.scalar.copy(out=s[0][:, r, halves[0]], in_=first[r][:, 0, :])
+            scatter_on_scalar(r, halves[0])
+        nc.vector.tensor_copy(s[1][:, :, halves[0]], high_low[:])
+        scatter_on_vector(3, halves[0])
+        nc.vector.tensor_copy(s[1][:, :, halves[1]], high_high[:])
+        nc.scalar.copy(out=s[0][:, :, halves[1]], in_=low_high[:])
+        scatter_on_scalar(0, halves[1])
+        store(0)
+        scatter_on_scalar(1, halves[1])
+        store(1)
+        scatter_on_vector(2, whole)
+        store(2)
+        scatter_on_scalar(3, halves[1])
+        store(3)

@@ -19,7 +19,7 @@ K = 512
 SLOTS = 512
 TOKENS = 1024
 BLOCKS = SLOTS // P
-WINDOWS = 6
+SCALAR_SHARE = 192
 VECTOR_SHARE = 352
 KIB = 1024
 EDGE = 64
@@ -74,11 +74,11 @@ def tile_attend_ghighw_kernel(tc, dy, wo, gT, cT, xT, wg, wc, offs, out_0, out_1
         def listed(slots):
             return offsets[:, slots.start // 16 : slots.stop // 16]
 
-        def gather_on_vector(picked, rows):
-            nc.vector.tensor_copy(picked, rows[:].indirect(offsets[:]))
+        def gather_on_vector(picked, rows, slots):
+            nc.vector.tensor_copy(picked[:, slots], rows[:].indirect(listed(slots)))
 
-        def gather_on_scalar(picked, rows):
-            nc.scalar.activation(picked, rows[:].indirect(offsets[:]), ACT.Copy)
+        def gather_on_scalar(picked, rows, slots):
+            nc.scalar.activation(picked[:, slots], rows[:].indirect(listed(slots)), ACT.Copy)
 
         def by_pairs(planes):
             return planes.rearrange("p t (c i) -> p c t i", i=2)
@@ -88,9 +88,9 @@ def tile_attend_ghighw_kernel(tc, dy, wo, gT, cT, xT, wg, wc, offs, out_0, out_1
 
         x_last_at, square_last_at, x_less_c_at = 0, 6 * KIB, 10 * KIB
         windows = []
-        for engine in (nc.vector, nc.gpsimd) * (WINDOWS // 2):
+        for engine in (nc.vector, nc.gpsimd) * 3:
             window = tile("window%d" % len(windows), [TOKENS], F32)
-            engine.memset(window[:].bitcast(I32), 0)
+            engine.memset(window[:], 0.0)
             windows.append(window)
 
         wo_raw = load_matrix(wo, "wo", None)
@@ -113,7 +113,7 @@ def tile_attend_ghighw_kernel(tc, dy, wo, gT, cT, xT, wg, wc, offs, out_0, out_1
         whole = slice(0, SLOTS)
         dr_planes = [psum.tile([P, SLOTS], F32, name="dr_plane%d" % t, tag="plane%d" % t) for t in range(PACK)]
         dr_blocks = [psum.tile([P, PACK, P], F32, name="dr_block%d" % j, tag="block%d" % j) for j in range(BLOCKS)]
-        early = slice(0, last * P)
+        early, late = slice(0, last * P), blocks[last]
         for t in range(PACK):
             for slots in (halves[0], blocks[2]):
                 product(dr_planes[t][:, slots], wo_mx, blocks[t], dy_mx, slots, True, True)
@@ -135,21 +135,22 @@ def tile_attend_ghighw_kernel(tc, dy, wo, gT, cT, xT, wg, wc, offs, out_0, out_1
                 raws.append(raw)
             return raws
 
-        def bring(label, gather=gather_on_vector, place=None):
-            picked = tile(label, [SLOTS], F32)[:]
-            gather(picked, load_plane(label, place))
-            return picked
-
         for t in range(PACK):
             if t == last:
                 w_low_raw = load_weights(0)
-            c = bring("c%d" % t, gather_on_scalar if t == 0 else gather_on_vector)
+            c = tile("c%d" % t, [SLOTS], F32)[:]
+            rows = load_plane("c%d" % t)
+            (gather_on_scalar if t == 0 else gather_on_vector)(c, rows, whole)
             square = tile("c_squared%d" % t, [SLOTS], F32, square_last_at if t == last else None)
             slope = tile("slope%d" % t, [SLOTS], F32)
-            nc.scalar.activation(square[:], c, ACT.Square)
-            nc.scalar.activation(slope[:], square[:], ACT.Copy, bias=1.0, scale=-1.0)
+            for slots in halves:
+                nc.scalar.activation(square[:, slots], c[:, slots], ACT.Square)
+            for slots in halves:
+                nc.scalar.activation(slope[:, slots], square[:, slots], ACT.Copy, bias=1.0, scale=-1.0)
             g = gates[:, t, :]
-            gather_on_vector(g, load_plane("g%d" % t))
+            rows = load_plane("g%d" % t)
+            for slots in (early, late):
+                gather_on_vector(g, rows, slots)
             nc.gpsimd.tensor_tensor(zc_factor[:, t, :], g, slope[:], ALU.mult)
             nc.vector.scalar_tensor_tensor(minus_dd[:, t, :], g[:, early], 1.0, dr_planes[t][:, early], ALU.subtract, ALU.mult)
             if t == last:
@@ -157,32 +158,27 @@ def tile_attend_ghighw_kernel(tc, dy, wo, gT, cT, xT, wg, wc, offs, out_0, out_1
                 for pair in range(2):
                     group(nc.scalar.copy, w_low[:, halves[pair], :], w_low_raw[pair][:])
             nc.scalar.activation(windows[t][:].indirect(listed(early)), minus_dd[:, t, :], ACT.Copy, scale=-1.0)
-            x = bring("x%d" % t, gather_on_vector, x_last_at if t == last else None)
+            x = tile("x%d" % t, [SLOTS], F32)[:]
+            rows = load_plane("x%d" % t, x_last_at if t == last else None)
+            gather_on_vector(x, rows, whole)
             x_less_c = tile("x_less_c%d" % t, [SLOTS], F32, x_less_c_at if t == last else None)
             nc.gpsimd.tensor_tensor(x_less_c[:], x, c, ALU.subtract)
             nc.gpsimd.tensor_tensor(zg_factor[:, t, :], g, x_less_c[:], ALU.mult)
 
         w_high_raw = load_weights(1)
-        minus_dd_late = together("minus_dd_late", P, x_last_at)
+        minus_dd_late = together("minus_dd_late", P)
         nc.vector.scalar_tensor_tensor(minus_dd_late, gates[:, :, blocks[last]], 1.0, dr_blocks[last][:], ALU.subtract, ALU.mult)
         for t in range(PACK):
             nc.scalar.activation(windows[t][:].indirect(listed(blocks[last])), minus_dd_late[:, t, :], ACT.Copy, scale=-1.0)
             nc.sync.dma_start(by_plane(out_1)[:, t, :], windows[t][:])
-        zc_grouped = tile("zc_grouped", [SLOTS, PACK], BF16, x_last_at + 2 * KIB)
+        zc_grouped = tile("zc_grouped", [SLOTS, PACK], BF16, x_last_at)
         for j in range(BLOCKS):
             nc.vector.tensor_tensor(
                 woven(zc_grouped[:, blocks[j], :]), by_pairs(zc_factor[:, :, blocks[j]]), by_pairs(dr_blocks[j][:]), ALU.mult
             )
 
-        def form_zg(h):
-            zg_grouped = tile("zg_grouped%d" % h, [SLOTS // 2, PACK], BF16)
-            if h == 0:
-                parts = [(halves[0], halves[0], minus_dd[:, :, halves[0]])]
-            else:
-                parts = [(blocks[0], blocks[2], minus_dd[:, :, blocks[2]]), (blocks[1], blocks[last], minus_dd_late)]
-            for place, slots, values in parts:
-                nc.vector.tensor_tensor(woven(zg_grouped[:, place, :]), by_pairs(zg_factor[:, :, slots]), by_pairs(values), ALU.mult)
-            return zg_grouped
+        def form_zg(grouped, slots, values):
+            nc.vector.tensor_tensor(woven(grouped), by_pairs(zg_factor[:, :, slots]), by_pairs(values), ALU.mult)
 
         def quantize_zc(h):
             return quantize(zc_grouped[:, halves[h], :], "zc%d" % h, E5M2, x_less_c_at + h * SLOTS // 2)
@@ -194,24 +190,8 @@ def tile_attend_ghighw_kernel(tc, dy, wo, gT, cT, xT, wg, wc, offs, out_0, out_1
                 product(bank[:, place, :], w_mx, blocks[2 + r], zg_mx, halves[0], False, True)
             return bank
 
-        zg_low = form_zg(0)
-        zc_low = quantize_zc(0)
-        w_low = quantize(w_low[:], "w0", E4M3, x_less_c_at + SLOTS)
-        zg_low = quantize(zg_low[:], "zg0", E5M2)
-        first = [second_product("plane%d" % r, [r], w_low, zc_low, zg_low) for r in range(2)]
-        w_high = tile("w_high", [K, PACK], BF16, x_less_c_at + 2 * SLOTS)
-        for pair in range(2):
-            group(nc.vector.tensor_copy, w_high[:, halves[pair], :], w_high_raw[pair][:])
-        zg_high = form_zg(1)
-        w_high = quantize(w_high[:], "w1", E4M3)
-        high_low = second_product("plane2", [0, 1], w_high, zc_low, zg_low)
-        zc_high = quantize_zc(1)
-        zg_high = quantize(zg_high[:], "zg1", E5M2)
-        low_high = second_product("plane3", [0, 1], w_low, zc_high, zg_high)
-        high_high = second_product("block0", [0, 1], w_high, zc_high, zg_high)
-
         s = [tile("s%d" % pair, [2 * SLOTS], F32)[:].rearrange("p (r n) -> p r n", r=2) for pair in range(2)]
-        s_windows = [windows[n] for n in (4, 5, 1, 0)]
+        s_windows = [windows[n] for n in (4, 5, 0, 1)]
 
         def scatter_on_scalar(r, slots):
             nc.scalar.activation(s_windows[r][:].indirect(listed(slots)), s[r // 2][:, r % 2, slots], ACT.Copy)
@@ -222,18 +202,39 @@ def tile_attend_ghighw_kernel(tc, dy, wo, gT, cT, xT, wg, wc, offs, out_0, out_1
         def store(r):
             nc.sync.dma_start(out_0[blocks[r], :], s_windows[r][:])
 
+        zg_low, zg_high = (tile("zg_grouped%d" % h, [SLOTS // 2, PACK], BF16) for h in range(2))
+        form_zg(zg_low[:], halves[0], minus_dd[:, :, halves[0]])
+        zc_low = quantize_zc(0)
+        w_low = quantize(w_low[:], "w0", E4M3, x_less_c_at + SLOTS)
+        zg_low = quantize(zg_low[:], "zg0", E5M2)
+        first = [second_product("plane%d" % r, [r], w_low, zc_low, zg_low) for r in range(2)]
+        w_high = tile("w_high", [K, PACK], BF16, x_less_c_at + 2 * SLOTS)
+        for pair in range(2):
+            group(nc.vector.tensor_copy, w_high[:, halves[pair], :], w_high_raw[pair][:])
+        form_zg(zg_high[:, blocks[0], :], blocks[2], minus_dd[:, :, blocks[2]])
+        w_high = quantize(w_high[:], "w1", E4M3)
+        high_low = second_product("plane2", [0, 1], w_high, zc_low, zg_low)
+        form_zg(zg_high[:, blocks[1], :], late, minus_dd_late)
+        zc_high = quantize_zc(1)
+        nc.vector.tensor_copy(s[1][:, :, halves[0]], high_low[:])
+        zg_high = quantize(zg_high[:], "zg1", E5M2)
+        high_high = second_product("block0", [0, 1], w_high, zc_high, zg_high)
+        low_high = second_product("plane3", [0, 1], w_low, zc_high, zg_high)
+
         for r in range(2):
             nc.scalar.copy(out=s[0][:, r, halves[0]], in_=first[r][:, 0, :])
+        for r in range(2):
             scatter_on_scalar(r, halves[0])
-        nc.vector.tensor_copy(s[1][:, :, halves[0]], high_low[:])
-        scatter_on_vector(3, halves[0])
-        nc.vector.tensor_copy(s[1][:, :, halves[1]], high_high[:])
+        scatter_on_vector(2, halves[0])
+        for r in range(2):
+            nc.vector.tensor_copy(s[1][:, r, halves[1]], high_high[:, r, :])
         nc.scalar.copy(out=s[0][:, :, halves[1]], in_=low_high[:])
+        scatter_on_scalar(3, slice(0, SCALAR_SHARE))
+        scatter_on_vector(2, halves[1])
+        store(2)
         scatter_on_scalar(0, halves[1])
         store(0)
+        scatter_on_vector(3, slice(SCALAR_SHARE, SLOTS))
+        store(3)
         scatter_on_scalar(1, halves[1])
         store(1)
-        scatter_on_vector(2, whole)
-        store(2)
-        scatter_on_scalar(3, halves[1])
-        store(3)

@@ -86,9 +86,9 @@ def tile_attend_ghighw_kernel(tc, dy, wo, gT, cT, xT, wg, wc, offs, out_0, out_1
         def woven(grouped):
             return grouped.rearrange("p (c i) t -> p c t i", i=2)
 
-        x_last_at, square_last_at, x_less_c_at = 0, 6 * KIB, 10 * KIB
+        x_last_at, x_less_c_at = 0, 6 * KIB
         windows = []
-        for engine in (nc.vector, nc.gpsimd) * 3:
+        for engine in (nc.vector, nc.vector, nc.gpsimd) * 2:
             window = tile("window%d" % len(windows), [TOKENS], F32)
             engine.memset(window[:], 0.0)
             windows.append(window)
@@ -127,21 +127,11 @@ def tile_attend_ghighw_kernel(tc, dy, wo, gT, cT, xT, wg, wc, offs, out_0, out_1
         gates, zg_factor, zc_factor = together("gates"), together("zg_factor"), together("zc_factor")
         minus_dd = together("minus_dd", last * P)
 
-        def load_weights(h):
-            raws = []
-            for label, matrix in (("wc", wc), ("wg", wg)):
-                raw = tile("%s_raw%d" % (label, h), [PACK, K // 2], F32)
-                nc.sync.dma_start(raw[:], by_plane(matrix)[:, :, halves[h]])
-                raws.append(raw)
-            return raws
-
         for t in range(PACK):
-            if t == last:
-                w_low_raw = load_weights(0)
             c = tile("c%d" % t, [SLOTS], F32)[:]
             rows = load_plane("c%d" % t)
             (gather_on_scalar if t == 0 else gather_on_vector)(c, rows, whole)
-            square = tile("c_squared%d" % t, [SLOTS], F32, square_last_at if t == last else None)
+            square = tile("c_squared%d" % t, [SLOTS], F32)
             slope = tile("slope%d" % t, [SLOTS], F32)
             for slots in halves:
                 nc.scalar.activation(square[:, slots], c[:, slots], ACT.Square)
@@ -153,11 +143,10 @@ def tile_attend_ghighw_kernel(tc, dy, wo, gT, cT, xT, wg, wc, offs, out_0, out_1
                 gather_on_vector(g, rows, slots)
             nc.gpsimd.tensor_tensor(zc_factor[:, t, :], g, slope[:], ALU.mult)
             nc.vector.scalar_tensor_tensor(minus_dd[:, t, :], g[:, early], 1.0, dr_planes[t][:, early], ALU.subtract, ALU.mult)
-            if t == last:
-                w_low = tile("w_low", [K, PACK], BF16, square_last_at)
-                for pair in range(2):
-                    group(nc.scalar.copy, w_low[:, halves[pair], :], w_low_raw[pair][:])
             nc.scalar.activation(windows[t][:].indirect(listed(early)), minus_dd[:, t, :], ACT.Copy, scale=-1.0)
+            if t == last:
+                wc_grouped = tile("wc_grouped", [K, PACK], BF16)
+                group(nc.scalar.copy, wc_grouped[:], load_matrix(wc, "wc", None)[:])
             x = tile("x%d" % t, [SLOTS], F32)[:]
             rows = load_plane("x%d" % t, x_last_at if t == last else None)
             gather_on_vector(x, rows, whole)
@@ -165,13 +154,13 @@ def tile_attend_ghighw_kernel(tc, dy, wo, gT, cT, xT, wg, wc, offs, out_0, out_1
             nc.gpsimd.tensor_tensor(x_less_c[:], x, c, ALU.subtract)
             nc.gpsimd.tensor_tensor(zg_factor[:, t, :], g, x_less_c[:], ALU.mult)
 
-        w_high_raw = load_weights(1)
-        minus_dd_late = together("minus_dd_late", P)
+        wg_raw = load_matrix(wg, "wg", None)
+        minus_dd_late = together("minus_dd_late", P, x_last_at)
         nc.vector.scalar_tensor_tensor(minus_dd_late, gates[:, :, blocks[last]], 1.0, dr_blocks[last][:], ALU.subtract, ALU.mult)
         for t in range(PACK):
             nc.scalar.activation(windows[t][:].indirect(listed(blocks[last])), minus_dd_late[:, t, :], ACT.Copy, scale=-1.0)
             nc.sync.dma_start(by_plane(out_1)[:, t, :], windows[t][:])
-        zc_grouped = tile("zc_grouped", [SLOTS, PACK], BF16, x_last_at)
+        zc_grouped = tile("zc_grouped", [SLOTS, PACK], BF16, x_last_at + 2 * KIB)
         for j in range(BLOCKS):
             nc.vector.tensor_tensor(
                 woven(zc_grouped[:, blocks[j], :]), by_pairs(zc_factor[:, :, blocks[j]]), by_pairs(dr_blocks[j][:]), ALU.mult
@@ -183,11 +172,11 @@ def tile_attend_ghighw_kernel(tc, dy, wo, gT, cT, xT, wg, wc, offs, out_0, out_1
         def quantize_zc(h):
             return quantize(zc_grouped[:, halves[h], :], "zc%d" % h, E5M2, x_less_c_at + h * SLOTS // 2)
 
-        def second_product(tag, rows, w_mx, zc_mx, zg_mx):
+        def second_product(tag, rows, wg_mx, zc_mx, zg_mx):
             bank = psum.tile([P, len(rows), SLOTS // 2], F32, name="s_" + tag, tag=tag)
             for place, r in enumerate(rows):
-                product(bank[:, place, :], w_mx, blocks[r], zc_mx, halves[0], True, False)
-                product(bank[:, place, :], w_mx, blocks[2 + r], zg_mx, halves[0], False, True)
+                product(bank[:, place, :], wc_mx, blocks[r], zc_mx, halves[0], True, False)
+                product(bank[:, place, :], wg_mx, blocks[r % 2], zg_mx, halves[0], False, True)
             return bank
 
         s = [tile("s%d" % pair, [2 * SLOTS], F32)[:].rearrange("p (r n) -> p r n", r=2) for pair in range(2)]
@@ -203,23 +192,24 @@ def tile_attend_ghighw_kernel(tc, dy, wo, gT, cT, xT, wg, wc, offs, out_0, out_1
             nc.sync.dma_start(out_0[blocks[r], :], s_windows[r][:])
 
         zg_low, zg_high = (tile("zg_grouped%d" % h, [SLOTS // 2, PACK], BF16) for h in range(2))
+        wg_grouped = tile("wg_grouped", [K, PACK], BF16, x_less_c_at + 2 * SLOTS)
+        group(nc.vector.tensor_copy, wg_grouped[:, halves[0], :], wg_raw[:, :, halves[0]])
         form_zg(zg_low[:], halves[0], minus_dd[:, :, halves[0]])
+        wc_mx = quantize(wc_grouped[:], "wc", E4M3, x_less_c_at + SLOTS)
         zc_low = quantize_zc(0)
-        w_low = quantize(w_low[:], "w0", E4M3, x_less_c_at + SLOTS)
+        wg_low = quantize(wg_grouped[:, halves[0], :], "wg0", E4M3)
         zg_low = quantize(zg_low[:], "zg0", E5M2)
-        first = [second_product("plane%d" % r, [r], w_low, zc_low, zg_low) for r in range(2)]
-        w_high = tile("w_high", [K, PACK], BF16, x_less_c_at + 2 * SLOTS)
-        for pair in range(2):
-            group(nc.vector.tensor_copy, w_high[:, halves[pair], :], w_high_raw[pair][:])
+        first = [second_product("plane%d" % r, [r], wg_low, zc_low, zg_low) for r in range(2)]
+        group(nc.vector.tensor_copy, wg_grouped[:, halves[1], :], wg_raw[:, :, halves[1]])
         form_zg(zg_high[:, blocks[0], :], blocks[2], minus_dd[:, :, blocks[2]])
-        w_high = quantize(w_high[:], "w1", E4M3)
-        high_low = second_product("plane2", [0, 1], w_high, zc_low, zg_low)
+        wg_high = quantize(wg_grouped[:, halves[1], :], "wg1", E4M3)
+        high_low = second_product("plane2", [2, 3], wg_high, zc_low, zg_low)
         form_zg(zg_high[:, blocks[1], :], late, minus_dd_late)
         zc_high = quantize_zc(1)
         nc.vector.tensor_copy(s[1][:, :, halves[0]], high_low[:])
         zg_high = quantize(zg_high[:], "zg1", E5M2)
-        high_high = second_product("block0", [0, 1], w_high, zc_high, zg_high)
-        low_high = second_product("plane3", [0, 1], w_low, zc_high, zg_high)
+        high_high = second_product("block0", [2, 3], wg_high, zc_high, zg_high)
+        low_high = second_product("plane3", [0, 1], wg_low, zc_high, zg_high)
 
         for r in range(2):
             nc.scalar.copy(out=s[0][:, r, halves[0]], in_=first[r][:, 0, :])

@@ -81,10 +81,10 @@ def tile_attend_ghighw_kernel(tc, dy, wo, gT, cT, xT, wg, wc, offs, out_0, out_1
             nc.scalar.activation(picked[:, slots], rows[:].indirect(listed(slots)), ACT.Copy)
 
         def by_pairs(planes):
-            return planes.rearrange("p t (c i) -> p c t i", i=2)
+            return planes.rearrange("p t (c i) -> p c t i", i=4)
 
         def woven(grouped):
-            return grouped.rearrange("p (c i) t -> p c t i", i=2)
+            return grouped.rearrange("p (c i) t -> p c t i", i=4)
 
         x_last_at, x_less_c_at = 0, 6 * KIB
         windows = []

@@ -19,7 +19,7 @@ K = 512
 SLOTS = 512
 TOKENS = 1024
 BLOCKS = SLOTS // P
-SCALAR_SHARE = 192
+SCALAR_SHARE = 160
 VECTOR_SHARE = 352
 KIB = 1024
 EDGE = 64
@@ -139,20 +139,24 @@ def tile_attend_ghighw_kernel(tc, dy, wo, gT, cT, xT, wg, wc, offs, out_0, out_1
                 nc.scalar.activation(slope[:, slots], square[:, slots], ACT.Copy, bias=1.0, scale=-1.0)
             g = gates[:, t, :]
             rows = load_plane("g%d" % t)
-            for slots in (early, late):
+            parts = (early,) if t == 0 else (halves[0], blocks[2])
+            for slots in parts:
                 gather_on_vector(g, rows, slots)
+            (gather_on_vector if t == 0 else gather_on_scalar)(g, rows, late)
             nc.gpsimd.tensor_tensor(zc_factor[:, t, :], g, slope[:], ALU.mult)
-            nc.vector.scalar_tensor_tensor(minus_dd[:, t, :], g[:, early], 1.0, dr_planes[t][:, early], ALU.subtract, ALU.mult)
+            for slots in parts:
+                nc.vector.scalar_tensor_tensor(minus_dd[:, t, slots], g[:, slots], 1.0, dr_planes[t][:, slots], ALU.subtract, ALU.mult)
             nc.scalar.activation(windows[t][:].indirect(listed(early)), minus_dd[:, t, :], ACT.Copy, scale=-1.0)
             if t == last:
                 wc_grouped = tile("wc_grouped", [K, PACK], BF16)
                 group(nc.scalar.copy, wc_grouped[:], load_matrix(wc, "wc", None)[:])
-            x = tile("x%d" % t, [SLOTS], F32)[:]
+            x = tile("x%d" % t, [SLOTS], F32, x_less_c_at if t == last else None)[:]
             rows = load_plane("x%d" % t, x_last_at if t == last else None)
             gather_on_vector(x, rows, whole)
-            x_less_c = tile("x_less_c%d" % t, [SLOTS], F32, x_less_c_at if t == last else None)
+            x_less_c = tile("x_less_c%d" % t, [SLOTS], F32)
             nc.gpsimd.tensor_tensor(x_less_c[:], x, c, ALU.subtract)
-            nc.gpsimd.tensor_tensor(zg_factor[:, t, :], g, x_less_c[:], ALU.mult)
+            if t < last:
+                nc.gpsimd.tensor_tensor(zg_factor[:, t, :], g, x_less_c[:], ALU.mult)
 
         wg_raw = load_matrix(wg, "wg", None)
         minus_dd_late = together("minus_dd_late", P, x_last_at)
@@ -172,59 +176,60 @@ def tile_attend_ghighw_kernel(tc, dy, wo, gT, cT, xT, wg, wc, offs, out_0, out_1
         def quantize_zc(h):
             return quantize(zc_grouped[:, halves[h], :], "zc%d" % h, E5M2, x_less_c_at + h * SLOTS // 2)
 
-        def second_product(tag, rows, wg_mx, zc_mx, zg_mx):
+        def second_product(tag, rows, zc_mx, zg_mx):
             bank = psum.tile([P, len(rows), SLOTS // 2], F32, name="s_" + tag, tag=tag)
             for place, r in enumerate(rows):
                 product(bank[:, place, :], wc_mx, blocks[r], zc_mx, halves[0], True, False)
-                product(bank[:, place, :], wg_mx, blocks[r % 2], zg_mx, halves[0], False, True)
+                product(bank[:, place, :], wg_mx[r // 2], blocks[r % 2], zg_mx, halves[0], False, True)
             return bank
 
-        s = [tile("s%d" % pair, [2 * SLOTS], F32)[:].rearrange("p (r n) -> p r n", r=2) for pair in range(2)]
+        s = together("s")
         s_windows = [windows[n] for n in (4, 5, 0, 1)]
 
         def scatter_on_scalar(r, slots):
-            nc.scalar.activation(s_windows[r][:].indirect(listed(slots)), s[r // 2][:, r % 2, slots], ACT.Copy)
+            nc.scalar.activation(s_windows[r][:].indirect(listed(slots)), s[:, r, slots], ACT.Copy)
 
         def scatter_on_vector(r, slots):
-            nc.vector.tensor_copy(s_windows[r][:].indirect(listed(slots)), s[r // 2][:, r % 2, slots])
+            nc.vector.tensor_copy(s_windows[r][:].indirect(listed(slots)), s[:, r, slots])
 
         def store(r):
             nc.sync.dma_start(out_0[blocks[r], :], s_windows[r][:])
 
         zg_low, zg_high = (tile("zg_grouped%d" % h, [SLOTS // 2, PACK], BF16) for h in range(2))
+        nc.vector.tensor_tensor(zg_factor[:, last, :], g, x_less_c[:], ALU.mult)
         wg_grouped = tile("wg_grouped", [K, PACK], BF16, x_less_c_at + 2 * SLOTS)
         group(nc.vector.tensor_copy, wg_grouped[:, halves[0], :], wg_raw[:, :, halves[0]])
         form_zg(zg_low[:], halves[0], minus_dd[:, :, halves[0]])
         wc_mx = quantize(wc_grouped[:], "wc", E4M3, x_less_c_at + SLOTS)
         zc_low = quantize_zc(0)
-        wg_low = quantize(wg_grouped[:, halves[0], :], "wg0", E4M3)
+        wg_mx = [quantize(wg_grouped[:, halves[0], :], "wg0", E4M3)]
         zg_low = quantize(zg_low[:], "zg0", E5M2)
-        first = [second_product("plane%d" % r, [r], wg_low, zc_low, zg_low) for r in range(2)]
+        first = [second_product("plane%d" % r, [r], zc_low, zg_low) for r in range(2)]
         group(nc.vector.tensor_copy, wg_grouped[:, halves[1], :], wg_raw[:, :, halves[1]])
         form_zg(zg_high[:, blocks[0], :], blocks[2], minus_dd[:, :, blocks[2]])
-        wg_high = quantize(wg_grouped[:, halves[1], :], "wg1", E4M3)
-        high_low = second_product("plane2", [2, 3], wg_high, zc_low, zg_low)
+        wg_mx.append(quantize(wg_grouped[:, halves[1], :], "wg1", E4M3))
+        high_low = second_product("plane2", [2, 3], zc_low, zg_low)
         form_zg(zg_high[:, blocks[1], :], late, minus_dd_late)
         zc_high = quantize_zc(1)
-        nc.vector.tensor_copy(s[1][:, :, halves[0]], high_low[:])
+        nc.vector.tensor_copy(s[:, 2:PACK, halves[0]], high_low[:])
         zg_high = quantize(zg_high[:], "zg1", E5M2)
-        high_high = second_product("block0", [2, 3], wg_high, zc_high, zg_high)
-        low_high = second_product("plane3", [0, 1], wg_low, zc_high, zg_high)
+        outer = second_product("plane3", [0, 3], zc_high, zg_high)
+        inner = second_product("block0", [2, 1], zc_high, zg_high)
 
         for r in range(2):
-            nc.scalar.copy(out=s[0][:, r, halves[0]], in_=first[r][:, 0, :])
+            nc.scalar.copy(out=s[:, r, halves[0]], in_=first[r][:, 0, :])
         for r in range(2):
             scatter_on_scalar(r, halves[0])
-        scatter_on_vector(2, halves[0])
-        for r in range(2):
-            nc.vector.tensor_copy(s[1][:, r, halves[1]], high_high[:, r, :])
-        nc.scalar.copy(out=s[0][:, :, halves[1]], in_=low_high[:])
-        scatter_on_scalar(3, slice(0, SCALAR_SHARE))
-        scatter_on_vector(2, halves[1])
-        store(2)
+        scatter_on_vector(2, blocks[0])
+        nc.vector.tensor_copy(s[:, 0:PACK:last, halves[1]], outer[:])
+        for place, r in enumerate((2, 1)):
+            nc.vector.tensor_copy(s[:, r, halves[1]], inner[:, place, :])
         scatter_on_scalar(0, halves[1])
         store(0)
-        scatter_on_vector(3, slice(SCALAR_SHARE, SLOTS))
-        store(3)
+        scatter_on_scalar(3, slice(SLOTS - SCALAR_SHARE, SLOTS))
+        scatter_on_vector(2, slice(P, SLOTS))
+        store(2)
         scatter_on_scalar(1, halves[1])
         store(1)
+        scatter_on_vector(3, slice(0, SLOTS - SCALAR_SHARE))
+        store(3)

@@ -20,6 +20,7 @@ SLOTS = 512
 TOKENS = 1024
 BLOCKS = SLOTS // P
 SCALAR_SHARE = 160
+WG_TAIL = 64
 VECTOR_SHARE = 352
 KIB = 1024
 EDGE = 64
@@ -132,18 +133,23 @@ def tile_attend_ghighw_kernel(tc, dy, wo, gT, cT, xT, wg, wc, offs, out_0, out_1
             rows = load_plane("c%d" % t)
             (gather_on_scalar if t == 0 else gather_on_vector)(c, rows, whole)
             square = tile("c_squared%d" % t, [SLOTS], F32)
-            slope = tile("slope%d" % t, [SLOTS], F32)
+            slope = tile("slope%d" % t, [SLOTS], F32)[:] if t < last else zg_factor[:, last - 1, :]
             for slots in halves:
                 nc.scalar.activation(square[:, slots], c[:, slots], ACT.Square)
-            for slots in halves:
-                nc.scalar.activation(slope[:, slots], square[:, slots], ACT.Copy, bias=1.0, scale=-1.0)
+            if t % 2 == 0:
+                nc.gpsimd.tensor_scalar(slope, square[:], -1.0, 1.0, ALU.mult, ALU.add)
+            else:
+                for slots in halves:
+                    nc.scalar.activation(slope[:, slots], square[:, slots], ACT.Copy, bias=1.0, scale=-1.0)
             g = gates[:, t, :]
             rows = load_plane("g%d" % t)
-            parts = (early,) if t == 0 else (halves[0], blocks[2])
+            parts = (halves[0], blocks[2])
             for slots in parts:
                 gather_on_vector(g, rows, slots)
-            (gather_on_vector if t == 0 else gather_on_scalar)(g, rows, late)
-            nc.gpsimd.tensor_tensor(zc_factor[:, t, :], g, slope[:], ALU.mult)
+            gather_on_scalar(g, rows, late)
+            nc.gpsimd.tensor_tensor(zc_factor[:, t, :], g, slope, ALU.mult)
+            if t == last:
+                nc.gpsimd.tensor_tensor(zg_factor[:, t - 1, :], gates[:, t - 1, :], x_less_c[:], ALU.mult)
             for slots in parts:
                 nc.vector.scalar_tensor_tensor(minus_dd[:, t, slots], g[:, slots], 1.0, dr_planes[t][:, slots], ALU.subtract, ALU.mult)
             nc.scalar.activation(windows[t][:].indirect(listed(early)), minus_dd[:, t, :], ACT.Copy, scale=-1.0)
@@ -155,7 +161,7 @@ def tile_attend_ghighw_kernel(tc, dy, wo, gT, cT, xT, wg, wc, offs, out_0, out_1
             gather_on_vector(x, rows, whole)
             x_less_c = tile("x_less_c%d" % t, [SLOTS], F32)
             nc.gpsimd.tensor_tensor(x_less_c[:], x, c, ALU.subtract)
-            if t < last:
+            if t < last - 1:
                 nc.gpsimd.tensor_tensor(zg_factor[:, t, :], g, x_less_c[:], ALU.mult)
 
         wg_raw = load_matrix(wg, "wg", None)
@@ -176,10 +182,13 @@ def tile_attend_ghighw_kernel(tc, dy, wo, gT, cT, xT, wg, wc, offs, out_0, out_1
         def quantize_zc(h):
             return quantize(zc_grouped[:, halves[h], :], "zc%d" % h, E5M2, x_less_c_at + h * SLOTS // 2)
 
+        def quantize_wc(h):
+            return quantize(wc_grouped[:, halves[h], :], "wc%d" % h, E4M3, x_less_c_at + SLOTS + h * SLOTS // 2)
+
         def second_product(tag, rows, zc_mx, zg_mx):
             bank = psum.tile([P, len(rows), SLOTS // 2], F32, name="s_" + tag, tag=tag)
             for place, r in enumerate(rows):
-                product(bank[:, place, :], wc_mx, blocks[r], zc_mx, halves[0], True, False)
+                product(bank[:, place, :], wc_mx[r // 2], blocks[r % 2], zc_mx, halves[0], True, False)
                 product(bank[:, place, :], wg_mx[r // 2], blocks[r % 2], zg_mx, halves[0], False, True)
             return bank
 
@@ -200,18 +209,19 @@ def tile_attend_ghighw_kernel(tc, dy, wo, gT, cT, xT, wg, wc, offs, out_0, out_1
         wg_grouped = tile("wg_grouped", [K, PACK], BF16, x_less_c_at + 2 * SLOTS)
         group(nc.vector.tensor_copy, wg_grouped[:, halves[0], :], wg_raw[:, :, halves[0]])
         form_zg(zg_low[:], halves[0], minus_dd[:, :, halves[0]])
-        wc_mx = quantize(wc_grouped[:], "wc", E4M3, x_less_c_at + SLOTS)
         zc_low = quantize_zc(0)
+        wc_mx = [quantize_wc(0)]
         wg_mx = [quantize(wg_grouped[:, halves[0], :], "wg0", E4M3)]
         zg_low = quantize(zg_low[:], "zg0", E5M2)
         first = [second_product("plane%d" % r, [r], zc_low, zg_low) for r in range(2)]
-        group(nc.vector.tensor_copy, wg_grouped[:, halves[1], :], wg_raw[:, :, halves[1]])
+        for copy, cols in ((nc.vector.tensor_copy, slice(K // 2, K - WG_TAIL)), (nc.scalar.copy, slice(K - WG_TAIL, K))):
+            group(copy, wg_grouped[:, cols, :], wg_raw[:, :, cols])
         form_zg(zg_high[:, blocks[0], :], blocks[2], minus_dd[:, :, blocks[2]])
+        wc_mx.append(quantize_wc(1))
         wg_mx.append(quantize(wg_grouped[:, halves[1], :], "wg1", E4M3))
         high_low = second_product("plane2", [2, 3], zc_low, zg_low)
         form_zg(zg_high[:, blocks[1], :], late, minus_dd_late)
         zc_high = quantize_zc(1)
-        nc.vector.tensor_copy(s[:, 2:PACK, halves[0]], high_low[:])
         zg_high = quantize(zg_high[:], "zg1", E5M2)
         outer = second_product("plane3", [0, 3], zc_high, zg_high)
         inner = second_product("block0", [2, 1], zc_high, zg_high)
@@ -220,6 +230,8 @@ def tile_attend_ghighw_kernel(tc, dy, wo, gT, cT, xT, wg, wc, offs, out_0, out_1
             nc.scalar.copy(out=s[:, r, halves[0]], in_=first[r][:, 0, :])
         for r in range(2):
             scatter_on_scalar(r, halves[0])
+        for place, r in enumerate((2, 3)):
+            nc.vector.tensor_copy(s[:, r, halves[0]], high_low[:, place, :])
         scatter_on_vector(2, blocks[0])
         nc.vector.tensor_copy(s[:, 0:PACK:last, halves[1]], outer[:])
         for place, r in enumerate((2, 1)):

@@ -19,8 +19,8 @@ K = 512
 SLOTS = 512
 TOKENS = 1024
 BLOCKS = SLOTS // P
-SCALAR_SHARE = 160
-WG_TAIL = 64
+SCALAR_SHARE = 192
+WC_TAIL = 128
 VECTOR_SHARE = 352
 KIB = 1024
 EDGE = 64
@@ -87,7 +87,7 @@ def tile_attend_ghighw_kernel(tc, dy, wo, gT, cT, xT, wg, wc, offs, out_0, out_1
         def woven(grouped):
             return grouped.rearrange("p (c i) t -> p c t i", i=4)
 
-        x_last_at, x_less_c_at = 0, 6 * KIB
+        x_last_at, c_last_at = 0, 8 * KIB
         windows = []
         for engine in (nc.vector, nc.vector, nc.gpsimd) * 2:
             window = tile("window%d" % len(windows), [TOKENS], F32)
@@ -112,12 +112,11 @@ def tile_attend_ghighw_kernel(tc, dy, wo, gT, cT, xT, wg, wc, offs, out_0, out_1
         dy_mx = quantize(dy_grouped[:], "dy", E5M2)
 
         whole = slice(0, SLOTS)
-        dr_planes = [psum.tile([P, SLOTS], F32, name="dr_plane%d" % t, tag="plane%d" % t) for t in range(PACK)]
+        low, high = halves
+        dr_planes = [psum.tile([P, SLOTS // 2], F32, name="dr_plane%d" % t, tag="plane%d" % t) for t in range(PACK)]
         dr_blocks = [psum.tile([P, PACK, P], F32, name="dr_block%d" % j, tag="block%d" % j) for j in range(BLOCKS)]
-        early, late = slice(0, last * P), blocks[last]
         for t in range(PACK):
-            for slots in (halves[0], blocks[2]):
-                product(dr_planes[t][:, slots], wo_mx, blocks[t], dy_mx, slots, True, True)
+            product(dr_planes[t][:], wo_mx, blocks[t], dy_mx, low, True, True)
         for j in range(BLOCKS):
             for t in range(PACK):
                 product(dr_blocks[j][:, t, :], wo_mx, blocks[t], dy_mx, blocks[j], True, True)
@@ -126,64 +125,77 @@ def tile_attend_ghighw_kernel(tc, dy, wo, gT, cT, xT, wg, wc, offs, out_0, out_1
             return tile(label, [PACK * width], F32, place)[:].rearrange("p (t n) -> p t n", t=PACK)
 
         gates, zg_factor, zc_factor = together("gates"), together("zg_factor"), together("zc_factor")
-        minus_dd = together("minus_dd", last * P)
+        minus_dd = together("minus_dd", SLOTS // 2)
+
+        def late_dd(j, place=None):
+            values = together("minus_dd_block%d" % j, P, place)
+            nc.vector.scalar_tensor_tensor(values, gates[:, :, blocks[j]], 1.0, dr_blocks[j][:], ALU.subtract, ALU.mult)
+            return values
+
+        def scatter_dd(t, slots, values):
+            nc.scalar.activation(windows[t][:].indirect(listed(slots)), values, ACT.Copy, scale=-1.0)
 
         for t in range(PACK):
-            c = tile("c%d" % t, [SLOTS], F32)[:]
+            c = [tile("c%d_%d" % (t, h), [SLOTS // 2], F32, c_last_at if (t, h) == (last, 0) else None)[:] for h in range(2)] if t == last else None
+            if t < last:
+                c_whole = tile("c%d" % t, [SLOTS], F32)[:]
+                c = [c_whole[:, slots] for slots in halves]
             rows = load_plane("c%d" % t)
-            (gather_on_scalar if t == 0 else gather_on_vector)(c, rows, whole)
             square = tile("c_squared%d" % t, [SLOTS], F32)
-            slope = tile("slope%d" % t, [SLOTS], F32)[:] if t < last else zg_factor[:, last - 1, :]
-            for slots in halves:
-                nc.scalar.activation(square[:, slots], c[:, slots], ACT.Square)
-            if t % 2 == 0:
-                nc.gpsimd.tensor_scalar(slope, square[:], -1.0, 1.0, ALU.mult, ALU.add)
-            else:
-                for slots in halves:
-                    nc.scalar.activation(slope[:, slots], square[:, slots], ACT.Copy, bias=1.0, scale=-1.0)
+            for h in range(2):
+                nc.scalar.activation(c[h], rows[:].indirect(listed(halves[h])), ACT.Copy)
+            for h in range(2):
+                nc.scalar.activation(square[:, halves[h]], c[h], ACT.Square)
             g = gates[:, t, :]
             rows = load_plane("g%d" % t)
-            parts = (halves[0], blocks[2])
-            for slots in parts:
-                gather_on_vector(g, rows, slots)
-            gather_on_scalar(g, rows, late)
-            nc.gpsimd.tensor_tensor(zc_factor[:, t, :], g, slope, ALU.mult)
+            gather_on_vector(g, rows, low)
+            gather_on_vector(g, rows, blocks[2] if t == 0 else high)
+            if t == 0:
+                gather_on_scalar(g, rows, blocks[last])
+            nc.vector.scalar_tensor_tensor(minus_dd[:, t, :], g[:, low], 1.0, dr_planes[t][:], ALU.subtract, ALU.mult)
+            scatter_dd(t, low, minus_dd[:, t, :])
             if t == last:
-                nc.gpsimd.tensor_tensor(zg_factor[:, t - 1, :], gates[:, t - 1, :], x_less_c[:], ALU.mult)
-            for slots in parts:
-                nc.vector.scalar_tensor_tensor(minus_dd[:, t, slots], g[:, slots], 1.0, dr_planes[t][:, slots], ALU.subtract, ALU.mult)
-            nc.scalar.activation(windows[t][:].indirect(listed(early)), minus_dd[:, t, :], ACT.Copy, scale=-1.0)
-            if t == last:
-                wc_grouped = tile("wc_grouped", [K, PACK], BF16)
-                group(nc.scalar.copy, wc_grouped[:], load_matrix(wc, "wc", None)[:])
-            x = tile("x%d" % t, [SLOTS], F32, x_less_c_at if t == last else None)[:]
+                dd_third = late_dd(2)
+            nc.vector.scalar_tensor_tensor(zc_factor[:, t, :], square[:], 1.0, g, ALU.subtract, ALU.mult)
             rows = load_plane("x%d" % t, x_last_at if t == last else None)
-            gather_on_vector(x, rows, whole)
             x_less_c = tile("x_less_c%d" % t, [SLOTS], F32)
-            nc.gpsimd.tensor_tensor(x_less_c[:], x, c, ALU.subtract)
-            if t < last - 1:
-                nc.gpsimd.tensor_tensor(zg_factor[:, t, :], g, x_less_c[:], ALU.mult)
+            if t < last:
+                nc.vector.tensor_tensor(x_less_c[:], rows[:].indirect(listed(whole)), c_whole, ALU.subtract)
+            else:
+                for h in range(2):
+                    nc.vector.tensor_tensor(x_less_c[:, halves[h]], rows[:].indirect(listed(halves[h])), c[h], ALU.subtract)
+            nc.gpsimd.tensor_tensor(zg_factor[:, t, :], g, x_less_c[:], ALU.mult)
 
+        wc_raw = load_matrix(wc, "wc", None)
         wg_raw = load_matrix(wg, "wg", None)
-        minus_dd_late = together("minus_dd_late", P, x_last_at)
-        nc.vector.scalar_tensor_tensor(minus_dd_late, gates[:, :, blocks[last]], 1.0, dr_blocks[last][:], ALU.subtract, ALU.mult)
+        dd_fourth = late_dd(last, c_last_at)
         for t in range(PACK):
-            nc.scalar.activation(windows[t][:].indirect(listed(blocks[last])), minus_dd_late[:, t, :], ACT.Copy, scale=-1.0)
+            scatter_dd(t, blocks[2], dd_third[:, t, :])
+        for t in range(PACK):
+            scatter_dd(t, blocks[last], dd_fourth[:, t, :])
             nc.sync.dma_start(by_plane(out_1)[:, t, :], windows[t][:])
-        zc_grouped = tile("zc_grouped", [SLOTS, PACK], BF16, x_last_at + 2 * KIB)
+        zc_grouped = tile("zc_grouped", [SLOTS, PACK], BF16, x_last_at)
         for j in range(BLOCKS):
             nc.vector.tensor_tensor(
                 woven(zc_grouped[:, blocks[j], :]), by_pairs(zc_factor[:, :, blocks[j]]), by_pairs(dr_blocks[j][:]), ALU.mult
             )
+        wc_grouped = tile("wc_grouped", [K, PACK], BF16)
+        nc.gpsimd.tensor_scalar(wc_grouped[:, low, :], wc_raw[:, :, low].rearrange("p j n -> p n j"), -1.0, 0.0, ALU.mult, ALU.add)
+
+        def negate_on_vector(out, in_):
+            nc.vector.tensor_scalar(out, in_, -1.0, None, ALU.mult)
+
+        def negate_on_scalar(out, in_):
+            nc.scalar.activation(out, in_, ACT.Copy, scale=-1.0)
 
         def form_zg(grouped, slots, values):
             nc.vector.tensor_tensor(woven(grouped), by_pairs(zg_factor[:, :, slots]), by_pairs(values), ALU.mult)
 
         def quantize_zc(h):
-            return quantize(zc_grouped[:, halves[h], :], "zc%d" % h, E5M2, x_less_c_at + h * SLOTS // 2)
+            return quantize(zc_grouped[:, halves[h], :], "zc%d" % h, E5M2)
 
         def quantize_wc(h):
-            return quantize(wc_grouped[:, halves[h], :], "wc%d" % h, E4M3, x_less_c_at + SLOTS + h * SLOTS // 2)
+            return quantize(wc_grouped[:, halves[h], :], "wc%d" % h, E4M3)
 
         def second_product(tag, rows, zc_mx, zg_mx):
             bank = psum.tile([P, len(rows), SLOTS // 2], F32, name="s_" + tag, tag=tag)
@@ -205,22 +217,22 @@ def tile_attend_ghighw_kernel(tc, dy, wo, gT, cT, xT, wg, wc, offs, out_0, out_1
             nc.sync.dma_start(out_0[blocks[r], :], s_windows[r][:])
 
         zg_low, zg_high = (tile("zg_grouped%d" % h, [SLOTS // 2, PACK], BF16) for h in range(2))
-        nc.vector.tensor_tensor(zg_factor[:, last, :], g, x_less_c[:], ALU.mult)
-        wg_grouped = tile("wg_grouped", [K, PACK], BF16, x_less_c_at + 2 * SLOTS)
-        group(nc.vector.tensor_copy, wg_grouped[:, halves[0], :], wg_raw[:, :, halves[0]])
-        form_zg(zg_low[:], halves[0], minus_dd[:, :, halves[0]])
+        wg_grouped = tile("wg_grouped", [K, PACK], BF16)
+        form_zg(zg_low[:], low, minus_dd)
+        group(nc.vector.tensor_copy, wg_grouped[:, low, :], wg_raw[:, :, low])
         zc_low = quantize_zc(0)
         wc_mx = [quantize_wc(0)]
-        wg_mx = [quantize(wg_grouped[:, halves[0], :], "wg0", E4M3)]
+        wg_mx = [quantize(wg_grouped[:, low, :], "wg0", E4M3)]
         zg_low = quantize(zg_low[:], "zg0", E5M2)
         first = [second_product("plane%d" % r, [r], zc_low, zg_low) for r in range(2)]
-        for copy, cols in ((nc.vector.tensor_copy, slice(K // 2, K - WG_TAIL)), (nc.scalar.copy, slice(K - WG_TAIL, K))):
-            group(copy, wg_grouped[:, cols, :], wg_raw[:, :, cols])
-        form_zg(zg_high[:, blocks[0], :], blocks[2], minus_dd[:, :, blocks[2]])
+        for copy, cols in ((negate_on_vector, slice(K // 2, K - WC_TAIL)), (negate_on_scalar, slice(K - WC_TAIL, K))):
+            group(copy, wc_grouped[:, cols, :], wc_raw[:, :, cols])
+        group(nc.vector.tensor_copy, wg_grouped[:, high, :], wg_raw[:, :, high])
+        form_zg(zg_high[:, blocks[0], :], blocks[2], dd_third)
         wc_mx.append(quantize_wc(1))
-        wg_mx.append(quantize(wg_grouped[:, halves[1], :], "wg1", E4M3))
+        wg_mx.append(quantize(wg_grouped[:, high, :], "wg1", E4M3))
         high_low = second_product("plane2", [2, 3], zc_low, zg_low)
-        form_zg(zg_high[:, blocks[1], :], late, minus_dd_late)
+        form_zg(zg_high[:, blocks[1], :], blocks[last], dd_fourth)
         zc_high = quantize_zc(1)
         zg_high = quantize(zg_high[:], "zg1", E5M2)
         outer = second_product("plane3", [0, 3], zc_high, zg_high)

@@ -19,7 +19,7 @@ K = 512
 SLOTS = 512
 TOKENS = 1024
 BLOCKS = SLOTS // P
-SCALAR_SHARE = 192
+SCALAR_SHARE = 160
 WC_TAIL = 128
 VECTOR_SHARE = 352
 KIB = 1024
@@ -113,68 +113,84 @@ def tile_attend_ghighw_kernel(tc, dy, wo, gT, cT, xT, wg, wc, offs, out_0, out_1
 
         whole = slice(0, SLOTS)
         low, high = halves
-        dr_planes = [psum.tile([P, SLOTS // 2], F32, name="dr_plane%d" % t, tag="plane%d" % t) for t in range(PACK)]
+        early, late = slice(0, last * P), blocks[last]
+        dr_planes = [psum.tile([P, last * P], F32, name="dr_plane%d" % t, tag="plane%d" % t) for t in range(PACK)]
         dr_blocks = [psum.tile([P, PACK, P], F32, name="dr_block%d" % j, tag="block%d" % j) for j in range(BLOCKS)]
         for t in range(PACK):
-            product(dr_planes[t][:], wo_mx, blocks[t], dy_mx, low, True, True)
+            for slots in (low, blocks[2]):
+                product(dr_planes[t][:, slots], wo_mx, blocks[t], dy_mx, slots, True, True)
         for j in range(BLOCKS):
             for t in range(PACK):
                 product(dr_blocks[j][:, t, :], wo_mx, blocks[t], dy_mx, blocks[j], True, True)
 
-        def together(label, width=SLOTS, place=None):
-            return tile(label, [PACK * width], F32, place)[:].rearrange("p (t n) -> p t n", t=PACK)
+        def together(label, width=SLOTS):
+            return tile(label, [PACK * width], F32)[:].rearrange("p (t n) -> p t n", t=PACK)
 
         gates, zg_factor, zc_factor = together("gates"), together("zg_factor"), together("zc_factor")
-        minus_dd = together("minus_dd", SLOTS // 2)
-
-        def late_dd(j, place=None):
-            values = together("minus_dd_block%d" % j, P, place)
-            nc.vector.scalar_tensor_tensor(values, gates[:, :, blocks[j]], 1.0, dr_blocks[j][:], ALU.subtract, ALU.mult)
-            return values
+        minus_dd = together("minus_dd", last * P)
 
         def scatter_dd(t, slots, values):
             nc.scalar.activation(windows[t][:].indirect(listed(slots)), values, ACT.Copy, scale=-1.0)
 
+        def load_c(t, part):
+            columns = slice(part * TOKENS // 2, (part + 1) * TOKENS // 2)
+            nc.sync.dma_start(c_rows[t][:, columns], by_plane(cT)[:, t, columns])
+
+        c_rows = [tile("c%d_rows" % t, [TOKENS], F32) for t in range(PACK)]
         for t in range(PACK):
-            c = [tile("c%d_%d" % (t, h), [SLOTS // 2], F32, c_last_at if (t, h) == (last, 0) else None)[:] for h in range(2)] if t == last else None
-            if t < last:
-                c_whole = tile("c%d" % t, [SLOTS], F32)[:]
-                c = [c_whole[:, slots] for slots in halves]
-            rows = load_plane("c%d" % t)
-            square = tile("c_squared%d" % t, [SLOTS], F32)
-            for h in range(2):
-                nc.scalar.activation(c[h], rows[:].indirect(listed(halves[h])), ACT.Copy)
-            for h in range(2):
-                nc.scalar.activation(square[:, halves[h]], c[h], ACT.Square)
-            g = gates[:, t, :]
-            rows = load_plane("g%d" % t)
-            gather_on_vector(g, rows, low)
-            gather_on_vector(g, rows, blocks[2] if t == 0 else high)
-            if t == 0:
-                gather_on_scalar(g, rows, blocks[last])
-            nc.vector.scalar_tensor_tensor(minus_dd[:, t, :], g[:, low], 1.0, dr_planes[t][:], ALU.subtract, ALU.mult)
-            scatter_dd(t, low, minus_dd[:, t, :])
-            if t == last:
-                dd_third = late_dd(2)
-            nc.vector.scalar_tensor_tensor(zc_factor[:, t, :], square[:], 1.0, g, ALU.subtract, ALU.mult)
-            rows = load_plane("x%d" % t, x_last_at if t == last else None)
-            x_less_c = tile("x_less_c%d" % t, [SLOTS], F32)
-            if t < last:
-                nc.vector.tensor_tensor(x_less_c[:], rows[:].indirect(listed(whole)), c_whole, ALU.subtract)
+            c = tile("c%d" % t, [SLOTS], F32)[:]
+            g, square = gates[:, t, :], zg_factor[:, t, :]
+            x_less_c = tile("x_less_c%d" % t, [SLOTS], F32)[:]
+
+            def form_dd(slots):
+                nc.vector.scalar_tensor_tensor(minus_dd[:, t, slots], g[:, slots], 1.0, dr_planes[t][:, slots], ALU.subtract, ALU.mult)
+
+            def form_zc_factor():
+                nc.vector.scalar_tensor_tensor(zc_factor[:, t, :], square, 1.0, g, ALU.subtract, ALU.mult)
+
+            if t < 2:
+                nc.sync.dma_start(c_rows[t][:], by_plane(cT)[:, t, :])
             else:
-                for h in range(2):
-                    nc.vector.tensor_tensor(x_less_c[:, halves[h]], rows[:].indirect(listed(halves[h])), c[h], ALU.subtract)
-            nc.gpsimd.tensor_tensor(zg_factor[:, t, :], g, x_less_c[:], ALU.mult)
+                load_c(t, 1)
+            for slots in halves:
+                gather_on_scalar(c, c_rows[t], slots)
+            for slots in halves:
+                nc.scalar.activation(square[:, slots], c[:, slots], ACT.Square)
+            if t > 0:
+                x = tile("x%d" % t, [SLOTS], F32)[:]
+                gather_on_vector(x, load_plane("x%d" % t), whole)
+                nc.gpsimd.tensor_tensor(x_less_c, x, c, ALU.subtract)
+            if 0 < t < last:
+                load_c(t + 1, 0)
+            rows = load_plane("g%d" % t)
+            if t == 0:
+                gather_on_vector(g, rows, low)
+                gather_on_vector(g, rows, blocks[2])
+                gather_on_scalar(g, rows, late)
+            else:
+                for slots in (halves if t == last else halves[::-1]):
+                    gather_on_vector(g, rows, slots)
+            if t in (0, last):
+                form_dd(low)
+                form_dd(blocks[2])
+                form_zc_factor()
+            else:
+                form_dd(blocks[2])
+                form_zc_factor()
+                form_dd(low)
+            scatter_dd(t, early, minus_dd[:, t, :])
+            if t == 0:
+                nc.vector.tensor_tensor(x_less_c, load_plane("x0")[:].indirect(listed(whole)), c, ALU.subtract)
+            nc.gpsimd.tensor_tensor(zg_factor[:, t, :], g, x_less_c, ALU.mult)
 
         wc_raw = load_matrix(wc, "wc", None)
         wg_raw = load_matrix(wg, "wg", None)
-        dd_fourth = late_dd(last, c_last_at)
+        minus_dd_late = together("minus_dd_late", P)
+        nc.vector.scalar_tensor_tensor(minus_dd_late, gates[:, :, late], 1.0, dr_blocks[last][:], ALU.subtract, ALU.mult)
         for t in range(PACK):
-            scatter_dd(t, blocks[2], dd_third[:, t, :])
-        for t in range(PACK):
-            scatter_dd(t, blocks[last], dd_fourth[:, t, :])
+            scatter_dd(t, late, minus_dd_late[:, t, :])
             nc.sync.dma_start(by_plane(out_1)[:, t, :], windows[t][:])
-        zc_grouped = tile("zc_grouped", [SLOTS, PACK], BF16, x_last_at)
+        zc_grouped = tile("zc_grouped", [SLOTS, PACK], BF16)
         for j in range(BLOCKS):
             nc.vector.tensor_tensor(
                 woven(zc_grouped[:, blocks[j], :]), by_pairs(zc_factor[:, :, blocks[j]]), by_pairs(dr_blocks[j][:]), ALU.mult
@@ -218,21 +234,20 @@ def tile_attend_ghighw_kernel(tc, dy, wo, gT, cT, xT, wg, wc, offs, out_0, out_1
 
         zg_low, zg_high = (tile("zg_grouped%d" % h, [SLOTS // 2, PACK], BF16) for h in range(2))
         wg_grouped = tile("wg_grouped", [K, PACK], BF16)
-        form_zg(zg_low[:], low, minus_dd)
+        form_zg(zg_low[:], low, minus_dd[:, :, low])
         group(nc.vector.tensor_copy, wg_grouped[:, low, :], wg_raw[:, :, low])
         zc_low = quantize_zc(0)
         wc_mx = [quantize_wc(0)]
         wg_mx = [quantize(wg_grouped[:, low, :], "wg0", E4M3)]
         zg_low = quantize(zg_low[:], "zg0", E5M2)
         first = [second_product("plane%d" % r, [r], zc_low, zg_low) for r in range(2)]
-        for copy, cols in ((negate_on_vector, slice(K // 2, K - WC_TAIL)), (negate_on_scalar, slice(K - WC_TAIL, K))):
-            group(copy, wc_grouped[:, cols, :], wc_raw[:, :, cols])
+        group(negate_on_scalar, wc_grouped[:, high, :], wc_raw[:, :, high])
         group(nc.vector.tensor_copy, wg_grouped[:, high, :], wg_raw[:, :, high])
-        form_zg(zg_high[:, blocks[0], :], blocks[2], dd_third)
+        form_zg(zg_high[:, blocks[0], :], blocks[2], minus_dd[:, :, blocks[2]])
         wc_mx.append(quantize_wc(1))
         wg_mx.append(quantize(wg_grouped[:, high, :], "wg1", E4M3))
         high_low = second_product("plane2", [2, 3], zc_low, zg_low)
-        form_zg(zg_high[:, blocks[1], :], blocks[last], dd_fourth)
+        form_zg(zg_high[:, blocks[1], :], late, minus_dd_late)
         zc_high = quantize_zc(1)
         zg_high = quantize(zg_high[:], "zg1", E5M2)
         outer = second_product("plane3", [0, 3], zc_high, zg_high)

@@ -196,7 +196,7 @@ def tile_attend_ghighw_kernel(tc, dy, wo, gT, cT, xT, wg, wc, offs, out_0, out_1
                 woven(zc_grouped[:, blocks[j], :]), by_pairs(zc_factor[:, :, blocks[j]]), by_pairs(dr_blocks[j][:]), ALU.mult
             )
         wc_grouped = tile("wc_grouped", [K, PACK], BF16)
-        nc.gpsimd.tensor_scalar(wc_grouped[:, low, :], wc_raw[:, :, low].rearrange("p j n -> p n j"), -1.0, 0.0, ALU.mult, ALU.add)
+        nc.gpsimd.tensor_scalar(wc_grouped[:, blocks[0], :], wc_raw[:, :, blocks[0]].rearrange("p j n -> p n j"), -1.0, 0.0, ALU.mult, ALU.add)
 
         def negate_on_vector(out, in_):
             nc.vector.tensor_scalar(out, in_, -1.0, None, ALU.mult)
@@ -235,6 +235,7 @@ def tile_attend_ghighw_kernel(tc, dy, wo, gT, cT, xT, wg, wc, offs, out_0, out_1
         zg_low, zg_high = (tile("zg_grouped%d" % h, [SLOTS // 2, PACK], BF16) for h in range(2))
         wg_grouped = tile("wg_grouped", [K, PACK], BF16)
         form_zg(zg_low[:], low, minus_dd[:, :, low])
+        group(negate_on_vector, wc_grouped[:, blocks[1], :], wc_raw[:, :, blocks[1]])
         group(nc.vector.tensor_copy, wg_grouped[:, low, :], wg_raw[:, :, low])
         zc_low = quantize_zc(0)
         wc_mx = [quantize_wc(0)]

@@ -19,8 +19,8 @@ K = 512
 SLOTS = 512
 TOKENS = 1024
 BLOCKS = SLOTS // P
-SCALAR_SHARE = 160
-WC_TAIL = 128
+SCALAR_SHARE = 192
+GPSIMD_SHARE = 160
 VECTOR_SHARE = 352
 KIB = 1024
 EDGE = 64
@@ -196,7 +196,7 @@ def tile_attend_ghighw_kernel(tc, dy, wo, gT, cT, xT, wg, wc, offs, out_0, out_1
                 woven(zc_grouped[:, blocks[j], :]), by_pairs(zc_factor[:, :, blocks[j]]), by_pairs(dr_blocks[j][:]), ALU.mult
             )
         wc_grouped = tile("wc_grouped", [K, PACK], BF16)
-        nc.gpsimd.tensor_scalar(wc_grouped[:, blocks[0], :], wc_raw[:, :, blocks[0]].rearrange("p j n -> p n j"), -1.0, 0.0, ALU.mult, ALU.add)
+        nc.gpsimd.tensor_scalar(wc_grouped[:, 0:GPSIMD_SHARE, :], wc_raw[:, :, 0:GPSIMD_SHARE].rearrange("p j n -> p n j"), -1.0, 0.0, ALU.mult, ALU.add)
 
         def negate_on_vector(out, in_):
             nc.vector.tensor_scalar(out, in_, -1.0, None, ALU.mult)
@@ -213,12 +213,18 @@ def tile_attend_ghighw_kernel(tc, dy, wo, gT, cT, xT, wg, wc, offs, out_0, out_1
         def quantize_wc(h):
             return quantize(wc_grouped[:, halves[h], :], "wc%d" % h, E4M3)
 
-        def second_product(tag, rows, zc_mx, zg_mx):
-            bank = psum.tile([P, len(rows), SLOTS // 2], F32, name="s_" + tag, tag=tag)
+        def s_bank(tag, rows):
+            return rows, psum.tile([P, len(rows), SLOTS // 2], F32, name="s_" + tag, tag=tag)
+
+        def passes(banks, weights, moving, opens):
+            for rows, bank in banks:
+                for place, r in enumerate(rows):
+                    product(bank[:, place, :], weights[r // 2], blocks[r % 2], moving, low, opens and place == 0, not opens and place == len(rows) - 1)
+
+        def empty(copy, bank, slots):
+            rows, sums = bank
             for place, r in enumerate(rows):
-                product(bank[:, place, :], wc_mx[r // 2], blocks[r % 2], zc_mx, halves[0], True, False)
-                product(bank[:, place, :], wg_mx[r // 2], blocks[r % 2], zg_mx, halves[0], False, True)
-            return bank
+                copy(out=s[:, r, slots], in_=sums[:, place, :])
 
         s = together("s")
         s_windows = [windows[n] for n in (4, 5, 0, 1)]
@@ -235,41 +241,42 @@ def tile_attend_ghighw_kernel(tc, dy, wo, gT, cT, xT, wg, wc, offs, out_0, out_1
         zg_low, zg_high = (tile("zg_grouped%d" % h, [SLOTS // 2, PACK], BF16) for h in range(2))
         wg_grouped = tile("wg_grouped", [K, PACK], BF16)
         form_zg(zg_low[:], low, minus_dd[:, :, low])
-        group(negate_on_vector, wc_grouped[:, blocks[1], :], wc_raw[:, :, blocks[1]])
+        group(negate_on_vector, wc_grouped[:, GPSIMD_SHARE : K // 2, :], wc_raw[:, :, GPSIMD_SHARE : K // 2])
         group(nc.vector.tensor_copy, wg_grouped[:, low, :], wg_raw[:, :, low])
         zc_low = quantize_zc(0)
-        wc_mx = [quantize_wc(0)]
-        wg_mx = [quantize(wg_grouped[:, low, :], "wg0", E4M3)]
+        wc_mx, wg_mx = {0: quantize_wc(0)}, {0: quantize(wg_grouped[:, low, :], "wg0", E4M3)}
+        low_0, low_1, low_23 = s_bank("plane0", [0]), s_bank("plane1", [1]), s_bank("plane2", [2, 3])
+        high_0, high_23, high_1 = s_bank("plane3", [0]), s_bank("block0", [2, 3]), s_bank("block1", [1])
+        passes([low_0, low_1], wc_mx, zc_low, True)
         zg_low = quantize(zg_low[:], "zg0", E5M2)
-        first = [second_product("plane%d" % r, [r], zc_low, zg_low) for r in range(2)]
+        passes([low_0, low_1], wg_mx, zg_low, False)
         group(negate_on_scalar, wc_grouped[:, high, :], wc_raw[:, :, high])
         group(nc.vector.tensor_copy, wg_grouped[:, high, :], wg_raw[:, :, high])
-        form_zg(zg_high[:, blocks[0], :], blocks[2], minus_dd[:, :, blocks[2]])
-        wc_mx.append(quantize_wc(1))
-        wg_mx.append(quantize(wg_grouped[:, high, :], "wg1", E4M3))
-        high_low = second_product("plane2", [2, 3], zc_low, zg_low)
-        form_zg(zg_high[:, blocks[1], :], late, minus_dd_late)
         zc_high = quantize_zc(1)
+        passes([high_0, high_1], wc_mx, zc_high, True)
+        wg_mx[1] = quantize(wg_grouped[:, high, :], "wg1", E4M3)
+        passes([low_23], wg_mx, zg_low, True)
+        form_zg(zg_high[:, blocks[0], :], blocks[2], minus_dd[:, :, blocks[2]])
+        wc_mx[1] = quantize_wc(1)
+        passes([low_23], wc_mx, zc_low, False)
+        passes([high_23], wc_mx, zc_high, True)
+        form_zg(zg_high[:, blocks[1], :], late, minus_dd_late)
+        empty(nc.scalar.copy, low_0, low)
+        scatter_on_scalar(0, low)
+        empty(nc.vector.tensor_copy, low_1, low)
+        scatter_on_scalar(1, low)
         zg_high = quantize(zg_high[:], "zg1", E5M2)
-        outer = second_product("plane3", [0, 3], zc_high, zg_high)
-        inner = second_product("block0", [2, 1], zc_high, zg_high)
+        passes([high_0, high_23, high_1], wg_mx, zg_high, False)
 
+        empty(nc.vector.tensor_copy, low_23, low)
+        empty(nc.vector.tensor_copy, high_0, high)
+        nc.vector.tensor_copy(s[:, 2:PACK, high], high_23[1][:])
+        empty(nc.vector.tensor_copy, high_1, high)
         for r in range(2):
-            nc.scalar.copy(out=s[:, r, halves[0]], in_=first[r][:, 0, :])
-        for r in range(2):
-            scatter_on_scalar(r, halves[0])
-        for place, r in enumerate((2, 3)):
-            nc.vector.tensor_copy(s[:, r, halves[0]], high_low[:, place, :])
-        scatter_on_vector(2, blocks[0])
-        nc.vector.tensor_copy(s[:, 0:PACK:last, halves[1]], outer[:])
-        for place, r in enumerate((2, 1)):
-            nc.vector.tensor_copy(s[:, r, halves[1]], inner[:, place, :])
-        scatter_on_scalar(0, halves[1])
-        store(0)
-        scatter_on_scalar(3, slice(SLOTS - SCALAR_SHARE, SLOTS))
-        scatter_on_vector(2, slice(P, SLOTS))
-        store(2)
-        scatter_on_scalar(1, halves[1])
-        store(1)
+            scatter_on_scalar(r, high)
+            store(r)
         scatter_on_vector(3, slice(0, SLOTS - SCALAR_SHARE))
+        scatter_on_scalar(3, slice(SLOTS - SCALAR_SHARE, SLOTS))
         store(3)
+        scatter_on_vector(2, whole)
+        store(2)

from contextlib import ExitStack

import concourse.mybir as mybir

F32 = mybir.dt.float32
BF16 = mybir.dt.bfloat16
U32 = mybir.dt.uint32
I32 = mybir.dt.int32
U16 = mybir.dt.uint16
U8 = mybir.dt.uint8
E4M3 = mybir.dt.float8_e4m3fn_x4
E5M2 = mybir.dt.float8_e5m2_x4
ALU = mybir.AluOpType
ACT = mybir.ActivationFunctionType

P = 128
PACK = 4
K = 512
SLOTS = 512
TOKENS = 1024
BLOCKS = SLOTS // P
SCALAR_SHARE = 192
GPSIMD_SHARE = 160
VECTOR_SHARE = 352
KIB = 1024
EDGE = 64
FLOPS = 3 * 2 * K * K * SLOTS


def tile_attend_ghighw_kernel(tc, dy, wo, gT, cT, xT, wg, wc, offs, out_0, out_1):
    nc = tc.nc
    with ExitStack() as ctx:
        lists = ctx.enter_context(tc.tile_pool(name="lists", bufs=1))
        sb = ctx.enter_context(tc.tile_pool(name="sb", bufs=1))
        shared = ctx.enter_context(tc.tile_pool(name="shared", bufs=1))
        psum = ctx.enter_context(tc.psum_pool(name="psum", bufs=1))
        blocks = [slice(j * P, (j + 1) * P) for j in range(BLOCKS)]
        halves = [slice(h * SLOTS // 2, (h + 1) * SLOTS // 2) for h in range(2)]
        last = PACK - 1

        def tile(label, shape, dtype, place=None):
            if place is None:
                return sb.tile([P] + shape, dtype, name=label, align_bytes=64)
            return shared.tile([P] + shape, dtype, name=label, align_bytes=64, offset=place)

        def by_plane(matrix):
            return matrix.rearrange("(p t) n -> p t n", t=PACK)

        def load_matrix(matrix, label, place):
            raw = tile(label + "_raw", [PACK, K], F32, place)
            nc.sync.dma_start(raw[:], by_plane(matrix))
            return raw

        def load_plane(label, place=None):
            rows = tile(label + "_rows", [TOKENS], F32, place)
            nc.sync.dma_start(rows[:], by_plane({"g": gT, "c": cT, "x": xT}[label[0]])[:, int(label[1]), :])
            return rows

        def group(copy, grouped, raw):
            copy(out=grouped.rearrange("p (c i) j -> p c j i", i=4), in_=raw.rearrange("p j (c i) -> p c j i", i=4))

        def quantize(grouped, label, fmt, place=None, codes_place=None):
            width = grouped.shape[1]
            codes = tile(label + "_codes", [width], U32, codes_place)
            scales = tile(label + "_scales", [width], U8, place)
            nc.vector.quantize_mx(out=codes[:].bitcast(fmt), scales=scales[:], in_=grouped.rearrange("p n j -> p (n j)"))
            return codes, scales

        def product(out, weights, columns, moving, slots, start, stop):
            nc.tensor.matmul_mx(
                out=out, lhsT=weights[0][:, columns].bitcast(E4M3), lhsT_scale=weights[1][:, columns],
                rhs=moving[0][:, slots].bitcast(E5M2), rhs_scale=moving[1][:, slots], start=start, stop=stop,
            )

        def listed(slots):
            return offsets[:, slots.start // 16 : slots.stop // 16]

        def gather_on_vector(picked, rows, slots):
            nc.vector.tensor_copy(picked[:, slots], rows[:].indirect(listed(slots)))

        def gather_on_scalar(picked, rows, slots):
            nc.scalar.activation(picked[:, slots], rows[:].indirect(listed(slots)), ACT.Copy)

        def by_pairs(planes):
            return planes.rearrange("p t (c i) -> p c t i", i=4)

        def woven(grouped):
            return grouped.rearrange("p (c i) t -> p c t i", i=4)

        x_last_at, c_last_at = 0, 8 * KIB
        windows = []
        for engine in (nc.vector, nc.vector, nc.gpsimd) * 2:
            window = tile("window%d" % len(windows), [TOKENS], F32)
            engine.memset(window[:], 0.0)
            windows.append(window)

        wo_raw = load_matrix(wo, "wo", None)
        dy_raw = load_matrix(dy, "dy", None)
        offsets = lists.tile([P, SLOTS // 16], U16, name="offsets")
        nc.sync.dma_start(offsets[:], offs)

        wo_grouped = tile("wo_grouped", [K, PACK], BF16)
        dealt = wo_grouped[:].rearrange("p (t m) j -> p m j t", t=PACK)
        source = wo_raw[:].rearrange("p j (m t) -> p m j t", t=PACK)
        cut = VECTOR_SHARE // PACK
        nc.vector.tensor_copy(out=dealt[:, 0:cut], in_=source[:, 0:cut])
        nc.scalar.copy(out=dealt[:, cut:], in_=source[:, cut:])
        wo_mx = quantize(wo_grouped[:], "wo", E4M3)
        dy_grouped = tile("dy_grouped", [SLOTS, PACK], BF16)
        for copy, cols in ((nc.vector.tensor_copy, slice(0, VECTOR_SHARE)), (nc.scalar.copy, slice(VECTOR_SHARE, K))):
            group(copy, dy_grouped[:, cols, :], dy_raw[:, :, cols])
        dy_mx = quantize(dy_grouped[:], "dy", E5M2)

        whole = slice(0, SLOTS)
        low, high = halves
        early, late = slice(0, last * P), blocks[last]
        dr_planes = [psum.tile([P, last * P], F32, name="dr_plane%d" % t, tag="plane%d" % t) for t in range(PACK)]
        dr_blocks = [psum.tile([P, PACK, P], F32, name="dr_block%d" % j, tag="block%d" % j) for j in range(BLOCKS)]
        for t in range(PACK):
            for slots in (low, blocks[2]):
                product(dr_planes[t][:, slots], wo_mx, blocks[t], dy_mx, slots, True, True)
        for j in range(BLOCKS):
            for t in range(PACK):
                product(dr_blocks[j][:, t, :], wo_mx, blocks[t], dy_mx, blocks[j], True, True)

        def together(label, width=SLOTS):
            return tile(label, [PACK * width], F32)[:].rearrange("p (t n) -> p t n", t=PACK)

        gates, zg_factor, zc_factor = together("gates"), together("zg_factor"), together("zc_factor")
        minus_dd = together("minus_dd", last * P)

        def scatter_dd(t, slots, values):
            nc.scalar.activation(windows[t][:].indirect(listed(slots)), values, ACT.Copy, scale=-1.0)

        def load_c(t, part):
            columns = slice(part * TOKENS // 2, (part + 1) * TOKENS // 2)
            nc.sync.dma_start(c_rows[t][:, columns], by_plane(cT)[:, t, columns])

        c_rows = [tile("c%d_rows" % t, [TOKENS], F32) for t in range(PACK)]
        for t in range(PACK):
            c = tile("c%d" % t, [SLOTS], F32)[:]
            g, square = gates[:, t, :], zg_factor[:, t, :]
            x_less_c = tile("x_less_c%d" % t, [SLOTS], F32)[:]

            def form_dd(slots):
                nc.vector.scalar_tensor_tensor(minus_dd[:, t, slots], g[:, slots], 1.0, dr_planes[t][:, slots], ALU.subtract, ALU.mult)

            def form_zc_factor():
                nc.vector.scalar_tensor_tensor(zc_factor[:, t, :], square, 1.0, g, ALU.subtract, ALU.mult)

            if t < 2:
                nc.sync.dma_start(c_rows[t][:], by_plane(cT)[:, t, :])
            else:
                load_c(t, 1)
            for slots in halves:
                gather_on_scalar(c, c_rows[t], slots)
            for slots in halves:
                nc.scalar.activation(square[:, slots], c[:, slots], ACT.Square)
            if t > 0:
                x = tile("x%d" % t, [SLOTS], F32)[:]
                gather_on_vector(x, load_plane("x%d" % t), whole)
                nc.gpsimd.tensor_tensor(x_less_c, x, c, ALU.subtract)
            if 0 < t < last:
                load_c(t + 1, 0)
            rows = load_plane("g%d" % t)
            if t == 0:
                gather_on_vector(g, rows, low)
                gather_on_vector(g, rows, blocks[2])
                gather_on_scalar(g, rows, late)
            else:
                for slots in (halves if t == last else halves[::-1]):
                    gather_on_vector(g, rows, slots)
            if t in (0, last):
                form_dd(low)
                form_dd(blocks[2])
                form_zc_factor()
            else:
                form_dd(blocks[2])
                form_zc_factor()
                form_dd(low)
            scatter_dd(t, early, minus_dd[:, t, :])
            if t == 0:
                nc.vector.tensor_tensor(x_less_c, load_plane("x0")[:].indirect(listed(whole)), c, ALU.subtract)
            nc.gpsimd.tensor_tensor(zg_factor[:, t, :], g, x_less_c, ALU.mult)

        wc_raw = load_matrix(wc, "wc", None)
        wg_raw = load_matrix(wg, "wg", None)
        minus_dd_late = together("minus_dd_late", P)
        nc.vector.scalar_tensor_tensor(minus_dd_late, gates[:, :, late], 1.0, dr_blocks[last][:], ALU.subtract, ALU.mult)
        for t in range(PACK):
            scatter_dd(t, late, minus_dd_late[:, t, :])
            nc.sync.dma_start(by_plane(out_1)[:, t, :], windows[t][:])
        zc_grouped = tile("zc_grouped", [SLOTS, PACK], BF16)
        for j in range(BLOCKS):
            nc.vector.tensor_tensor(
                woven(zc_grouped[:, blocks[j], :]), by_pairs(zc_factor[:, :, blocks[j]]), by_pairs(dr_blocks[j][:]), ALU.mult
            )
        wc_grouped = tile("wc_grouped", [K, PACK], BF16)
        nc.gpsimd.tensor_scalar(wc_grouped[:, 0:GPSIMD_SHARE, :], wc_raw[:, :, 0:GPSIMD_SHARE].rearrange("p j n -> p n j"), -1.0, 0.0, ALU.mult, ALU.add)

        def negate_on_vector(out, in_):
            nc.vector.tensor_scalar(out, in_, -1.0, None, ALU.mult)

        def negate_on_scalar(out, in_):
            nc.scalar.activation(out, in_, ACT.Copy, scale=-1.0)

        def form_zg(grouped, slots, values):
            nc.vector.tensor_tensor(woven(grouped), by_pairs(zg_factor[:, :, slots]), by_pairs(values), ALU.mult)

        def quantize_zc(h):
            return quantize(zc_grouped[:, halves[h], :], "zc%d" % h, E5M2)

        def quantize_wc(h):
            return quantize(wc_grouped[:, halves[h], :], "wc%d" % h, E4M3)

        def s_bank(tag, rows):
            return rows, psum.tile([P, len(rows), SLOTS // 2], F32, name="s_" + tag, tag=tag)

        def passes(banks, weights, moving, opens):
            for rows, bank in banks:
                for place, r in enumerate(rows):
                    product(bank[:, place, :], weights[r // 2], blocks[r % 2], moving, low, opens and place == 0, not opens and place == len(rows) - 1)

        def empty(copy, bank, slots):
            rows, sums = bank
            for place, r in enumerate(rows):
                copy(out=s[:, r, slots], in_=sums[:, place, :])

        s = together("s")
        s_windows = [windows[n] for n in (4, 5, 0, 1)]

        def scatter_on_scalar(r, slots):
            nc.scalar.activation(s_windows[r][:].indirect(listed(slots)), s[:, r, slots], ACT.Copy)

        def scatter_on_vector(r, slots):
            nc.vector.tensor_copy(s_windows[r][:].indirect(listed(slots)), s[:, r, slots])

        def store(r):
            nc.sync.dma_start(out_0[blocks[r], :], s_windows[r][:])

        zg_low, zg_high = (tile("zg_grouped%d" % h, [SLOTS // 2, PACK], BF16) for h in range(2))
        wg_grouped = tile("wg_grouped", [K, PACK], BF16)
        form_zg(zg_low[:], low, minus_dd[:, :, low])
        group(negate_on_vector, wc_grouped[:, GPSIMD_SHARE : K // 2, :], wc_raw[:, :, GPSIMD_SHARE : K // 2])
        group(nc.vector.tensor_copy, wg_grouped[:, low, :], wg_raw[:, :, low])
        zc_low = quantize_zc(0)
        wc_mx, wg_mx = {0: quantize_wc(0)}, {0: quantize(wg_grouped[:, low, :], "wg0", E4M3)}
        low_0, low_1, low_23 = s_bank("plane0", [0]), s_bank("plane1", [1]), s_bank("plane2", [2, 3])
        high_0, high_23, high_1 = s_bank("plane3", [0]), s_bank("block0", [2, 3]), s_bank("block1", [1])
        passes([low_0, low_1], wc_mx, zc_low, True)
        zg_low = quantize(zg_low[:], "zg0", E5M2)
        passes([low_0, low_1], wg_mx, zg_low, False)
        group(negate_on_scalar, wc_grouped[:, high, :], wc_raw[:, :, high])
        group(nc.vector.tensor_copy, wg_grouped[:, high, :], wg_raw[:, :, high])
        zc_high = quantize_zc(1)
        passes([high_0, high_1], wc_mx, zc_high, True)
        wg_mx[1] = quantize(wg_grouped[:, high, :], "wg1", E4M3)
        passes([low_23], wg_mx, zg_low, True)
        form_zg(zg_high[:, blocks[0], :], blocks[2], minus_dd[:, :, blocks[2]])
        wc_mx[1] = quantize_wc(1)
        passes([low_23], wc_mx, zc_low, False)
        passes([high_23], wc_mx, zc_high, True)
        form_zg(zg_high[:, blocks[1], :], late, minus_dd_late)
        empty(nc.scalar.copy, low_0, low)
        scatter_on_scalar(0, low)
        empty(nc.vector.tensor_copy, low_1, low)
        scatter_on_scalar(1, low)
        zg_high = quantize(zg_high[:], "zg1", E5M2)
        passes([high_0, high_23, high_1], wg_mx, zg_high, False)

        empty(nc.vector.tensor_copy, low_23, low)
        empty(nc.vector.tensor_copy, high_0, high)
        nc.vector.tensor_copy(s[:, 2:PACK, high], high_23[1][:])
        empty(nc.vector.tensor_copy, high_1, high)
        for r in range(2):
            scatter_on_scalar(r, high)
            store(r)
        scatter_on_vector(3, slice(0, SLOTS - SCALAR_SHARE))
        scatter_on_scalar(3, slice(SLOTS - SCALAR_SHARE, SLOTS))
        store(3)
        scatter_on_vector(2, whole)
        store(2)
